import numpy as np
import ml_dtypes


def mxq(x, axis, fmt="e4m3"):
    dtype, down = {"e4m3": (ml_dtypes.float8_e4m3fn, 7), "e5m2": (ml_dtypes.float8_e5m2, 14)}[fmt]
    v = np.moveaxis(np.asarray(x, np.float32).astype(ml_dtypes.bfloat16).astype(np.float64), axis, -1)
    blocks = v.reshape(v.shape[:-1] + (-1, 32))
    amax = np.abs(blocks).max(-1, keepdims=True)
    byte = np.maximum(np.where(amax > 0, np.frexp(amax)[1] - 1 + 127, 0) - down, 1)
    scale = np.exp2(byte - 127.0)
    codes = (blocks / scale).astype(np.float32).astype(dtype).astype(np.float64)
    return np.moveaxis((codes * scale).reshape(v.shape), -1, axis)


WIDE = False


def mx_kscale(k):
    if not WIDE:
        return np.ones(k)
    levels = np.array([24, -24, 12, -12, 0])
    if k % 512:
        return np.exp2(np.random.permutation(np.resize(levels, k // 32))).repeat(32)
    a = np.empty((k // 512, 16))
    for p in range(k // 512):
        a[p, :8] = np.random.permutation(np.resize(levels, 8))
        for g in range(8):
            far = levels[np.abs(levels - a[p, g]) >= 10]
            a[p, g + 8] = far[np.random.randint(len(far))]
    return np.exp2(a.ravel()).repeat(32)


def f64(x):
    return np.asarray(x).astype(np.float64)


def striped(idx):
    return np.tile(idx.reshape(-1, 16).T, (8, 1)).astype(np.uint16)


def unstriped(offs):
    return offs[:16].T.reshape(-1).astype(np.int64)


E2M1 = np.array([0.0, 0.5, 1.0, 1.5, 2.0, 3.0, 4.0, 6.0, -0.0, -0.5, -1.0, -1.5, -2.0, -3.0, -4.0, -6.0])


def pack_weight(w, fmt):
    k, n = w.shape
    w = f64(np.asarray(w, np.float32).astype(ml_dtypes.bfloat16)).reshape(k // 32, 32, n)
    amax = np.abs(w).max(1)
    if fmt == "e4m3":
        byte = np.frexp(amax)[1] - 1 + 127 - 7
    else:
        mant, ex = np.frexp(amax / 6.0)
        byte = np.where(mant > 0.5, ex, ex - 1) + 127
    byte = np.clip(np.where(amax > 0, byte, 1), 1, 254)
    scaled = (w * np.exp2(127.0 - byte)[:, None, :]).reshape(k, n).astype(np.float32)
    by_word = np.ascontiguousarray(scaled.reshape(k // 512, 128, 4, n).transpose(0, 1, 3, 2))
    if fmt == "e4m3":
        words = by_word.astype(ml_dtypes.float8_e4m3fn).view(np.uint8)
    else:
        c = by_word.astype(ml_dtypes.float4_e2m1fn).view(np.uint8) & 0xF
        words = (c[..., 0::2] | (c[..., 1::2] << 4)).reshape(k // 512, 128, 2 * n)
    return np.ascontiguousarray(words), np.ascontiguousarray(byte.astype(np.uint8).reshape(k // 512, 16, n))


def unpack_weight(words, scales, fmt):
    g, _, n = scales.shape
    words = np.ascontiguousarray(words).reshape(g, 128, n, -1)
    if fmt == "e4m3":
        vals = words.view(ml_dtypes.float8_e4m3fn).astype(np.float64)
    else:
        nib = np.empty((g, 128, n, 4), np.uint8)
        nib[..., 0::2] = words & 0xF
        nib[..., 1::2] = words >> 4
        vals = E2M1[nib]
    vals = vals * np.repeat(np.exp2(scales.astype(np.float64) - 127.0), 8, axis=1)[..., None]
    return vals.transpose(0, 1, 3, 2).reshape(g * 512, n)


def pack_table4(v):
    words, scales = pack_weight(v, "e2m1")
    g, t = words.shape[0] // 2, v.shape[1]
    return np.ascontiguousarray(words.reshape(g, 2, 128, t, 2).transpose(0, 2, 3, 1, 4).reshape(g, 128, t, 4)), scales


def unpack_table4(words, scales):
    g, _, t, _ = words.shape
    return unpack_weight(words.reshape(g, 128, t, 2, 2).transpose(0, 3, 1, 2, 4).reshape(2 * g, 128, 2 * t), scales, "e2m1")


def silu(f):
    return f / (1.0 + np.exp(-np.maximum(f, -700.0)))


K, R, N, T, J = 1024, 1024, 512, 2048, 1024


def setup_inputs():
    n = np.random.standard_normal
    s = mx_kscale(K)[:, None]
    u = mx_kscale(R)[:, None]
    wd = n((R, N)) / np.sqrt(R) / u
    p_tab = pack_table4(n((K, T)) * s)
    p_wu = pack_weight(n((K, R)) / np.sqrt(K) / s * u.T, "e4m3")
    p_wd8 = pack_weight(wd[:512], "e4m3")
    p_wd4 = pack_weight(wd[512:], "e2m1")
    return {
        "tab_words": p_tab[0],
        "tab_scales": p_tab[1],
        "wg": (n((K, R)) / np.sqrt(K) / s).astype(np.float32),
        "wu_words": p_wu[0],
        "wu_scales": p_wu[1],
        "wd8_words": p_wd8[0],
        "wd8_scales": p_wd8[1],
        "wd4_words": p_wd4[0],
        "wd4_scales": p_wd4[1],
        "gT": (n((N, T))).astype(np.float32),
        "wgo": np.tile(np.random.uniform(0.5, 2.0, J), (128, 1)).astype(np.float32),
        "offs": striped(np.random.permutation(T)[:J]),
    }


def reference(tab_words, tab_scales, wg, wu_words, wu_scales, wd8_words, wd8_scales, wd4_words, wd4_scales, gT, wgo, offs):
    idx = unstriped(offs)
    tab_ = unpack_table4(tab_words, tab_scales)[:, idx]
    wg_ = mxq(f64(wg), 0, "e4m3")
    wu_ = unpack_weight(wu_words, wu_scales, "e4m3")
    ga = wg_.T @ tab_
    ub = wu_.T @ tab_
    h = silu(ga) * ub
    h_ = mxq(h, 0, "e4m3")
    wd8_ = unpack_weight(wd8_words, wd8_scales, "e4m3")
    wd4_ = unpack_weight(wd4_words, wd4_scales, "e2m1")
    y = wd8_.T @ h_[:512] + wd4_.T @ h_[512:]
    out = np.zeros((N, T))
    out[:, idx] = f64(wgo)[0] * (y * f64(gT)[:, idx])
    return out

@@ -1,0 +1,203 @@
+from contextlib import ExitStack
+
+import concourse.mybir as mybir
+
+K, R, N, T, J = 1024, 1024, 512, 2048, 1024
+FLOPS = 2 * K * R * J * 2 + 2 * R * N * J
+
+F32 = mybir.dt.float32
+BF16 = mybir.dt.bfloat16
+I32 = mybir.dt.int32
+U32 = mybir.dt.uint32
+U16 = mybir.dt.uint16
+U8 = mybir.dt.uint8
+FP8X4 = mybir.dt.float8_e4m3fn_x4
+FP4X4 = mybir.dt.float4_e2m1fn_x4
+MULT = mybir.AluOpType.mult
+SILU = mybir.ActivationFunctionType.Silu
+
+P = 128
+PACK = 4
+PASS = P * PACK
+HALF = J // 2
+CHUNK = 128
+
+
+def tile_list_modp_gsilu_mix_gate_kernel(tc, tab_words, tab_scales, wg, wu_words, wu_scales, wd8_words, wd8_scales, wd4_words, wd4_scales, gT, wgo, offs, out):
+    nc = tc.nc
+    with ExitStack() as ctx:
+        keep = ctx.enter_context(tc.tile_pool(name="keep", bufs=1))
+        ring = ctx.enter_context(tc.tile_pool(name="ring", bufs=3))
+        big = ctx.enter_context(tc.tile_pool(name="big", bufs=3))
+        psum = ctx.enter_context(tc.psum_pool(name="psum", bufs=1))
+
+        offsets = keep.tile([P, J // 16], U16, name="offsets")
+        nc.sync.dma_start(offsets[:], offs)
+
+        tab_s = keep.tile([P, T], U8, name="tab_s", align_bytes=64)
+        wu_s_raw = keep.tile([P, 2 * R], U8, name="wu_s_raw", tag="raw_scales", align_bytes=64)
+        v_s = keep.tile([P, 2 * J], U8, name="v_s", align_bytes=64)
+        for q in range(4):
+            nc.vector.memset(tab_s[32 * q : 32 * q + 24, :].bitcast(I32), 0)
+        nc.vector.memset(v_s[:].bitcast(I32), 0)
+        nc.gpsimd.memset(wu_s_raw[:].bitcast(I32), 0)
+        for q in range(4):
+            nc.gpsimd.dma_start(wu_s_raw[32 * q : 32 * q + 4, :].bitcast(I32).rearrange("r (a c) -> r a c", a=2), wu_scales[:, 4 * q : 4 * q + 4, :].bitcast(I32).rearrange("a r c -> r a c"))
+
+        pages = [keep.tile([P, T], F32, name=f"page{n}") for n in range(3)]
+        nc.vector.memset(pages[0][:], 0.0)
+        for n in (1, 2):
+            nc.gpsimd.memset(pages[n][:], 0.0)
+
+        for q in range(4):
+            nc.sync.dma_start(tab_s[32 * q + 24 : 32 * q + 32, :].bitcast(I32), tab_scales[:, 4 * q : 4 * q + 4, :].bitcast(I32))
+        tab_w = big.tile([P, T], I32, name="tab_w", tag="big")
+        nc.sync.dma_start(tab_w[:], tab_words[0].rearrange("p t i -> p (t i)").bitcast(I32))
+
+        wgo_sb = keep.tile([P, J], F32, name="wgo_sb")
+        gates, wg_raw = {}, {}
+
+        def load_wg(a, b):
+            wg_raw[a, b] = big.tile([P, PACK, PASS], F32, name=f"wg_raw{a}{b}", tag="big")
+            nc.sync.dma_start(wg_raw[a, b][:], wg[PASS * a : PASS * (a + 1), PASS * b : PASS * (b + 1)].rearrange("(p i) c -> p i c", i=PACK))
+
+        def load_gate(n):
+            gates[n] = big.tile([P, T], F32, name=f"gate{n}", tag="big")
+            nc.sync.dma_start(gates[n][:], gT[P * n : P * (n + 1), :])
+
+        load_wg(0, 0)
+        nc.sync.dma_start(wgo_sb[:], wgo)
+        load_gate(0)
+        load_wg(1, 0)
+        wu_raw = big.tile([P, 2, R], I32, name="wu_raw", tag="big")
+        nc.sync.dma_start(wu_raw[:], wu_words.rearrange("a p r i -> p a (r i)").bitcast(I32))
+        load_gate(1)
+        load_wg(0, 1)
+        load_wg(1, 1)
+        wd8_w = keep.tile([P, N], I32, name="wd8_w", align_bytes=64)
+        nc.sync.dma_start(wd8_w[:], wd8_words[0].rearrange("p n i -> p (n i)").bitcast(I32))
+        wd4_w = keep.tile([P, 2 * N], U8, name="wd4_w", align_bytes=64)
+        nc.sync.dma_start(wd4_w[:].bitcast(I32), wd4_words[0].bitcast(I32))
+        load_gate(2)
+        load_gate(3)
+
+        v_s_raw = keep.tile([P, J], U8, name="v_s_raw", align_bytes=64)
+        nc.vector.tensor_copy(v_s_raw[:], tab_s[:].indirect(offsets[:]))
+        for a in range(2):
+            shift = 24 + 4 * a
+            nc.scalar.dma_start(v_s[0 : P - shift, J * a : J * (a + 1)].bitcast(I32), v_s_raw[shift:P, :].bitcast(I32))
+        v_pairs = keep.tile([P, J], U32, name="v_pairs")
+        nc.vector.tensor_copy(v_pairs[:], tab_w[:].bitcast(U32).indirect(offsets[:]))
+        v_w = keep.tile([P, 2, J], U16, name="v_w", align_bytes=64)
+        nc.vector.tensor_copy(
+            v_w[:].rearrange("p d (g e) -> p g d e", e=8),
+            v_pairs[:].bitcast(U16).rearrange("p (g e d) -> p g d e", e=8, d=2),
+        )
+
+        wu_s = keep.tile([P, 2 * R], U8, name="wu_s", align_bytes=64)
+        nc.vector.tensor_copy(
+            wu_s[:].rearrange("p (s t g e) -> p s g t e", s=4, t=PACK, e=16),
+            wu_s_raw[:].rearrange("p (s g e t) -> p s g t e", s=4, t=PACK, e=16),
+        )
+        wd_s = keep.tile([P, 2 * N], U8, name="wd_s", tag="raw_scales", align_bytes=64)
+        nc.gpsimd.memset(wd_s[:].bitcast(I32), 0)
+        for q in range(4):
+            nc.gpsimd.dma_start(wd_s[32 * q : 32 * q + 4, 0:N].bitcast(I32), wd8_scales[0, 4 * q : 4 * q + 4, :].bitcast(I32))
+            nc.gpsimd.dma_start(wd_s[32 * q : 32 * q + 4, N : 2 * N].bitcast(I32), wd4_scales[0, 4 * q : 4 * q + 4, :].bitcast(I32))
+
+        gw = [keep.tile([P, J], F32, name=f"gw{n}") for n in range(4)]
+
+        def gather_gate(n):
+            nc.vector.tensor_tensor(gw[n][:], gates[n][:].indirect(offsets[:]), wgo_sb[:], MULT)
+
+        wg_w, wg_s = {}, {}
+
+        def quantize_wg(a, b):
+            woven = ring.tile([P, PACK, P, PACK], BF16, name="wg_woven", align_bytes=64)
+            nc.scalar.copy(woven[:].rearrange("p t m i -> p m t i"), wg_raw[a, b][:].rearrange("p i (m t) -> p m t i", t=PACK))
+            wg_w[a, b] = keep.tile([P, PASS], U32, name=f"wg_w{a}{b}", align_bytes=64)
+            wg_s[a, b] = keep.tile([P, PASS], U8, name=f"wg_s{a}{b}", align_bytes=64)
+            nc.vector.quantize_mx(out=wg_w[a, b][:].bitcast(FP8X4), scales=wg_s[a, b][:], in_=woven[:].rearrange("p t m i -> p (t m i)"))
+
+        wu_w = keep.tile([P, 2 * R], I32, name="wu_w", align_bytes=64)
+
+        def deal_wu():
+            nc.vector.tensor_copy(
+                wu_w[:].rearrange("p (s t g e) -> p s g t e", s=4, t=PACK, e=4),
+                wu_raw[:].rearrange("p a (b g e t) -> p (a b) g t e", b=2, t=PACK, e=4),
+            )
+
+        h_w, h_s = {}, {}
+
+        h_tiles = {}
+
+        def up(half, b, chunks):
+            if (half, b) not in h_tiles:
+                h_tiles[half, b] = ring.tile([P, HALF, PACK], BF16, name="h", align_bytes=64)
+            h = h_tiles[half, b]
+            for c in chunks:
+                tok = slice(HALF * half + CHUNK * c, HALF * half + CHUNK * (c + 1))
+                ga = psum.tile([P, PACK, CHUNK], F32, name="ga", bufs=3)
+                ub = psum.tile([P, PACK, CHUNK], F32, name="ub", bufs=3)
+                for t in range(PACK):
+                    for a in range(2):
+                        cols = slice(P * t, P * (t + 1))
+                        nc.tensor.matmul_mx(out=ga[:, t, :], lhsT=wg_w[a, b][:, cols].bitcast(FP8X4), lhsT_scale=wg_s[a, b][:, cols],
+                                            rhs=v_w[:, a, tok].bitcast(FP4X4), rhs_scale=v_s[:, J * a + tok.start : J * a + tok.stop], start=(a == 0), stop=(a == 1))
+                for t in range(PACK):
+                    for a in range(2):
+                        r0 = PASS * b + P * t
+                        nc.tensor.matmul_mx(out=ub[:, t, :], lhsT=wu_w[:, R * a + r0 : R * a + r0 + P].bitcast(FP8X4), lhsT_scale=wu_s[:, R * a + r0 : R * a + r0 + P],
+                                            rhs=v_w[:, a, tok].bitcast(FP4X4), rhs_scale=v_s[:, J * a + tok.start : J * a + tok.stop], start=(a == 0), stop=(a == 1))
+                act = ring.tile([P, CHUNK, PACK], F32, name="act")
+                nc.scalar.activation(act[:], ga[:].rearrange("p t j -> p j t"), SILU)
+                nc.vector.tensor_tensor(h[:, CHUNK * c : CHUNK * (c + 1), :], ub[:].rearrange("p t j -> p j t"), act[:], MULT)
+
+        def quantize_h(half, b):
+            h = h_tiles[half, b]
+            h_w[half, b] = keep.tile([P, HALF], U32, name=f"h_w{half}{b}", align_bytes=64)
+            h_s[half, b] = keep.tile([P, HALF], U8, name=f"h_s{half}{b}", align_bytes=64)
+            nc.vector.quantize_mx(out=h_w[half, b][:].bitcast(FP8X4), scales=h_s[half, b][:], in_=h[:].rearrange("p j t -> p (j t)"))
+
+        def down(half, n):
+            y = psum.tile([P, HALF], F32, name="y", bufs=2)
+            cols = slice(P * n, P * (n + 1))
+            nc.tensor.matmul_mx(out=y[:], lhsT=wd8_w[:, cols].bitcast(FP8X4), lhsT_scale=wd_s[:, cols],
+                                rhs=h_w[half, 0][:].bitcast(FP8X4), rhs_scale=h_s[half, 0][:], start=True, stop=False)
+            nc.tensor.matmul_mx(out=y[:], lhsT=wd4_w[:, 2 * P * n : 2 * P * (n + 1)].bitcast(FP4X4), lhsT_scale=wd_s[:, N + P * n : N + P * (n + 1)],
+                                rhs=h_w[half, 1][:].bitcast(FP8X4), rhs_scale=h_s[half, 1][:], start=False, stop=True)
+            y_sb = ring.tile([P, HALF], F32, name="y_sb", bufs=4)
+            nc.scalar.copy(y_sb[:], y[:])
+            places = offsets[:, HALF // 16 * half : HALF // 16 * (half + 1)]
+            nc.vector.tensor_tensor(pages[n % 3][:].indirect(places), y_sb[:], gw[n][:, HALF * half : HALF * (half + 1)], MULT)
+
+        def store(n):
+            nc.sync.dma_start(out[P * n : P * (n + 1), :], pages[n % 3][:])
+
+        quantize_wg(0, 0)
+        gather_gate(0)
+        quantize_wg(1, 0)
+        deal_wu()
+        gather_gate(1)
+        up(0, 0, range(4))
+        quantize_h(0, 0)
+        quantize_wg(0, 1)
+        quantize_wg(1, 1)
+        up(1, 0, range(4))
+        quantize_h(1, 0)
+        gather_gate(2)
+        up(0, 1, range(4))
+        quantize_h(0, 1)
+        gather_gate(3)
+        down(0, 0)
+        up(1, 1, (0, 1))
+        down(0, 1)
+        up(1, 1, (2, 3))
+        quantize_h(1, 1)
+        down(0, 2)
+        for n in range(3):
+            down(1, n)
+            store(n)
+        down(0, 3)
+        down(1, 3)
+        store(3)

@@ -23,54 +23,62 @@ HALF = J // 2
 CHUNK = 128
 
 
+def clear_odd(nc, words):
+    n = words.shape[1]
+    nc.vector.memset(words[:, 0 : n // 2 - 1], 0)
+    nc.vector.memset(words[:, n // 2 - 1 : n], 0)
+
+
 def tile_list_modp_gsilu_mix_gate_kernel(tc, tab_words, tab_scales, wg, wu_words, wu_scales, wd8_words, wd8_scales, wd4_words, wd4_scales, gT, wgo, offs, out):
     nc = tc.nc
     with ExitStack() as ctx:
         keep = ctx.enter_context(tc.tile_pool(name="keep", bufs=1))
         ring = ctx.enter_context(tc.tile_pool(name="ring", bufs=3))
-        big = ctx.enter_context(tc.tile_pool(name="big", bufs=3))
         psum = ctx.enter_context(tc.psum_pool(name="psum", bufs=1))
 
         offsets = keep.tile([P, J // 16], U16, name="offsets")
         nc.sync.dma_start(offsets[:], offs)
 
         tab_s = keep.tile([P, T], U8, name="tab_s", align_bytes=64)
-        wu_s_raw = keep.tile([P, 2 * R], U8, name="wu_s_raw", tag="raw_scales", align_bytes=64)
+        wu_s_raw = keep.tile([P, 2 * R], U8, name="wu_s_raw", align_bytes=64)
         v_s = keep.tile([P, 2 * J], U8, name="v_s", align_bytes=64)
+        wd_s = keep.tile([P, 2 * N], U8, name="wd_s", align_bytes=64)
         for q in range(4):
-            nc.vector.memset(tab_s[32 * q : 32 * q + 24, :].bitcast(I32), 0)
-        nc.vector.memset(v_s[:].bitcast(I32), 0)
-        nc.gpsimd.memset(wu_s_raw[:].bitcast(I32), 0)
+            clear_odd(nc, tab_s[32 * q : 32 * q + 24, :].bitcast(I32))
+        clear_odd(nc, wu_s_raw[:].bitcast(I32))
+        nc.gpsimd.memset(v_s[:].bitcast(I32), 0)
+        nc.gpsimd.memset(wd_s[:].bitcast(I32), 0)
         for q in range(4):
-            nc.gpsimd.dma_start(wu_s_raw[32 * q : 32 * q + 4, :].bitcast(I32).rearrange("r (a c) -> r a c", a=2), wu_scales[:, 4 * q : 4 * q + 4, :].bitcast(I32).rearrange("a r c -> r a c"))
+            nc.scalar.dma_start(wu_s_raw[32 * q : 32 * q + 4, :].bitcast(I32).rearrange("r (a c) -> r a c", a=2), wu_scales[:, 4 * q : 4 * q + 4, :].bitcast(I32).rearrange("a r c -> r a c"))
 
         pages = [keep.tile([P, T], F32, name=f"page{n}") for n in range(3)]
-        nc.vector.memset(pages[0][:], 0.0)
-        for n in (1, 2):
+        for n in range(3):
             nc.gpsimd.memset(pages[n][:], 0.0)
 
         for q in range(4):
             nc.sync.dma_start(tab_s[32 * q + 24 : 32 * q + 32, :].bitcast(I32), tab_scales[:, 4 * q : 4 * q + 4, :].bitcast(I32))
-        tab_w = big.tile([P, T], I32, name="tab_w", tag="big")
+        tab_w = keep.tile([P, T], I32, name="tab_w")
         nc.sync.dma_start(tab_w[:], tab_words[0].rearrange("p t i -> p (t i)").bitcast(I32))
 
         wgo_sb = keep.tile([P, J], F32, name="wgo_sb")
-        gates, wg_raw = {}, {}
+        gates = [keep.tile([P, T], F32, name=f"gate{n}") for n in range(4)]
+        wu_raw = keep.tile([P, 2, R], I32, name="wu_raw")
+        wg_raw = {}
+        for b in range(2):
+            for a in range(2):
+                wg_raw[a, b] = keep.tile([P, PACK, PASS], F32, name=f"wg_raw{a}{b}")
 
         def load_wg(a, b):
-            wg_raw[a, b] = big.tile([P, PACK, PASS], F32, name=f"wg_raw{a}{b}", tag="big")
             nc.sync.dma_start(wg_raw[a, b][:], wg[PASS * a : PASS * (a + 1), PASS * b : PASS * (b + 1)].rearrange("(p i) c -> p i c", i=PACK))
 
         def load_gate(n):
-            gates[n] = big.tile([P, T], F32, name=f"gate{n}", tag="big")
             nc.sync.dma_start(gates[n][:], gT[P * n : P * (n + 1), :])
 
         load_wg(0, 0)
+        load_wg(1, 0)
+        nc.sync.dma_start(wu_raw[:], wu_words.rearrange("a p r i -> p a (r i)").bitcast(I32))
         nc.sync.dma_start(wgo_sb[:], wgo)
         load_gate(0)
-        load_wg(1, 0)
-        wu_raw = big.tile([P, 2, R], I32, name="wu_raw", tag="big")
-        nc.sync.dma_start(wu_raw[:], wu_words.rearrange("a p r i -> p a (r i)").bitcast(I32))
         load_gate(1)
         load_wg(0, 1)
         load_wg(1, 1)
@@ -80,6 +88,9 @@ def tile_list_modp_gsilu_mix_gate_kernel(tc, tab_words, tab_scales, wg, wu_words
         nc.sync.dma_start(wd4_w[:].bitcast(I32), wd4_words[0].bitcast(I32))
         load_gate(2)
         load_gate(3)
+        for q in range(4):
+            nc.sync.dma_start(wd_s[32 * q : 32 * q + 4, 0:N].bitcast(I32), wd8_scales[0, 4 * q : 4 * q + 4, :].bitcast(I32))
+            nc.sync.dma_start(wd_s[32 * q : 32 * q + 4, N : 2 * N].bitcast(I32), wd4_scales[0, 4 * q : 4 * q + 4, :].bitcast(I32))
 
         v_s_raw = keep.tile([P, J], U8, name="v_s_raw", align_bytes=64)
         nc.vector.tensor_copy(v_s_raw[:], tab_s[:].indirect(offsets[:]))
@@ -99,22 +110,22 @@ def tile_list_modp_gsilu_mix_gate_kernel(tc, tab_words, tab_scales, wg, wu_words
             wu_s[:].rearrange("p (s t g e) -> p s g t e", s=4, t=PACK, e=16),
             wu_s_raw[:].rearrange("p (s g e t) -> p s g t e", s=4, t=PACK, e=16),
         )
-        wd_s = keep.tile([P, 2 * N], U8, name="wd_s", tag="raw_scales", align_bytes=64)
-        nc.gpsimd.memset(wd_s[:].bitcast(I32), 0)
-        for q in range(4):
-            nc.gpsimd.dma_start(wd_s[32 * q : 32 * q + 4, 0:N].bitcast(I32), wd8_scales[0, 4 * q : 4 * q + 4, :].bitcast(I32))
-            nc.gpsimd.dma_start(wd_s[32 * q : 32 * q + 4, N : 2 * N].bitcast(I32), wd4_scales[0, 4 * q : 4 * q + 4, :].bitcast(I32))
 
-        gw = [keep.tile([P, J], F32, name=f"gw{n}") for n in range(4)]
+        gw = {}
 
-        def gather_gate(n):
+        def gather_gate(n, after):
+            gw[n] = keep.tile([P, J], F32, name=f"gw{n}", tag=after, align_bytes=64)
             nc.vector.tensor_tensor(gw[n][:], gates[n][:].indirect(offsets[:]), wgo_sb[:], MULT)
 
         wg_w, wg_s = {}, {}
 
-        def quantize_wg(a, b):
-            woven = ring.tile([P, PACK, P, PACK], BF16, name="wg_woven", align_bytes=64)
-            nc.scalar.copy(woven[:].rearrange("p t m i -> p m t i"), wg_raw[a, b][:].rearrange("p i (m t) -> p m t i", t=PACK))
+        def quantize_wg(a, b, after):
+            woven = keep.tile([P, PACK, P, PACK], BF16, name=f"woven{a}{b}", tag=after, align_bytes=64)
+            for ms in (slice(0, P // 2), slice(P // 2, P)):
+                nc.scalar.copy(
+                    woven[:, :, ms, :].rearrange("p t m i -> p m t i"),
+                    wg_raw[a, b][:].rearrange("p i (m t) -> p m t i", t=PACK)[:, ms, :, :],
+                )
             wg_w[a, b] = keep.tile([P, PASS], U32, name=f"wg_w{a}{b}", align_bytes=64)
             wg_s[a, b] = keep.tile([P, PASS], U8, name=f"wg_s{a}{b}", align_bytes=64)
             nc.vector.quantize_mx(out=wg_w[a, b][:].bitcast(FP8X4), scales=wg_s[a, b][:], in_=woven[:].rearrange("p t m i -> p (t m i)"))
@@ -133,7 +144,7 @@ def tile_list_modp_gsilu_mix_gate_kernel(tc, tab_words, tab_scales, wg, wu_words
 
         def up(half, b, chunks):
             if (half, b) not in h_tiles:
-                h_tiles[half, b] = ring.tile([P, HALF, PACK], BF16, name="h", align_bytes=64)
+                h_tiles[half, b] = keep.tile([P, HALF, PACK], BF16, name="h", tag=f"h{half}{b}", align_bytes=64)
             h = h_tiles[half, b]
             for c in chunks:
                 tok = slice(HALF * half + CHUNK * c, HALF * half + CHUNK * (c + 1))
@@ -149,7 +160,7 @@ def tile_list_modp_gsilu_mix_gate_kernel(tc, tab_words, tab_scales, wg, wu_words
                         r0 = PASS * b + P * t
                         nc.tensor.matmul_mx(out=ub[:, t, :], lhsT=wu_w[:, R * a + r0 : R * a + r0 + P].bitcast(FP8X4), lhsT_scale=wu_s[:, R * a + r0 : R * a + r0 + P],
                                             rhs=v_w[:, a, tok].bitcast(FP4X4), rhs_scale=v_s[:, J * a + tok.start : J * a + tok.stop], start=(a == 0), stop=(a == 1))
-                act = ring.tile([P, CHUNK, PACK], F32, name="act")
+                act = keep.tile([P, CHUNK, PACK], F32, name="act", tag=f"act{half}{b}{c}", align_bytes=64)
                 nc.scalar.activation(act[:], ga[:].rearrange("p t j -> p j t"), SILU)
                 nc.vector.tensor_tensor(h[:, CHUNK * c : CHUNK * (c + 1), :], ub[:].rearrange("p t j -> p j t"), act[:], MULT)
 
@@ -174,21 +185,21 @@ def tile_list_modp_gsilu_mix_gate_kernel(tc, tab_words, tab_scales, wg, wu_words
         def store(n):
             nc.sync.dma_start(out[P * n : P * (n + 1), :], pages[n % 3][:])
 
-        quantize_wg(0, 0)
-        gather_gate(0)
-        quantize_wg(1, 0)
+        quantize_wg(0, 0, "woven00")
+        quantize_wg(1, 0, "woven10")
         deal_wu()
-        gather_gate(1)
+        gather_gate(0, "woven10")
         up(0, 0, range(4))
         quantize_h(0, 0)
-        quantize_wg(0, 1)
-        quantize_wg(1, 1)
+        gather_gate(1, "act002")
+        quantize_wg(0, 1, "act001")
         up(1, 0, range(4))
+        quantize_wg(1, 1, "act100")
         quantize_h(1, 0)
-        gather_gate(2)
+        gather_gate(2, "h10")
         up(0, 1, range(4))
         quantize_h(0, 1)
-        gather_gate(3)
+        gather_gate(3, "h01")
         down(0, 0)
         up(1, 1, (0, 1))
         down(0, 1)

@@ -62,7 +62,7 @@ def tile_list_modp_gsilu_mix_gate_kernel(tc, tab_words, tab_scales, wg, wu_words
 
         wgo_sb = keep.tile([P, J], F32, name="wgo_sb")
         gates = [keep.tile([P, T], F32, name=f"gate{n}") for n in range(4)]
-        wu_raw = keep.tile([P, 2, R], I32, name="wu_raw")
+        wu_raw = [keep.tile([P, 2, PASS], I32, name=f"wu_raw{b}") for b in range(2)]
         wg_raw = {}
         for b in range(2):
             for a in range(2):
@@ -71,17 +71,21 @@ def tile_list_modp_gsilu_mix_gate_kernel(tc, tab_words, tab_scales, wg, wu_words
         def load_wg(a, b):
             nc.sync.dma_start(wg_raw[a, b][:], wg[PASS * a : PASS * (a + 1), PASS * b : PASS * (b + 1)].rearrange("(p i) c -> p i c", i=PACK))
 
+        def load_wu(b):
+            nc.sync.dma_start(wu_raw[b][:], wu_words[:, :, PASS * b : PASS * (b + 1), :].rearrange("a p r i -> p a (r i)").bitcast(I32))
+
         def load_gate(n):
             nc.sync.dma_start(gates[n][:], gT[P * n : P * (n + 1), :])
 
         load_wg(0, 0)
         load_wg(1, 0)
-        nc.sync.dma_start(wu_raw[:], wu_words.rearrange("a p r i -> p a (r i)").bitcast(I32))
+        load_wu(0)
         nc.sync.dma_start(wgo_sb[:], wgo)
         load_gate(0)
         load_gate(1)
         load_wg(0, 1)
         load_wg(1, 1)
+        load_wu(1)
         wd8_w = keep.tile([P, N], I32, name="wd8_w", align_bytes=64)
         nc.sync.dma_start(wd8_w[:], wd8_words[0].rearrange("p n i -> p (n i)").bitcast(I32))
         wd4_w = keep.tile([P, 2 * N], U8, name="wd4_w", align_bytes=64)
@@ -121,21 +125,22 @@ def tile_list_modp_gsilu_mix_gate_kernel(tc, tab_words, tab_scales, wg, wu_words
 
         def quantize_wg(a, b, after):
             woven = keep.tile([P, PACK, P, PACK], BF16, name=f"woven{a}{b}", tag=after, align_bytes=64)
-            for ms in (slice(0, P // 2), slice(P // 2, P)):
+            for ts in (slice(0, 2), slice(2, 4)):
                 nc.scalar.copy(
-                    woven[:, :, ms, :].rearrange("p t m i -> p m t i"),
-                    wg_raw[a, b][:].rearrange("p i (m t) -> p m t i", t=PACK)[:, ms, :, :],
+                    woven[:, ts, :, :].rearrange("p t m i -> p m i t"),
+                    wg_raw[a, b][:].rearrange("p i (m t) -> p m i t", t=PACK)[:, :, :, ts],
                 )
             wg_w[a, b] = keep.tile([P, PASS], U32, name=f"wg_w{a}{b}", align_bytes=64)
             wg_s[a, b] = keep.tile([P, PASS], U8, name=f"wg_s{a}{b}", align_bytes=64)
             nc.vector.quantize_mx(out=wg_w[a, b][:].bitcast(FP8X4), scales=wg_s[a, b][:], in_=woven[:].rearrange("p t m i -> p (t m i)"))
 
-        wu_w = keep.tile([P, 2 * R], I32, name="wu_w", align_bytes=64)
+        wu_w = {}
 
-        def deal_wu():
+        def deal_wu(b, after):
+            wu_w[b] = keep.tile([P, 2 * PASS], I32, name=f"wu_w{b}", tag=after, align_bytes=64)
             nc.vector.tensor_copy(
-                wu_w[:].rearrange("p (s t g e) -> p s g t e", s=4, t=PACK, e=4),
-                wu_raw[:].rearrange("p a (b g e t) -> p (a b) g t e", b=2, t=PACK, e=4),
+                wu_w[b][:].rearrange("p (a u e m) -> p a u m e", a=2, u=2, e=2),
+                wu_raw[b][:].rearrange("p a (m u e) -> p a u m e", u=2, e=2),
             )
 
         h_w, h_s = {}, {}
@@ -158,11 +163,16 @@ def tile_list_modp_gsilu_mix_gate_kernel(tc, tab_words, tab_scales, wg, wu_words
                 for t in range(PACK):
                     for a in range(2):
                         r0 = PASS * b + P * t
-                        nc.tensor.matmul_mx(out=ub[:, t, :], lhsT=wu_w[:, R * a + r0 : R * a + r0 + P].bitcast(FP8X4), lhsT_scale=wu_s[:, R * a + r0 : R * a + r0 + P],
+                        nc.tensor.matmul_mx(out=ub[:, t, :], lhsT=wu_w[b][:, PASS * a + P * t : PASS * a + P * (t + 1)].bitcast(FP8X4), lhsT_scale=wu_s[:, R * a + r0 : R * a + r0 + P],
                                             rhs=v_w[:, a, tok].bitcast(FP4X4), rhs_scale=v_s[:, J * a + tok.start : J * a + tok.stop], start=(a == 0), stop=(a == 1))
-                act = keep.tile([P, CHUNK, PACK], F32, name="act", tag=f"act{half}{b}{c}", align_bytes=64)
-                nc.scalar.activation(act[:], ga[:].rearrange("p t j -> p j t"), SILU)
-                nc.vector.tensor_tensor(h[:, CHUNK * c : CHUNK * (c + 1), :], ub[:].rearrange("p t j -> p j t"), act[:], MULT)
+                act = keep.tile([P, CHUNK // 2, PACK, 2], F32, name="act", tag=f"act{half}{b}{c}", align_bytes=64)
+                nc.scalar.activation(act[:], ga[:].rearrange("p t (j e) -> p j t e", e=2), SILU)
+                nc.vector.tensor_tensor(
+                    h[:, CHUNK * c : CHUNK * (c + 1), :].rearrange("p (j e) t -> p j t e", e=2),
+                    ub[:].rearrange("p t (j e) -> p j t e", e=2),
+                    act[:],
+                    MULT,
+                )
 
         def quantize_h(half, b):
             h = h_tiles[half, b]
@@ -187,7 +197,7 @@ def tile_list_modp_gsilu_mix_gate_kernel(tc, tab_words, tab_scales, wg, wu_words
 
         quantize_wg(0, 0, "woven00")
         quantize_wg(1, 0, "woven10")
-        deal_wu()
+        deal_wu(0, "wu_w0")
         gather_gate(0, "woven10")
         up(0, 0, range(4))
         quantize_h(0, 0)
@@ -195,6 +205,7 @@ def tile_list_modp_gsilu_mix_gate_kernel(tc, tab_words, tab_scales, wg, wu_words
         quantize_wg(0, 1, "act001")
         up(1, 0, range(4))
         quantize_wg(1, 1, "act100")
+        deal_wu(1, "act102")
         quantize_h(1, 0)
         gather_gate(2, "h10")
         up(0, 1, range(4))

@@ -1,6 +1,7 @@
 from contextlib import ExitStack
 
 import concourse.mybir as mybir
+from concourse.masks import make_identity
 
 K, R, N, T, J = 1024, 1024, 512, 2048, 1024
 FLOPS = 2 * K * R * J * 2 + 2 * R * N * J
@@ -33,40 +34,51 @@ def tile_list_modp_gsilu_mix_gate_kernel(tc, tab_words, tab_scales, wg, wu_words
     nc = tc.nc
     with ExitStack() as ctx:
         keep = ctx.enter_context(tc.tile_pool(name="keep", bufs=1))
-        ring = ctx.enter_context(tc.tile_pool(name="ring", bufs=3))
+        share = ctx.enter_context(tc.tile_pool(name="share", bufs=1))
         psum = ctx.enter_context(tc.psum_pool(name="psum", bufs=1))
 
         offsets = keep.tile([P, J // 16], U16, name="offsets")
         nc.sync.dma_start(offsets[:], offs)
 
+        w_col = keep.tile([P, J // P], F32, name="w_col")
+        nc.sync.dma_start(w_col[:], wgo[0].rearrange("(p c) -> p c", p=P))
+
         tab_s = keep.tile([P, T], U8, name="tab_s", align_bytes=64)
         wu_s_raw = keep.tile([P, 2 * R], U8, name="wu_s_raw", align_bytes=64)
         v_s = keep.tile([P, 2 * J], U8, name="v_s", align_bytes=64)
-        wd_s = keep.tile([P, 2 * N], U8, name="wd_s", align_bytes=64)
+        ident = keep.tile([P, P], F32, name="ident")
+        pages = [keep.tile([P, T], F32, name=f"page{n}") for n in range(2)]
+
+        def clear_page(after):
+            page = keep.tile([P, T], F32, name=f"page{len(pages)}", tag=after, align_bytes=64)
+            nc.gpsimd.memset(page[:], 0.0)
+            pages.append(page)
+
         for q in range(4):
             clear_odd(nc, tab_s[32 * q : 32 * q + 24, :].bitcast(I32))
-        clear_odd(nc, wu_s_raw[:].bitcast(I32))
+        nc.gpsimd.memset(wu_s_raw[:].bitcast(I32), 0)
+        make_identity(nc, ident[:])
         nc.gpsimd.memset(v_s[:].bitcast(I32), 0)
-        nc.gpsimd.memset(wd_s[:].bitcast(I32), 0)
-        for q in range(4):
-            nc.scalar.dma_start(wu_s_raw[32 * q : 32 * q + 4, :].bitcast(I32).rearrange("r (a c) -> r a c", a=2), wu_scales[:, 4 * q : 4 * q + 4, :].bitcast(I32).rearrange("a r c -> r a c"))
-
-        pages = [keep.tile([P, T], F32, name=f"page{n}") for n in range(3)]
-        for n in range(3):
-            nc.gpsimd.memset(pages[n][:], 0.0)
+        for page in pages:
+            nc.gpsimd.memset(page[:], 0.0)
 
         for q in range(4):
             nc.sync.dma_start(tab_s[32 * q + 24 : 32 * q + 32, :].bitcast(I32), tab_scales[:, 4 * q : 4 * q + 4, :].bitcast(I32))
         tab_w = keep.tile([P, T], I32, name="tab_w")
         nc.sync.dma_start(tab_w[:], tab_words[0].rearrange("p t i -> p (t i)").bitcast(I32))
 
-        wgo_sb = keep.tile([P, J], F32, name="wgo_sb")
-        gates = [keep.tile([P, T], F32, name=f"gate{n}") for n in range(4)]
-        wu_raw = [keep.tile([P, 2, PASS], I32, name=f"wu_raw{b}") for b in range(2)]
+        gates = [share.tile([P, T], F32, name=f"gate{n}", offset=4 * T * n, align_bytes=64) for n in range(4)]
+
+        def held(shape, dtype, name, after):
+            if isinstance(after, str):
+                return keep.tile(shape, dtype, name=name, tag=after, align_bytes=64)
+            return share.tile(shape, dtype, name=name, offset=4 * T * after[0] + after[1], align_bytes=64)
+
+        wu_raw = [keep.tile([P, 2, PASS], I32, name=f"wu_raw{b}", tag=f"wu_raw{b}", align_bytes=64) for b in range(2)]
         wg_raw = {}
         for b in range(2):
             for a in range(2):
-                wg_raw[a, b] = keep.tile([P, PACK, PASS], F32, name=f"wg_raw{a}{b}")
+                wg_raw[a, b] = keep.tile([P, PACK, PASS], F32, name=f"wg_raw{a}{b}", tag=f"wg_raw{a}{b}", align_bytes=64)
 
         def load_wg(a, b):
             nc.sync.dma_start(wg_raw[a, b][:], wg[PASS * a : PASS * (a + 1), PASS * b : PASS * (b + 1)].rearrange("(p i) c -> p i c", i=PACK))
@@ -77,62 +89,99 @@ def tile_list_modp_gsilu_mix_gate_kernel(tc, tab_words, tab_scales, wg, wu_words
         def load_gate(n):
             nc.sync.dma_start(gates[n][:], gT[P * n : P * (n + 1), :])
 
+        for q in range(4):
+            nc.sync.dma_start(wu_s_raw[32 * q : 32 * q + 4, :].bitcast(I32).rearrange("r (a c) -> r a c", a=2), wu_scales[:, 4 * q : 4 * q + 4, :].bitcast(I32).rearrange("a r c -> r a c"))
         load_wg(0, 0)
         load_wg(1, 0)
         load_wu(0)
-        nc.sync.dma_start(wgo_sb[:], wgo)
         load_gate(0)
-        load_gate(1)
         load_wg(0, 1)
+        load_gate(1)
         load_wg(1, 1)
         load_wu(1)
+        load_gate(3)
+        load_gate(2)
         wd8_w = keep.tile([P, N], I32, name="wd8_w", align_bytes=64)
         nc.sync.dma_start(wd8_w[:], wd8_words[0].rearrange("p n i -> p (n i)").bitcast(I32))
         wd4_w = keep.tile([P, 2 * N], U8, name="wd4_w", align_bytes=64)
         nc.sync.dma_start(wd4_w[:].bitcast(I32), wd4_words[0].bitcast(I32))
-        load_gate(2)
-        load_gate(3)
-        for q in range(4):
-            nc.sync.dma_start(wd_s[32 * q : 32 * q + 4, 0:N].bitcast(I32), wd8_scales[0, 4 * q : 4 * q + 4, :].bitcast(I32))
-            nc.sync.dma_start(wd_s[32 * q : 32 * q + 4, N : 2 * N].bitcast(I32), wd4_scales[0, 4 * q : 4 * q + 4, :].bitcast(I32))
+
+        planes = {}
+
+        def load_wd_scales(after):
+            wd_s = keep.tile([P, 2 * N], U8, name="wd_s", tag=after, align_bytes=64)
+            nc.gpsimd.memset(wd_s[:].bitcast(I32), 0)
+            for q in range(4):
+                nc.scalar.dma_start(wd_s[32 * q : 32 * q + 4, 0:N].bitcast(I32), wd8_scales[0, 4 * q : 4 * q + 4, :].bitcast(I32))
+                nc.scalar.dma_start(wd_s[32 * q : 32 * q + 4, N : 2 * N].bitcast(I32), wd4_scales[0, 4 * q : 4 * q + 4, :].bitcast(I32))
+            planes["wd"] = wd_s
+
+        wgo_sb = keep.tile([P, P, J // P], F32, name="wgo_sb", tag="wg_raw10", align_bytes=64)
+
+        def spread_wgo():
+            for g in range(2):
+                spread = psum.tile([P, PACK, P], F32, name="spread", tag="y", bufs=2)
+                for c in range(PACK):
+                    nc.tensor.transpose(spread[:, c, :], w_col[:, PACK * g + c : PACK * g + c + 1].to_broadcast([P, P]), ident[:])
+                nc.scalar.copy(wgo_sb[:, :, PACK * g : PACK * (g + 1)], spread[:].rearrange("q c p -> q p c"))
+
+        wgo_all = wgo_sb[:].rearrange("q p c -> q (p c)")
 
         v_s_raw = keep.tile([P, J], U8, name="v_s_raw", align_bytes=64)
         nc.vector.tensor_copy(v_s_raw[:], tab_s[:].indirect(offsets[:]))
         for a in range(2):
             shift = 24 + 4 * a
             nc.scalar.dma_start(v_s[0 : P - shift, J * a : J * (a + 1)].bitcast(I32), v_s_raw[shift:P, :].bitcast(I32))
-        v_pairs = keep.tile([P, J], U32, name="v_pairs")
-        nc.vector.tensor_copy(v_pairs[:], tab_w[:].bitcast(U32).indirect(offsets[:]))
-        v_w = keep.tile([P, 2, J], U16, name="v_w", align_bytes=64)
-        nc.vector.tensor_copy(
-            v_w[:].rearrange("p d (g e) -> p g d e", e=8),
-            v_pairs[:].bitcast(U16).rearrange("p (g e d) -> p g d e", e=8, d=2),
-        )
+        v_pairs = [keep.tile([P, HALF], U32, name=f"v_pairs{half}") for half in range(2)]
+        for half in range(2):
+            nc.vector.tensor_copy(v_pairs[half][:], tab_w[:].bitcast(U32).indirect(offsets[:, HALF // 16 * half : HALF // 16 * (half + 1)]))
+        v_w = [keep.tile([P, 2, HALF], U16, name=f"v_w{half}", align_bytes=64) for half in range(2)]
+        for half in range(2):
+            nc.vector.tensor_copy(
+                v_w[half][:].rearrange("p d (g e) -> p g d e", e=8),
+                v_pairs[half][:].bitcast(U16).rearrange("p (g e d) -> p g d e", e=8, d=2),
+            )
 
-        wu_s = keep.tile([P, 2 * R], U8, name="wu_s", align_bytes=64)
-        nc.vector.tensor_copy(
-            wu_s[:].rearrange("p (s t g e) -> p s g t e", s=4, t=PACK, e=16),
-            wu_s_raw[:].rearrange("p (s g e t) -> p s g t e", s=4, t=PACK, e=16),
-        )
+        wu_s = {}
+
+        def deal_wu_scales(b, after):
+            wu_s[b] = keep.tile([P, 2 * PASS], U8, name=f"wu_s{b}", tag=after, align_bytes=64)
+            nc.vector.tensor_copy(
+                wu_s[b][:].rearrange("p (a t g e) -> p a g t e", a=2, t=PACK, e=16),
+                wu_s_raw[:].rearrange("p (a b g e t) -> p b a g t e", a=2, b=2, t=PACK, e=16)[:, b],
+            )
 
         gw = {}
 
         def gather_gate(n, after):
-            gw[n] = keep.tile([P, J], F32, name=f"gw{n}", tag=after, align_bytes=64)
-            nc.vector.tensor_tensor(gw[n][:], gates[n][:].indirect(offsets[:]), wgo_sb[:], MULT)
+            whole = keep.tile([P, J], F32, name=f"gw{n}", tag=after, align_bytes=64)
+            nc.vector.tensor_tensor(whole[:], gates[n][:].indirect(offsets[:]), wgo_all, MULT)
+            gw[n] = whole[:]
+            for half in range(2):
+                gw[n, half] = whole[:, HALF * half : HALF * (half + 1)]
+
+        def gather_gate_half(n, half, after):
+            part = keep.tile([P, HALF], F32, name=f"gw{n}{half}", tag=after, align_bytes=64)
+            nc.vector.tensor_tensor(part[:], gates[n][:].indirect(offsets[:, HALF // 16 * half : HALF // 16 * (half + 1)]), wgo_all[:, HALF * half : HALF * (half + 1)], MULT)
+            gw[n, half] = part[:]
 
         wg_w, wg_s = {}, {}
 
+        woven = {}
+
+        def weave_wg(a, b, u, copy):
+            if (a, b) not in woven:
+                woven[a, b] = keep.tile([P, PACK, P, PACK], BF16, name=f"woven{a}{b}", tag=f"woven{a}{b}", align_bytes=64)
+            ts = slice(2 * u, 2 * u + 2)
+            copy(
+                woven[a, b][:, ts, :, :].rearrange("p t m i -> p m i t"),
+                wg_raw[a, b][:].rearrange("p i (m t) -> p m i t", t=PACK)[:, :, :, ts],
+            )
+
         def quantize_wg(a, b, after):
-            woven = keep.tile([P, PACK, P, PACK], BF16, name=f"woven{a}{b}", tag=after, align_bytes=64)
-            for ts in (slice(0, 2), slice(2, 4)):
-                nc.scalar.copy(
-                    woven[:, ts, :, :].rearrange("p t m i -> p m i t"),
-                    wg_raw[a, b][:].rearrange("p i (m t) -> p m i t", t=PACK)[:, :, :, ts],
-                )
             wg_w[a, b] = keep.tile([P, PASS], U32, name=f"wg_w{a}{b}", align_bytes=64)
-            wg_s[a, b] = keep.tile([P, PASS], U8, name=f"wg_s{a}{b}", align_bytes=64)
-            nc.vector.quantize_mx(out=wg_w[a, b][:].bitcast(FP8X4), scales=wg_s[a, b][:], in_=woven[:].rearrange("p t m i -> p (t m i)"))
+            wg_s[a, b] = held([P, PASS], U8, f"wg_s{a}{b}", after)
+            nc.vector.quantize_mx(out=wg_w[a, b][:].bitcast(FP8X4), scales=wg_s[a, b][:], in_=woven[a, b][:].rearrange("p t m i -> p (t m i)"))
 
         wu_w = {}
 
@@ -143,29 +192,32 @@ def tile_list_modp_gsilu_mix_gate_kernel(tc, tab_words, tab_scales, wg, wu_words
                 wu_raw[b][:].rearrange("p a (m u e) -> p a u m e", u=2, e=2),
             )
 
-        h_w, h_s = {}, {}
-
+        h_w = [keep.tile([P, J], U32, name=f"h_w{b}", align_bytes=64) for b in range(2)]
+        h_s = [keep.tile([P, J], U8, name=f"h_s{b}", align_bytes=64) for b in range(2)]
         h_tiles = {}
 
-        def up(half, b, chunks):
-            if (half, b) not in h_tiles:
-                h_tiles[half, b] = keep.tile([P, HALF, PACK], BF16, name="h", tag=f"h{half}{b}", align_bytes=64)
-            h = h_tiles[half, b]
-            for c in chunks:
-                tok = slice(HALF * half + CHUNK * c, HALF * half + CHUNK * (c + 1))
+        def new_h(b, first, count, after):
+            h = held([P, CHUNK * count, PACK], BF16, f"h{b}{first}", after)
+            for c in range(count):
+                h_tiles[b, first + c] = (h, c)
+
+        def up(b, chunks, act_tags={}):
+            for chunk in chunks:
+                h, c = h_tiles[b, chunk]
+                tok = slice(CHUNK * chunk, CHUNK * (chunk + 1))
+                words = v_w[tok.start // HALF][:, :, tok.start % HALF : tok.start % HALF + CHUNK]
                 ga = psum.tile([P, PACK, CHUNK], F32, name="ga", bufs=3)
                 ub = psum.tile([P, PACK, CHUNK], F32, name="ub", bufs=3)
                 for t in range(PACK):
                     for a in range(2):
                         cols = slice(P * t, P * (t + 1))
                         nc.tensor.matmul_mx(out=ga[:, t, :], lhsT=wg_w[a, b][:, cols].bitcast(FP8X4), lhsT_scale=wg_s[a, b][:, cols],
-                                            rhs=v_w[:, a, tok].bitcast(FP4X4), rhs_scale=v_s[:, J * a + tok.start : J * a + tok.stop], start=(a == 0), stop=(a == 1))
+                                            rhs=words[:, a, :].bitcast(FP4X4), rhs_scale=v_s[:, J * a + tok.start : J * a + tok.stop], start=(a == 0), stop=(a == 1))
                 for t in range(PACK):
                     for a in range(2):
-                        r0 = PASS * b + P * t
-                        nc.tensor.matmul_mx(out=ub[:, t, :], lhsT=wu_w[b][:, PASS * a + P * t : PASS * a + P * (t + 1)].bitcast(FP8X4), lhsT_scale=wu_s[:, R * a + r0 : R * a + r0 + P],
-                                            rhs=v_w[:, a, tok].bitcast(FP4X4), rhs_scale=v_s[:, J * a + tok.start : J * a + tok.stop], start=(a == 0), stop=(a == 1))
-                act = keep.tile([P, CHUNK // 2, PACK, 2], F32, name="act", tag=f"act{half}{b}{c}", align_bytes=64)
+                        nc.tensor.matmul_mx(out=ub[:, t, :], lhsT=wu_w[b][:, PASS * a + P * t : PASS * a + P * (t + 1)].bitcast(FP8X4), lhsT_scale=wu_s[b][:, PASS * a + P * t : PASS * a + P * (t + 1)],
+                                            rhs=words[:, a, :].bitcast(FP4X4), rhs_scale=v_s[:, J * a + tok.start : J * a + tok.stop], start=(a == 0), stop=(a == 1))
+                act = keep.tile([P, CHUNK // 2, PACK, 2], F32, name="act", tag=act_tags.get(chunk, f"act{b}{chunk}"), align_bytes=64)
                 nc.scalar.activation(act[:], ga[:].rearrange("p t (j e) -> p j t e", e=2), SILU)
                 nc.vector.tensor_tensor(
                     h[:, CHUNK * c : CHUNK * (c + 1), :].rearrange("p (j e) t -> p j t e", e=2),
@@ -174,52 +226,84 @@ def tile_list_modp_gsilu_mix_gate_kernel(tc, tab_words, tab_scales, wg, wu_words
                     MULT,
                 )
 
-        def quantize_h(half, b):
-            h = h_tiles[half, b]
-            h_w[half, b] = keep.tile([P, HALF], U32, name=f"h_w{half}{b}", align_bytes=64)
-            h_s[half, b] = keep.tile([P, HALF], U8, name=f"h_s{half}{b}", align_bytes=64)
-            nc.vector.quantize_mx(out=h_w[half, b][:].bitcast(FP8X4), scales=h_s[half, b][:], in_=h[:].rearrange("p j t -> p (j t)"))
+        def quantize_h(b, first, count):
+            h, c = h_tiles[b, first]
+            tok = slice(CHUNK * first, CHUNK * (first + count))
+            nc.vector.quantize_mx(out=h_w[b][:, tok].bitcast(FP8X4), scales=h_s[b][:, tok], in_=h[:, CHUNK * c : CHUNK * (c + count), :].rearrange("p j t -> p (j t)"))
 
-        def down(half, n):
-            y = psum.tile([P, HALF], F32, name="y", bufs=2)
+        def down(half, n, y_sb):
+            y = psum.tile([P, HALF], F32, name="y", tag="y", bufs=2)
+            wd_s = planes["wd"]
             cols = slice(P * n, P * (n + 1))
+            tok = slice(HALF * half, HALF * (half + 1))
             nc.tensor.matmul_mx(out=y[:], lhsT=wd8_w[:, cols].bitcast(FP8X4), lhsT_scale=wd_s[:, cols],
-                                rhs=h_w[half, 0][:].bitcast(FP8X4), rhs_scale=h_s[half, 0][:], start=True, stop=False)
+                                rhs=h_w[0][:, tok].bitcast(FP8X4), rhs_scale=h_s[0][:, tok], start=True, stop=False)
             nc.tensor.matmul_mx(out=y[:], lhsT=wd4_w[:, 2 * P * n : 2 * P * (n + 1)].bitcast(FP4X4), lhsT_scale=wd_s[:, N + P * n : N + P * (n + 1)],
-                                rhs=h_w[half, 1][:].bitcast(FP8X4), rhs_scale=h_s[half, 1][:], start=False, stop=True)
-            y_sb = ring.tile([P, HALF], F32, name="y_sb", bufs=4)
-            nc.scalar.copy(y_sb[:], y[:])
+                                rhs=h_w[1][:, tok].bitcast(FP8X4), rhs_scale=h_s[1][:, tok], start=False, stop=True)
+            nc.scalar.copy(y_sb, y[:])
+
+        def place_half(half, n, after):
+            y_sb = keep.tile([P, HALF], F32, name=f"y{half}{n}", tag=after, align_bytes=64)
+            down(half, n, y_sb[:])
             places = offsets[:, HALF // 16 * half : HALF // 16 * (half + 1)]
-            nc.vector.tensor_tensor(pages[n % 3][:].indirect(places), y_sb[:], gw[n][:, HALF * half : HALF * (half + 1)], MULT)
+            nc.vector.tensor_tensor(pages[n % 3][:].indirect(places), y_sb[:], gw[n, half], MULT)
+
+        def place_all(n):
+            y_sb = keep.tile([P, J], F32, name=f"y{n}", align_bytes=64)
+            for half in range(2):
+                down(half, n, y_sb[:, HALF * half : HALF * (half + 1)])
+            nc.vector.tensor_tensor(pages[n % 3][:].indirect(offsets[:]), y_sb[:], gw[n], MULT)
 
         def store(n):
             nc.sync.dma_start(out[P * n : P * (n + 1), :], pages[n % 3][:])
 
-        quantize_wg(0, 0, "woven00")
-        quantize_wg(1, 0, "woven10")
-        deal_wu(0, "wu_w0")
-        gather_gate(0, "woven10")
-        up(0, 0, range(4))
-        quantize_h(0, 0)
-        gather_gate(1, "act002")
-        quantize_wg(0, 1, "act001")
-        up(1, 0, range(4))
-        quantize_wg(1, 1, "act100")
-        deal_wu(1, "act102")
-        quantize_h(1, 0)
-        gather_gate(2, "h10")
-        up(0, 1, range(4))
-        quantize_h(0, 1)
-        gather_gate(3, "h01")
-        down(0, 0)
-        up(1, 1, (0, 1))
-        down(0, 1)
-        up(1, 1, (2, 3))
-        quantize_h(1, 1)
-        down(0, 2)
+        deal_wu_scales(0, "wu_s0")
+        deal_wu_scales(1, "wu_s1")
+        weave_wg(0, 0, 0, nc.scalar.copy)
+        weave_wg(0, 0, 1, nc.scalar.copy)
+        weave_wg(1, 0, 0, nc.scalar.copy)
+        quantize_wg(0, 0, "wg_s00")
+        weave_wg(1, 0, 1, nc.vector.tensor_copy)
+        spread_wgo()
+        quantize_wg(1, 0, "wg_s10")
+        deal_wu(0, "woven10")
+        clear_page("wu_raw0")
+        gather_gate(0, "woven00")
+        new_h(0, 0, 2, (0, 0))
+        up(0, (0, 1))
+        weave_wg(0, 1, 0, nc.scalar.copy)
+        weave_wg(0, 1, 1, nc.scalar.copy)
+        gather_gate(1, "gw1")
+        quantize_h(0, 0, 2)
+        new_h(0, 2, 2, (1, 0))
+        up(0, (2, 3), {3: "wg_raw01"})
+        quantize_wg(0, 1, (1, 2048))
+        new_h(0, 4, 4, (1, 4096))
+        up(0, (4,))
+        weave_wg(1, 1, 0, nc.scalar.copy)
+        weave_wg(1, 1, 1, nc.scalar.copy)
+        deal_wu(1, "wg_raw01")
+        quantize_wg(1, 1, "wg_s11")
+        load_wd_scales("woven11")
+        up(0, (5, 6, 7), {5: "wg_raw11"})
+        quantize_h(0, 2, 2)
+        gather_gate(3, "act06")
+        quantize_h(0, 4, 4)
+        new_h(1, 0, 4, (3, 0))
+        up(1, (0, 1))
+        gather_gate_half(2, 0, "act10")
+        up(1, (2, 3))
+        new_h(1, 4, 4, "h14")
+        up(1, (4,))
+        quantize_h(1, 0, 4)
+        gather_gate_half(2, 1, "act13")
+        place_half(0, 0, "y00")
+        up(1, (5, 6, 7))
+        place_half(0, 1, "act15")
+        quantize_h(1, 4, 4)
+        place_half(0, 2, "act17")
         for n in range(3):
-            down(1, n)
+            place_half(1, n, f"y1{n}")
             store(n)
-        down(0, 3)
-        down(1, 3)
+        place_all(3)
         store(3)

@@ -78,7 +78,7 @@ def tile_list_modp_gsilu_mix_gate_kernel(tc, tab_words, tab_scales, wg, wu_words
         wg_raw = {}
         for b in range(2):
             for a in range(2):
-                wg_raw[a, b] = keep.tile([P, PACK, PASS], F32, name=f"wg_raw{a}{b}", tag=f"wg_raw{a}{b}", align_bytes=64)
+                wg_raw[a, b] = share.tile([P, PACK, PASS], F32, name=f"wg_raw{a}{b}", offset=4 * T * (4 + 2 * b + a), align_bytes=64)
 
         def load_wg(a, b):
             nc.sync.dma_start(wg_raw[a, b][:], wg[PASS * a : PASS * (a + 1), PASS * b : PASS * (b + 1)].rearrange("(p i) c -> p i c", i=PACK))
@@ -92,7 +92,16 @@ def tile_list_modp_gsilu_mix_gate_kernel(tc, tab_words, tab_scales, wg, wu_words
         for q in range(4):
             nc.sync.dma_start(wu_s_raw[32 * q : 32 * q + 4, :].bitcast(I32).rearrange("r (a c) -> r a c", a=2), wu_scales[:, 4 * q : 4 * q + 4, :].bitcast(I32).rearrange("a r c -> r a c"))
         load_wg(0, 0)
+        v_s_raw = keep.tile([P, J], U8, name="v_s_raw", align_bytes=64)
+        nc.vector.tensor_copy(v_s_raw[:], tab_s[:].indirect(offsets[:]))
+
+        def shift_planes():
+            for a in range(2):
+                shift = 24 + 4 * a
+                nc.sync.dma_start(v_s[0 : P - shift, J * a : J * (a + 1)].bitcast(I32), v_s_raw[shift:P, :].bitcast(I32))
+
         load_wg(1, 0)
+        shift_planes()
         load_wu(0)
         load_gate(0)
         load_wg(0, 1)
@@ -116,7 +125,7 @@ def tile_list_modp_gsilu_mix_gate_kernel(tc, tab_words, tab_scales, wg, wu_words
                 nc.scalar.dma_start(wd_s[32 * q : 32 * q + 4, N : 2 * N].bitcast(I32), wd4_scales[0, 4 * q : 4 * q + 4, :].bitcast(I32))
             planes["wd"] = wd_s
 
-        wgo_sb = keep.tile([P, P, J // P], F32, name="wgo_sb", tag="wg_raw10", align_bytes=64)
+        wgo_sb = keep.tile([P, P, J // P], F32, name="wgo_sb")
 
         def spread_wgo():
             for g in range(2):
@@ -127,11 +136,6 @@ def tile_list_modp_gsilu_mix_gate_kernel(tc, tab_words, tab_scales, wg, wu_words
 
         wgo_all = wgo_sb[:].rearrange("q p c -> q (p c)")
 
-        v_s_raw = keep.tile([P, J], U8, name="v_s_raw", align_bytes=64)
-        nc.vector.tensor_copy(v_s_raw[:], tab_s[:].indirect(offsets[:]))
-        for a in range(2):
-            shift = 24 + 4 * a
-            nc.scalar.dma_start(v_s[0 : P - shift, J * a : J * (a + 1)].bitcast(I32), v_s_raw[shift:P, :].bitcast(I32))
         v_pairs = [keep.tile([P, HALF], U32, name=f"v_pairs{half}") for half in range(2)]
         for half in range(2):
             nc.vector.tensor_copy(v_pairs[half][:], tab_w[:].bitcast(U32).indirect(offsets[:, HALF // 16 * half : HALF // 16 * (half + 1)]))
@@ -154,7 +158,7 @@ def tile_list_modp_gsilu_mix_gate_kernel(tc, tab_words, tab_scales, wg, wu_words
         gw = {}
 
         def gather_gate(n, after):
-            whole = keep.tile([P, J], F32, name=f"gw{n}", tag=after, align_bytes=64)
+            whole = held([P, J], F32, f"gw{n}", after)
             nc.vector.tensor_tensor(whole[:], gates[n][:].indirect(offsets[:]), wgo_all, MULT)
             gw[n] = whole[:]
             for half in range(2):
@@ -186,7 +190,7 @@ def tile_list_modp_gsilu_mix_gate_kernel(tc, tab_words, tab_scales, wg, wu_words
         wu_w = {}
 
         def deal_wu(b, after):
-            wu_w[b] = keep.tile([P, 2 * PASS], I32, name=f"wu_w{b}", tag=after, align_bytes=64)
+            wu_w[b] = held([P, 2 * PASS], I32, f"wu_w{b}", after)
             nc.vector.tensor_copy(
                 wu_w[b][:].rearrange("p (a u e m) -> p a u m e", a=2, u=2, e=2),
                 wu_raw[b][:].rearrange("p a (m u e) -> p a u m e", u=2, e=2),
@@ -217,7 +221,7 @@ def tile_list_modp_gsilu_mix_gate_kernel(tc, tab_words, tab_scales, wg, wu_words
                     for a in range(2):
                         nc.tensor.matmul_mx(out=ub[:, t, :], lhsT=wu_w[b][:, PASS * a + P * t : PASS * a + P * (t + 1)].bitcast(FP8X4), lhsT_scale=wu_s[b][:, PASS * a + P * t : PASS * a + P * (t + 1)],
                                             rhs=words[:, a, :].bitcast(FP4X4), rhs_scale=v_s[:, J * a + tok.start : J * a + tok.stop], start=(a == 0), stop=(a == 1))
-                act = keep.tile([P, CHUNK // 2, PACK, 2], F32, name="act", tag=act_tags.get(chunk, f"act{b}{chunk}"), align_bytes=64)
+                act = held([P, CHUNK // 2, PACK, 2], F32, f"act{b}{chunk}", act_tags.get(chunk, f"act{b}{chunk}"))
                 nc.scalar.activation(act[:], ga[:].rearrange("p t (j e) -> p j t e", e=2), SILU)
                 nc.vector.tensor_tensor(
                     h[:, CHUNK * c : CHUNK * (c + 1), :].rearrange("p (j e) t -> p j t e", e=2),
@@ -257,6 +261,7 @@ def tile_list_modp_gsilu_mix_gate_kernel(tc, tab_words, tab_scales, wg, wu_words
         def store(n):
             nc.sync.dma_start(out[P * n : P * (n + 1), :], pages[n % 3][:])
 
+        spread_wgo()
         deal_wu_scales(0, "wu_s0")
         deal_wu_scales(1, "wu_s1")
         weave_wg(0, 0, 0, nc.scalar.copy)
@@ -264,7 +269,6 @@ def tile_list_modp_gsilu_mix_gate_kernel(tc, tab_words, tab_scales, wg, wu_words
         weave_wg(1, 0, 0, nc.scalar.copy)
         quantize_wg(0, 0, "wg_s00")
         weave_wg(1, 0, 1, nc.vector.tensor_copy)
-        spread_wgo()
         quantize_wg(1, 0, "wg_s10")
         deal_wu(0, "woven10")
         clear_page("wu_raw0")
@@ -276,18 +280,18 @@ def tile_list_modp_gsilu_mix_gate_kernel(tc, tab_words, tab_scales, wg, wu_words
         gather_gate(1, "gw1")
         quantize_h(0, 0, 2)
         new_h(0, 2, 2, (1, 0))
-        up(0, (2, 3), {3: "wg_raw01"})
+        up(0, (2, 3), {3: (6, 0)})
         quantize_wg(0, 1, (1, 2048))
         new_h(0, 4, 4, (1, 4096))
-        up(0, (4,))
+        up(0, (4,), {4: (6, 2048)})
         weave_wg(1, 1, 0, nc.scalar.copy)
         weave_wg(1, 1, 1, nc.scalar.copy)
-        deal_wu(1, "wg_raw01")
+        deal_wu(1, (6, 0))
         quantize_wg(1, 1, "wg_s11")
+        up(0, (5, 6, 7), {5: (7, 0), 6: (7, 2048), 7: (7, 4096)})
         load_wd_scales("woven11")
-        up(0, (5, 6, 7), {5: "wg_raw11"})
         quantize_h(0, 2, 2)
-        gather_gate(3, "act06")
+        gather_gate(3, (7, 0))
         quantize_h(0, 4, 4)
         new_h(1, 0, 4, (3, 0))
         up(1, (0, 1))

@@ -43,29 +43,30 @@ def tile_list_modp_gsilu_mix_gate_kernel(tc, tab_words, tab_scales, wg, wu_words
         w_col = keep.tile([P, J // P], F32, name="w_col")
         nc.sync.dma_start(w_col[:], wgo[0].rearrange("(p c) -> p c", p=P))
 
-        tab_s = keep.tile([P, T], U8, name="tab_s", align_bytes=64)
-        wu_s_raw = keep.tile([P, 2 * R], U8, name="wu_s_raw", align_bytes=64)
-        v_s = keep.tile([P, 2 * J], U8, name="v_s", align_bytes=64)
+        tab_s = keep.tile([P, T], U8, name="tab_s", tag="tab_s", align_bytes=64)
+        wu_s_raw = keep.tile([P, 2 * R], U8, name="wu_s_raw", tag="wu_s_raw", align_bytes=64)
+        v_s1 = keep.tile([P, J], U8, name="v_s1", align_bytes=64)
+        wd_s = keep.tile([P, 2 * N], U8, name="wd_s", align_bytes=64)
         ident = keep.tile([P, P], F32, name="ident")
         pages = [keep.tile([P, T], F32, name=f"page{n}") for n in range(2)]
 
         def clear_page(after):
-            page = keep.tile([P, T], F32, name=f"page{len(pages)}", tag=after, align_bytes=64)
+            page = held([P, T], F32, f"page{len(pages)}", after)
             nc.gpsimd.memset(page[:], 0.0)
             pages.append(page)
 
-        for q in range(4):
-            clear_odd(nc, tab_s[32 * q : 32 * q + 24, :].bitcast(I32))
+        clear_odd(nc, tab_s[:].bitcast(I32))
         nc.gpsimd.memset(wu_s_raw[:].bitcast(I32), 0)
         make_identity(nc, ident[:])
-        nc.gpsimd.memset(v_s[:].bitcast(I32), 0)
+        nc.gpsimd.memset(v_s1[96:P, :].bitcast(I32), 0)
+        nc.gpsimd.memset(wd_s[:].bitcast(I32), 0)
         for page in pages:
             nc.gpsimd.memset(page[:], 0.0)
 
-        for q in range(4):
-            nc.sync.dma_start(tab_s[32 * q + 24 : 32 * q + 32, :].bitcast(I32), tab_scales[:, 4 * q : 4 * q + 4, :].bitcast(I32))
-        tab_w = keep.tile([P, T], I32, name="tab_w")
+        tab_w = keep.tile([P, T], I32, name="tab_w", tag="tab_w", align_bytes=64)
         nc.sync.dma_start(tab_w[:], tab_words[0].rearrange("p t i -> p (t i)").bitcast(I32))
+        for q in range(4):
+            nc.sync.dma_start(tab_s[32 * q : 32 * q + 8, :].bitcast(I32), tab_scales[:, 4 * q : 4 * q + 4, :].bitcast(I32))
 
         gates = [share.tile([P, T], F32, name=f"gate{n}", offset=4 * T * n, align_bytes=64) for n in range(4)]
 
@@ -86,44 +87,45 @@ def tile_list_modp_gsilu_mix_gate_kernel(tc, tab_words, tab_scales, wg, wu_words
         def load_wu(b):
             nc.sync.dma_start(wu_raw[b][:], wu_words[:, :, PASS * b : PASS * (b + 1), :].rearrange("a p r i -> p a (r i)").bitcast(I32))
 
+        wd8_w = keep.tile([P, N], I32, name="wd8_w", align_bytes=64)
+        wd4_w = keep.tile([P, 2 * N], U8, name="wd4_w", align_bytes=64)
+
+        def load_wd():
+            nc.sync.dma_start(wd8_w[:], wd8_words[0].rearrange("p n i -> p (n i)").bitcast(I32))
+            nc.sync.dma_start(wd4_w[:].bitcast(I32), wd4_words[0].bitcast(I32))
+
+        def load_wd_scales(q):
+            nc.sync.dma_start(wd_s[32 * q : 32 * q + 4, 0:N].bitcast(I32), wd8_scales[0, 4 * q : 4 * q + 4, :].bitcast(I32))
+            nc.sync.dma_start(wd_s[32 * q : 32 * q + 4, N : 2 * N].bitcast(I32), wd4_scales[0, 4 * q : 4 * q + 4, :].bitcast(I32))
+
         def load_gate(n):
             nc.sync.dma_start(gates[n][:], gT[P * n : P * (n + 1), :])
 
+        load_wg(0, 0)
         for q in range(4):
             nc.sync.dma_start(wu_s_raw[32 * q : 32 * q + 4, :].bitcast(I32).rearrange("r (a c) -> r a c", a=2), wu_scales[:, 4 * q : 4 * q + 4, :].bitcast(I32).rearrange("a r c -> r a c"))
-        load_wg(0, 0)
         v_s_raw = keep.tile([P, J], U8, name="v_s_raw", align_bytes=64)
         nc.vector.tensor_copy(v_s_raw[:], tab_s[:].indirect(offsets[:]))
 
         def shift_planes():
-            for a in range(2):
-                shift = 24 + 4 * a
-                nc.sync.dma_start(v_s[0 : P - shift, J * a : J * (a + 1)].bitcast(I32), v_s_raw[shift:P, :].bitcast(I32))
+            nc.sync.dma_start(v_s1[0:112, :].bitcast(I32), v_s_raw[4:116, :].bitcast(I32))
+
+        v_s = [v_s_raw, v_s1]
 
         load_wg(1, 0)
-        shift_planes()
         load_wu(0)
+        shift_planes()
         load_gate(0)
         load_wg(0, 1)
         load_gate(1)
         load_wg(1, 1)
         load_wu(1)
-        load_gate(3)
         load_gate(2)
-        wd8_w = keep.tile([P, N], I32, name="wd8_w", align_bytes=64)
-        nc.sync.dma_start(wd8_w[:], wd8_words[0].rearrange("p n i -> p (n i)").bitcast(I32))
-        wd4_w = keep.tile([P, 2 * N], U8, name="wd4_w", align_bytes=64)
-        nc.sync.dma_start(wd4_w[:].bitcast(I32), wd4_words[0].bitcast(I32))
+        load_wd()
+        for q in range(4):
+            load_wd_scales(q)
+        load_gate(3)
 
-        planes = {}
-
-        def load_wd_scales(after):
-            wd_s = keep.tile([P, 2 * N], U8, name="wd_s", tag=after, align_bytes=64)
-            nc.gpsimd.memset(wd_s[:].bitcast(I32), 0)
-            for q in range(4):
-                nc.scalar.dma_start(wd_s[32 * q : 32 * q + 4, 0:N].bitcast(I32), wd8_scales[0, 4 * q : 4 * q + 4, :].bitcast(I32))
-                nc.scalar.dma_start(wd_s[32 * q : 32 * q + 4, N : 2 * N].bitcast(I32), wd4_scales[0, 4 * q : 4 * q + 4, :].bitcast(I32))
-            planes["wd"] = wd_s
 
         wgo_sb = keep.tile([P, P, J // P], F32, name="wgo_sb")
 
@@ -139,7 +141,7 @@ def tile_list_modp_gsilu_mix_gate_kernel(tc, tab_words, tab_scales, wg, wu_words
         v_pairs = [keep.tile([P, HALF], U32, name=f"v_pairs{half}") for half in range(2)]
         for half in range(2):
             nc.vector.tensor_copy(v_pairs[half][:], tab_w[:].bitcast(U32).indirect(offsets[:, HALF // 16 * half : HALF // 16 * (half + 1)]))
-        v_w = [keep.tile([P, 2, HALF], U16, name=f"v_w{half}", align_bytes=64) for half in range(2)]
+        v_w = [keep.tile([P, 2, HALF], U16, name=f"v_w{half}", tag=("tab_s", "tab_w")[half], align_bytes=64) for half in range(2)]
         for half in range(2):
             nc.vector.tensor_copy(
                 v_w[half][:].rearrange("p d (g e) -> p g d e", e=8),
@@ -165,7 +167,7 @@ def tile_list_modp_gsilu_mix_gate_kernel(tc, tab_words, tab_scales, wg, wu_words
                 gw[n, half] = whole[:, HALF * half : HALF * (half + 1)]
 
         def gather_gate_half(n, half, after):
-            part = keep.tile([P, HALF], F32, name=f"gw{n}{half}", tag=after, align_bytes=64)
+            part = held([P, HALF], F32, f"gw{n}{half}", after)
             nc.vector.tensor_tensor(part[:], gates[n][:].indirect(offsets[:, HALF // 16 * half : HALF // 16 * (half + 1)]), wgo_all[:, HALF * half : HALF * (half + 1)], MULT)
             gw[n, half] = part[:]
 
@@ -205,7 +207,7 @@ def tile_list_modp_gsilu_mix_gate_kernel(tc, tab_words, tab_scales, wg, wu_words
             for c in range(count):
                 h_tiles[b, first + c] = (h, c)
 
-        def up(b, chunks, act_tags={}):
+        def up(b, chunks, act_tags={}, on_gpsimd=False):
             for chunk in chunks:
                 h, c = h_tiles[b, chunk]
                 tok = slice(CHUNK * chunk, CHUNK * (chunk + 1))
@@ -216,11 +218,18 @@ def tile_list_modp_gsilu_mix_gate_kernel(tc, tab_words, tab_scales, wg, wu_words
                     for a in range(2):
                         cols = slice(P * t, P * (t + 1))
                         nc.tensor.matmul_mx(out=ga[:, t, :], lhsT=wg_w[a, b][:, cols].bitcast(FP8X4), lhsT_scale=wg_s[a, b][:, cols],
-                                            rhs=words[:, a, :].bitcast(FP4X4), rhs_scale=v_s[:, J * a + tok.start : J * a + tok.stop], start=(a == 0), stop=(a == 1))
+                                            rhs=words[:, a, :].bitcast(FP4X4), rhs_scale=v_s[a][:, tok], start=(a == 0), stop=(a == 1))
                 for t in range(PACK):
                     for a in range(2):
                         nc.tensor.matmul_mx(out=ub[:, t, :], lhsT=wu_w[b][:, PASS * a + P * t : PASS * a + P * (t + 1)].bitcast(FP8X4), lhsT_scale=wu_s[b][:, PASS * a + P * t : PASS * a + P * (t + 1)],
-                                            rhs=words[:, a, :].bitcast(FP4X4), rhs_scale=v_s[:, J * a + tok.start : J * a + tok.stop], start=(a == 0), stop=(a == 1))
+                                            rhs=words[:, a, :].bitcast(FP4X4), rhs_scale=v_s[a][:, tok], start=(a == 0), stop=(a == 1))
+                if on_gpsimd:
+                    act = held([P, CHUNK, PACK], F32, f"act{b}{chunk}", f"act{b}{chunk}")
+                    nc.scalar.activation(act[:].rearrange("p (j e) t -> p j t e", e=2), ga[:].rearrange("p t (j e) -> p j t e", e=2), SILU)
+                    ub_sb = keep.tile([P, CHUNK, PACK], F32, name=f"ub_sb{b}{chunk}", tag=f"ub_sb{b}{chunk}", align_bytes=64)
+                    nc.scalar.copy(ub_sb[:].rearrange("p (j e) t -> p j t e", e=2), ub[:].rearrange("p t (j e) -> p j t e", e=2))
+                    nc.gpsimd.tensor_tensor(h[:, CHUNK * c : CHUNK * (c + 1), :], ub_sb[:], act[:], MULT)
+                    continue
                 act = held([P, CHUNK // 2, PACK, 2], F32, f"act{b}{chunk}", act_tags.get(chunk, f"act{b}{chunk}"))
                 nc.scalar.activation(act[:], ga[:].rearrange("p t (j e) -> p j t e", e=2), SILU)
                 nc.vector.tensor_tensor(
@@ -235,27 +244,39 @@ def tile_list_modp_gsilu_mix_gate_kernel(tc, tab_words, tab_scales, wg, wu_words
             tok = slice(CHUNK * first, CHUNK * (first + count))
             nc.vector.quantize_mx(out=h_w[b][:, tok].bitcast(FP8X4), scales=h_s[b][:, tok], in_=h[:, CHUNK * c : CHUNK * (c + count), :].rearrange("p j t -> p (j t)"))
 
-        def down(half, n, y_sb):
+        def down(half, n):
             y = psum.tile([P, HALF], F32, name="y", tag="y", bufs=2)
-            wd_s = planes["wd"]
             cols = slice(P * n, P * (n + 1))
             tok = slice(HALF * half, HALF * (half + 1))
             nc.tensor.matmul_mx(out=y[:], lhsT=wd8_w[:, cols].bitcast(FP8X4), lhsT_scale=wd_s[:, cols],
                                 rhs=h_w[0][:, tok].bitcast(FP8X4), rhs_scale=h_s[0][:, tok], start=True, stop=False)
             nc.tensor.matmul_mx(out=y[:], lhsT=wd4_w[:, 2 * P * n : 2 * P * (n + 1)].bitcast(FP4X4), lhsT_scale=wd_s[:, N + P * n : N + P * (n + 1)],
                                 rhs=h_w[1][:, tok].bitcast(FP8X4), rhs_scale=h_s[1][:, tok], start=False, stop=True)
-            nc.scalar.copy(y_sb, y[:])
+            return y
 
         def place_half(half, n, after):
-            y_sb = keep.tile([P, HALF], F32, name=f"y{half}{n}", tag=after, align_bytes=64)
-            down(half, n, y_sb[:])
+            y_sb = held([P, HALF], F32, f"y{half}{n}", after)
+            nc.scalar.copy(y_sb[:], down(half, n)[:])
             places = offsets[:, HALF // 16 * half : HALF // 16 * (half + 1)]
             nc.vector.tensor_tensor(pages[n % 3][:].indirect(places), y_sb[:], gw[n, half], MULT)
+
+        def product(n, on_gpsimd, after):
+            z = held([P, HALF], F32, f"z{n}", after)
+            if on_gpsimd:
+                y_sb = keep.tile([P, HALF], F32, name=f"y0{n}", align_bytes=64)
+                nc.scalar.copy(y_sb[:], down(0, n)[:])
+                nc.gpsimd.tensor_tensor(z[:], y_sb[:], gw[n, 0], MULT)
+            else:
+                nc.vector.tensor_tensor(z[:], down(0, n)[:], gw[n, 0], MULT)
+            return z
+
+        def place_product(n, z):
+            nc.vector.tensor_copy(pages[n][:].indirect(offsets[:, 0 : HALF // 16]), z[:])
 
         def place_all(n):
             y_sb = keep.tile([P, J], F32, name=f"y{n}", align_bytes=64)
             for half in range(2):
-                down(half, n, y_sb[:, HALF * half : HALF * (half + 1)])
+                nc.scalar.copy(y_sb[:, HALF * half : HALF * (half + 1)], down(half, n)[:])
             nc.vector.tensor_tensor(pages[n % 3][:].indirect(offsets[:]), y_sb[:], gw[n], MULT)
 
         def store(n):
@@ -273,14 +294,15 @@ def tile_list_modp_gsilu_mix_gate_kernel(tc, tab_words, tab_scales, wg, wu_words
         deal_wu(0, "woven10")
         clear_page("wu_raw0")
         gather_gate(0, "woven00")
-        new_h(0, 0, 2, (0, 0))
-        up(0, (0, 1))
+        new_h(0, 0, 3, (0, 0))
+        up(0, (0, 1, 2))
         weave_wg(0, 1, 0, nc.scalar.copy)
         weave_wg(0, 1, 1, nc.scalar.copy)
         gather_gate(1, "gw1")
         quantize_h(0, 0, 2)
-        new_h(0, 2, 2, (1, 0))
-        up(0, (2, 3), {3: (6, 0)})
+        quantize_h(0, 2, 1)
+        new_h(0, 3, 1, (1, 0))
+        up(0, (3,), {3: (6, 0)})
         quantize_wg(0, 1, (1, 2048))
         new_h(0, 4, 4, (1, 4096))
         up(0, (4,), {4: (6, 2048)})
@@ -289,23 +311,23 @@ def tile_list_modp_gsilu_mix_gate_kernel(tc, tab_words, tab_scales, wg, wu_words
         deal_wu(1, (6, 0))
         quantize_wg(1, 1, "wg_s11")
         up(0, (5, 6, 7), {5: (7, 0), 6: (7, 2048), 7: (7, 4096)})
-        load_wd_scales("woven11")
-        quantize_h(0, 2, 2)
-        gather_gate(3, (7, 0))
+        quantize_h(0, 3, 1)
         quantize_h(0, 4, 4)
-        new_h(1, 0, 4, (3, 0))
+        gather_gate_half(2, 0, (7, 2048))
+        new_h(1, 0, 4, "h10")
         up(1, (0, 1))
-        gather_gate_half(2, 0, "act10")
+        gather_gate_half(2, 1, "act10")
         up(1, (2, 3))
-        new_h(1, 4, 4, "h14")
-        up(1, (4,))
         quantize_h(1, 0, 4)
-        gather_gate_half(2, 1, "act13")
-        place_half(0, 0, "y00")
-        up(1, (5, 6, 7))
-        place_half(0, 1, "act15")
+        gather_gate(3, "act13")
+        z0 = product(0, False, (3, 0))
+        z1 = product(1, True, (3, 2048))
+        new_h(1, 4, 4, (3, 4096))
+        up(1, (4, 5, 6, 7), {}, True)
+        place_product(0, z0)
+        place_product(1, z1)
         quantize_h(1, 4, 4)
-        place_half(0, 2, "act17")
+        place_half(0, 2, "ub_sb17")
         for n in range(3):
             place_half(1, n, f"y1{n}")
             store(n)

@@ -24,12 +24,6 @@ HALF = J // 2
 CHUNK = 128
 
 
-def clear_odd(nc, words):
-    n = words.shape[1]
-    nc.vector.memset(words[:, 0 : n // 2 - 1], 0)
-    nc.vector.memset(words[:, n // 2 - 1 : n], 0)
-
-
 def tile_list_modp_gsilu_mix_gate_kernel(tc, tab_words, tab_scales, wg, wu_words, wu_scales, wd8_words, wd8_scales, wd4_words, wd4_scales, gT, wgo, offs, out):
     nc = tc.nc
     with ExitStack() as ctx:
@@ -55,18 +49,18 @@ def tile_list_modp_gsilu_mix_gate_kernel(tc, tab_words, tab_scales, wg, wu_words
             nc.gpsimd.memset(page[:], 0.0)
             pages.append(page)
 
-        clear_odd(nc, tab_s[:].bitcast(I32))
-        nc.gpsimd.memset(wu_s_raw[:].bitcast(I32), 0)
+        nc.vector.memset(tab_s[:].bitcast(I32), 0)
         make_identity(nc, ident[:])
+        nc.gpsimd.memset(wu_s_raw[:].bitcast(I32), 0)
         nc.gpsimd.memset(v_s1[96:P, :].bitcast(I32), 0)
         nc.gpsimd.memset(wd_s[:].bitcast(I32), 0)
         for page in pages:
             nc.gpsimd.memset(page[:], 0.0)
 
-        tab_w = keep.tile([P, T], I32, name="tab_w", tag="tab_w", align_bytes=64)
+        for r in range(4):
+            nc.sync.dma_start(tab_s[r:P:16, :].bitcast(I32), tab_scales.rearrange("a (q r) c -> r q a c", r=4)[r].bitcast(I32))
+        tab_w = keep.tile([P, T], I32, name="tab_w")
         nc.sync.dma_start(tab_w[:], tab_words[0].rearrange("p t i -> p (t i)").bitcast(I32))
-        for q in range(4):
-            nc.sync.dma_start(tab_s[32 * q : 32 * q + 8, :].bitcast(I32), tab_scales[:, 4 * q : 4 * q + 4, :].bitcast(I32))
 
         gates = [share.tile([P, T], F32, name=f"gate{n}", offset=4 * T * n, align_bytes=64) for n in range(4)]
 
@@ -98,23 +92,26 @@ def tile_list_modp_gsilu_mix_gate_kernel(tc, tab_words, tab_scales, wg, wu_words
             nc.sync.dma_start(wd_s[32 * q : 32 * q + 4, 0:N].bitcast(I32), wd8_scales[0, 4 * q : 4 * q + 4, :].bitcast(I32))
             nc.sync.dma_start(wd_s[32 * q : 32 * q + 4, N : 2 * N].bitcast(I32), wd4_scales[0, 4 * q : 4 * q + 4, :].bitcast(I32))
 
+        def load_wu_scales():
+            for q in range(4):
+                nc.sync.dma_start(wu_s_raw[32 * q : 32 * q + 4, :].bitcast(I32).rearrange("r (a c) -> r a c", a=2), wu_scales[:, 4 * q : 4 * q + 4, :].bitcast(I32).rearrange("a r c -> r a c"))
+
         def load_gate(n):
             nc.sync.dma_start(gates[n][:], gT[P * n : P * (n + 1), :])
 
+        load_wu_scales()
         load_wg(0, 0)
-        for q in range(4):
-            nc.sync.dma_start(wu_s_raw[32 * q : 32 * q + 4, :].bitcast(I32).rearrange("r (a c) -> r a c", a=2), wu_scales[:, 4 * q : 4 * q + 4, :].bitcast(I32).rearrange("a r c -> r a c"))
         v_s_raw = keep.tile([P, J], U8, name="v_s_raw", align_bytes=64)
         nc.vector.tensor_copy(v_s_raw[:], tab_s[:].indirect(offsets[:]))
 
         def shift_planes():
-            nc.sync.dma_start(v_s1[0:112, :].bitcast(I32), v_s_raw[4:116, :].bitcast(I32))
+            nc.sync.dma_start(v_s1[0:112, :].bitcast(I32), v_s_raw[16:P, :].bitcast(I32))
 
         v_s = [v_s_raw, v_s1]
 
         load_wg(1, 0)
-        load_wu(0)
         shift_planes()
+        load_wu(0)
         load_gate(0)
         load_wg(0, 1)
         load_gate(1)
@@ -141,7 +138,7 @@ def tile_list_modp_gsilu_mix_gate_kernel(tc, tab_words, tab_scales, wg, wu_words
         v_pairs = [keep.tile([P, HALF], U32, name=f"v_pairs{half}") for half in range(2)]
         for half in range(2):
             nc.vector.tensor_copy(v_pairs[half][:], tab_w[:].bitcast(U32).indirect(offsets[:, HALF // 16 * half : HALF // 16 * (half + 1)]))
-        v_w = [keep.tile([P, 2, HALF], U16, name=f"v_w{half}", tag=("tab_s", "tab_w")[half], align_bytes=64) for half in range(2)]
+        v_w = [keep.tile([P, 2, HALF], U16, name=f"v_w{half}", align_bytes=64) for half in range(2)]
         for half in range(2):
             nc.vector.tensor_copy(
                 v_w[half][:].rearrange("p d (g e) -> p g d e", e=8),
@@ -151,7 +148,7 @@ def tile_list_modp_gsilu_mix_gate_kernel(tc, tab_words, tab_scales, wg, wu_words
         wu_s = {}
 
         def deal_wu_scales(b, after):
-            wu_s[b] = keep.tile([P, 2 * PASS], U8, name=f"wu_s{b}", tag=after, align_bytes=64)
+            wu_s[b] = held([P, 2 * PASS], U8, f"wu_s{b}", after)
             nc.vector.tensor_copy(
                 wu_s[b][:].rearrange("p (a t g e) -> p a g t e", a=2, t=PACK, e=16),
                 wu_s_raw[:].rearrange("p (a b g e t) -> p b a g t e", a=2, b=2, t=PACK, e=16)[:, b],

@@ -42,20 +42,17 @@ def tile_list_modp_gsilu_mix_gate_kernel(tc, tab_words, tab_scales, wg, wu_words
         v_s1 = keep.tile([P, J], U8, name="v_s1", align_bytes=64)
         wd_s = keep.tile([P, 2 * N], U8, name="wd_s", align_bytes=64)
         ident = keep.tile([P, P], F32, name="ident")
-        pages = [keep.tile([P, T], F32, name=f"page{n}") for n in range(2)]
-
-        def clear_page(after):
-            page = held([P, T], F32, f"page{len(pages)}", after)
-            nc.gpsimd.memset(page[:], 0.0)
-            pages.append(page)
+        pages = [keep.tile([P, T], F32, name=f"page{n}") for n in range(3)]
 
         nc.vector.memset(tab_s[:].bitcast(I32), 0)
         make_identity(nc, ident[:])
         nc.gpsimd.memset(wu_s_raw[:].bitcast(I32), 0)
-        nc.gpsimd.memset(v_s1[96:P, :].bitcast(I32), 0)
+        nc.gpsimd.memset(v_s1[:].bitcast(I32), 0)
         nc.gpsimd.memset(wd_s[:].bitcast(I32), 0)
-        for page in pages:
+        for page in pages[:2]:
             nc.gpsimd.memset(page[:], 0.0)
+        nc.vector.memset(pages[2][:, 0 : T // 2 - 1], 0.0)
+        nc.vector.memset(pages[2][:, T // 2 - 1 : T], 0.0)
 
         for r in range(4):
             nc.sync.dma_start(tab_s[r:P:16, :].bitcast(I32), tab_scales.rearrange("a (q r) c -> r q a c", r=4)[r].bitcast(I32))
@@ -105,7 +102,8 @@ def tile_list_modp_gsilu_mix_gate_kernel(tc, tab_words, tab_scales, wg, wu_words
         nc.vector.tensor_copy(v_s_raw[:], tab_s[:].indirect(offsets[:]))
 
         def shift_planes():
-            nc.sync.dma_start(v_s1[0:112, :].bitcast(I32), v_s_raw[16:P, :].bitcast(I32))
+            for q in range(4):
+                nc.sync.dma_start(v_s1[32 * q : 32 * q + 4, :].bitcast(I32), v_s_raw[32 * q + 16 : 32 * q + 20, :].bitcast(I32))
 
         v_s = [v_s_raw, v_s1]
 
@@ -289,7 +287,6 @@ def tile_list_modp_gsilu_mix_gate_kernel(tc, tab_words, tab_scales, wg, wu_words
         weave_wg(1, 0, 1, nc.vector.tensor_copy)
         quantize_wg(1, 0, "wg_s10")
         deal_wu(0, "woven10")
-        clear_page("wu_raw0")
         gather_gate(0, "woven00")
         new_h(0, 0, 3, (0, 0))
         up(0, (0, 1, 2))

@@ -40,7 +40,7 @@ def tile_list_modp_gsilu_mix_gate_kernel(tc, tab_words, tab_scales, wg, wu_words
         tab_s = keep.tile([P, T], U8, name="tab_s", tag="tab_s", align_bytes=64)
         wu_s_raw = keep.tile([P, 2 * R], U8, name="wu_s_raw", tag="wu_s_raw", align_bytes=64)
         v_s1 = keep.tile([P, J], U8, name="v_s1", align_bytes=64)
-        wd_s = keep.tile([P, 2 * N], U8, name="wd_s", align_bytes=64)
+        wd_s = keep.tile([P, N], U8, name="wd_s", align_bytes=64)
         ident = keep.tile([P, P], F32, name="ident")
         pages = [keep.tile([P, T], F32, name=f"page{n}") for n in range(3)]
 
@@ -66,7 +66,7 @@ def tile_list_modp_gsilu_mix_gate_kernel(tc, tab_words, tab_scales, wg, wu_words
                 return keep.tile(shape, dtype, name=name, tag=after, align_bytes=64)
             return share.tile(shape, dtype, name=name, offset=4 * T * after[0] + after[1], align_bytes=64)
 
-        wu_raw = [keep.tile([P, 2, PASS], I32, name=f"wu_raw{b}", tag=f"wu_raw{b}", align_bytes=64) for b in range(2)]
+        wu_raw = [held([P, 2, PASS], I32, "wu_raw0", (8, 0)), held([P, 2, PASS], I32, "wu_raw1", "wu_raw1")]
         wg_raw = {}
         for b in range(2):
             for a in range(2):
@@ -85,9 +85,9 @@ def tile_list_modp_gsilu_mix_gate_kernel(tc, tab_words, tab_scales, wg, wu_words
             nc.sync.dma_start(wd8_w[:], wd8_words[0].rearrange("p n i -> p (n i)").bitcast(I32))
             nc.sync.dma_start(wd4_w[:].bitcast(I32), wd4_words[0].bitcast(I32))
 
-        def load_wd_scales(q):
-            nc.sync.dma_start(wd_s[32 * q : 32 * q + 4, 0:N].bitcast(I32), wd8_scales[0, 4 * q : 4 * q + 4, :].bitcast(I32))
-            nc.sync.dma_start(wd_s[32 * q : 32 * q + 4, N : 2 * N].bitcast(I32), wd4_scales[0, 4 * q : 4 * q + 4, :].bitcast(I32))
+        def load_wd_scales(first, scales):
+            for q in range(4):
+                nc.sync.dma_start(wd_s[32 * q + first : 32 * q + first + 4, :].bitcast(I32), scales[0, 4 * q : 4 * q + 4, :].bitcast(I32))
 
         def load_wu_scales():
             for q in range(4):
@@ -107,18 +107,18 @@ def tile_list_modp_gsilu_mix_gate_kernel(tc, tab_words, tab_scales, wg, wu_words
 
         v_s = [v_s_raw, v_s1]
 
-        load_wg(1, 0)
         shift_planes()
         load_wu(0)
+        load_wg(1, 0)
         load_gate(0)
+        load_wd_scales(4, wd8_scales)
         load_wg(0, 1)
         load_gate(1)
         load_wg(1, 1)
         load_wu(1)
         load_gate(2)
         load_wd()
-        for q in range(4):
-            load_wd_scales(q)
+        load_wd_scales(0, wd4_scales)
         load_gate(3)
 
 
@@ -126,7 +126,7 @@ def tile_list_modp_gsilu_mix_gate_kernel(tc, tab_words, tab_scales, wg, wu_words
 
         def spread_wgo():
             for g in range(2):
-                spread = psum.tile([P, PACK, P], F32, name="spread", tag="y", bufs=2)
+                spread = psum.tile([P, PACK, P], F32, name=f"spread{g}", tag=f"y{g}")
                 for c in range(PACK):
                     nc.tensor.transpose(spread[:, c, :], w_col[:, PACK * g + c : PACK * g + c + 1].to_broadcast([P, P]), ident[:])
                 nc.scalar.copy(wgo_sb[:, :, PACK * g : PACK * (g + 1)], spread[:].rearrange("q c p -> q p c"))
@@ -170,13 +170,13 @@ def tile_list_modp_gsilu_mix_gate_kernel(tc, tab_words, tab_scales, wg, wu_words
 
         woven = {}
 
-        def weave_wg(a, b, u, copy):
+        def weave_wg(a, b, u, copy, ms=slice(0, P)):
             if (a, b) not in woven:
                 woven[a, b] = keep.tile([P, PACK, P, PACK], BF16, name=f"woven{a}{b}", tag=f"woven{a}{b}", align_bytes=64)
             ts = slice(2 * u, 2 * u + 2)
             copy(
-                woven[a, b][:, ts, :, :].rearrange("p t m i -> p m i t"),
-                wg_raw[a, b][:].rearrange("p i (m t) -> p m i t", t=PACK)[:, :, :, ts],
+                woven[a, b][:, ts, ms, :].rearrange("p t m i -> p m i t"),
+                wg_raw[a, b][:].rearrange("p i (m t) -> p m i t", t=PACK)[:, ms, :, ts],
             )
 
         def quantize_wg(a, b, after):
@@ -194,59 +194,74 @@ def tile_list_modp_gsilu_mix_gate_kernel(tc, tab_words, tab_scales, wg, wu_words
             )
 
         h_w = [keep.tile([P, J], U32, name=f"h_w{b}", align_bytes=64) for b in range(2)]
-        h_s = [keep.tile([P, J], U8, name=f"h_s{b}", align_bytes=64) for b in range(2)]
+        h_s = {(0, 0): held([P, HALF], U8, "h_s00", "h_s00"), (0, 1): held([P, HALF], U8, "h_s01", "h_s01")}
+        for half in range(2):
+            h_s[1, half] = keep.tile([P, HALF], U8, name=f"h_s1{half}", align_bytes=64)
         h_tiles = {}
+        ub, act, staged = {}, {}, {}
+        turns = {"ga": [], "ub": []}
 
         def new_h(b, first, count, after):
             h = held([P, CHUNK * count, PACK], BF16, f"h{b}{first}", after)
             for c in range(count):
                 h_tiles[b, first + c] = (h, c)
 
-        def up(b, chunks, act_tags={}, on_gpsimd=False):
-            for chunk in chunks:
-                h, c = h_tiles[b, chunk]
-                tok = slice(CHUNK * chunk, CHUNK * (chunk + 1))
-                words = v_w[tok.start // HALF][:, :, tok.start % HALF : tok.start % HALF + CHUNK]
-                ga = psum.tile([P, PACK, CHUNK], F32, name="ga", bufs=3)
-                ub = psum.tile([P, PACK, CHUNK], F32, name="ub", bufs=3)
-                for t in range(PACK):
-                    for a in range(2):
-                        cols = slice(P * t, P * (t + 1))
-                        nc.tensor.matmul_mx(out=ga[:, t, :], lhsT=wg_w[a, b][:, cols].bitcast(FP8X4), lhsT_scale=wg_s[a, b][:, cols],
-                                            rhs=words[:, a, :].bitcast(FP4X4), rhs_scale=v_s[a][:, tok], start=(a == 0), stop=(a == 1))
-                for t in range(PACK):
-                    for a in range(2):
-                        nc.tensor.matmul_mx(out=ub[:, t, :], lhsT=wu_w[b][:, PASS * a + P * t : PASS * a + P * (t + 1)].bitcast(FP8X4), lhsT_scale=wu_s[b][:, PASS * a + P * t : PASS * a + P * (t + 1)],
-                                            rhs=words[:, a, :].bitcast(FP4X4), rhs_scale=v_s[a][:, tok], start=(a == 0), stop=(a == 1))
-                if on_gpsimd:
-                    act = held([P, CHUNK, PACK], F32, f"act{b}{chunk}", f"act{b}{chunk}")
-                    nc.scalar.activation(act[:].rearrange("p (j e) t -> p j t e", e=2), ga[:].rearrange("p t (j e) -> p j t e", e=2), SILU)
-                    ub_sb = keep.tile([P, CHUNK, PACK], F32, name=f"ub_sb{b}{chunk}", tag=f"ub_sb{b}{chunk}", align_bytes=64)
-                    nc.scalar.copy(ub_sb[:].rearrange("p (j e) t -> p j t e", e=2), ub[:].rearrange("p t (j e) -> p j t e", e=2))
-                    nc.gpsimd.tensor_tensor(h[:, CHUNK * c : CHUNK * (c + 1), :], ub_sb[:], act[:], MULT)
-                    continue
-                act = held([P, CHUNK // 2, PACK, 2], F32, f"act{b}{chunk}", act_tags.get(chunk, f"act{b}{chunk}"))
-                nc.scalar.activation(act[:], ga[:].rearrange("p t (j e) -> p j t e", e=2), SILU)
-                nc.vector.tensor_tensor(
-                    h[:, CHUNK * c : CHUNK * (c + 1), :].rearrange("p (j e) t -> p j t e", e=2),
-                    ub[:].rearrange("p t (j e) -> p j t e", e=2),
-                    act[:],
-                    MULT,
-                )
+        def first_product(name, spare, words, scales, chunk):
+            tok = slice(CHUNK * chunk, CHUNK * (chunk + 1))
+            table = v_w[tok.start // HALF][:, :, tok.start % HALF : tok.start % HALF + CHUNK]
+            if not spare:
+                turns[name].append(chunk)
+            bank = psum.tile([P, PACK, CHUNK], F32, name=f"{name}{len(ub)}_{len(act)}", tag=spare if spare else f"{name}{len(turns[name]) % 3}")
+            for t in range(PACK):
+                cols = slice(P * t, P * (t + 1))
+                for a in range(2):
+                    nc.tensor.matmul_mx(out=bank[:, t, :], lhsT=words[a][:, cols].bitcast(FP8X4), lhsT_scale=scales[a][:, cols],
+                                        rhs=table[:, a, :].bitcast(FP4X4), rhs_scale=v_s[a][:, tok], start=(a == 0), stop=(a == 1))
+            return bank[:].rearrange("p t (j e) -> p j t e", e=2)
+
+        def up(b, chunk, stage=None, spare=False):
+            words = [wu_w[b][:, PASS * a : PASS * (a + 1)] for a in range(2)]
+            scales = [wu_s[b][:, PASS * a : PASS * (a + 1)] for a in range(2)]
+            ub[b, chunk] = first_product("ub", spare, words, scales, chunk)
+            if stage is not None:
+                staged[b, chunk] = held([P, CHUNK, PACK], F32, f"ub_sb{b}{chunk}", stage)
+                nc.scalar.copy(staged[b, chunk][:].rearrange("p (j e) t -> p j t e", e=2), ub[b, chunk])
+
+        def gate(b, chunk, after=None, woven_order=False, spare=False):
+            ga = first_product("ga", spare, [wg_w[a, b][:] for a in range(2)], [wg_s[a, b][:] for a in range(2)], chunk)
+            name = f"act{b}{chunk}"
+            if woven_order:
+                act[b, chunk] = held([P, CHUNK, PACK], F32, name, after or name)
+                nc.scalar.activation(act[b, chunk][:].rearrange("p (j e) t -> p j t e", e=2), ga, SILU)
+            else:
+                act[b, chunk] = held([P, CHUNK // 2, PACK, 2], F32, name, after or name)
+                nc.scalar.activation(act[b, chunk][:], ga, SILU)
+
+        def multiply(b, chunk):
+            h, c = h_tiles[b, chunk]
+            rows = h[:, CHUNK * c : CHUNK * (c + 1), :]
+            if (b, chunk) in staged:
+                nc.gpsimd.tensor_tensor(rows, staged[b, chunk][:], act[b, chunk][:], MULT)
+            else:
+                nc.vector.tensor_tensor(rows.rearrange("p (j e) t -> p j t e", e=2), ub[b, chunk], act[b, chunk][:], MULT)
+
+        def both(b, chunk, after=None, stage=None):
+            gate(b, chunk, after, stage is not None)
+            up(b, chunk, stage)
 
         def quantize_h(b, first, count):
             h, c = h_tiles[b, first]
             tok = slice(CHUNK * first, CHUNK * (first + count))
-            nc.vector.quantize_mx(out=h_w[b][:, tok].bitcast(FP8X4), scales=h_s[b][:, tok], in_=h[:, CHUNK * c : CHUNK * (c + count), :].rearrange("p j t -> p (j t)"))
+            nc.vector.quantize_mx(out=h_w[b][:, tok].bitcast(FP8X4), scales=h_s[b, tok.start // HALF][:, tok.start % HALF : tok.start % HALF + CHUNK * count], in_=h[:, CHUNK * c : CHUNK * (c + count), :].rearrange("p j t -> p (j t)"))
 
         def down(half, n):
-            y = psum.tile([P, HALF], F32, name="y", tag="y", bufs=2)
+            y = psum.tile([P, HALF], F32, name=f"y{half}{n}_psum", tag=f"y{n % 2 if half else int(n % 3 == 0)}")
             cols = slice(P * n, P * (n + 1))
             tok = slice(HALF * half, HALF * (half + 1))
-            nc.tensor.matmul_mx(out=y[:], lhsT=wd8_w[:, cols].bitcast(FP8X4), lhsT_scale=wd_s[:, cols],
-                                rhs=h_w[0][:, tok].bitcast(FP8X4), rhs_scale=h_s[0][:, tok], start=True, stop=False)
-            nc.tensor.matmul_mx(out=y[:], lhsT=wd4_w[:, 2 * P * n : 2 * P * (n + 1)].bitcast(FP4X4), lhsT_scale=wd_s[:, N + P * n : N + P * (n + 1)],
-                                rhs=h_w[1][:, tok].bitcast(FP8X4), rhs_scale=h_s[1][:, tok], start=False, stop=True)
+            nc.tensor.matmul_mx(out=y[:], lhsT=wd8_w[:, cols].bitcast(FP8X4), lhsT_scale=wd_s[4:P, cols],
+                                rhs=h_w[0][:, tok].bitcast(FP8X4), rhs_scale=h_s[0, half][:], start=True, stop=False)
+            nc.tensor.matmul_mx(out=y[:], lhsT=wd4_w[:, 2 * P * n : 2 * P * (n + 1)].bitcast(FP4X4), lhsT_scale=wd_s[:, cols],
+                                rhs=h_w[1][:, tok].bitcast(FP8X4), rhs_scale=h_s[1, half][:], start=False, stop=True)
             return y
 
         def place_half(half, n, after):
@@ -262,7 +277,7 @@ def tile_list_modp_gsilu_mix_gate_kernel(tc, tab_words, tab_scales, wg, wu_words
                 nc.scalar.copy(y_sb[:], down(0, n)[:])
                 nc.gpsimd.tensor_tensor(z[:], y_sb[:], gw[n, 0], MULT)
             else:
-                nc.vector.tensor_tensor(z[:], down(0, n)[:], gw[n, 0], MULT)
+                nc.vector.tensor_tensor(z[:], gw[n, 0], down(0, n)[:], MULT)
             return z
 
         def place_product(n, z):
@@ -279,49 +294,63 @@ def tile_list_modp_gsilu_mix_gate_kernel(tc, tab_words, tab_scales, wg, wu_words
 
         spread_wgo()
         deal_wu_scales(0, "wu_s0")
-        deal_wu_scales(1, "wu_s1")
         weave_wg(0, 0, 0, nc.scalar.copy)
         weave_wg(0, 0, 1, nc.scalar.copy)
-        weave_wg(1, 0, 0, nc.scalar.copy)
-        quantize_wg(0, 0, "wg_s00")
+        deal_wu(0, "wu_w0")
+        deal_wu_scales(1, (8, 0))
+        quantize_wg(0, 0, (8, 1024))
+        weave_wg(1, 0, 0, nc.scalar.copy, slice(0, 80))
         weave_wg(1, 0, 1, nc.vector.tensor_copy)
+        weave_wg(1, 0, 0, nc.vector.tensor_copy, slice(80, P))
         quantize_wg(1, 0, "wg_s10")
-        deal_wu(0, "woven10")
         gather_gate(0, "woven00")
-        new_h(0, 0, 3, (0, 0))
-        up(0, (0, 1, 2))
+        new_h(0, 0, 4, "h00")
+        for chunk in range(4):
+            gate(0, chunk)
+            up(0, chunk, None, "y0" if chunk == 3 else None)
+            multiply(0, chunk)
         weave_wg(0, 1, 0, nc.scalar.copy)
         weave_wg(0, 1, 1, nc.scalar.copy)
         gather_gate(1, "gw1")
         quantize_h(0, 0, 2)
-        quantize_h(0, 2, 1)
-        new_h(0, 3, 1, (1, 0))
-        up(0, (3,), {3: (6, 0)})
+        quantize_h(0, 2, 2)
         quantize_wg(0, 1, (1, 2048))
-        new_h(0, 4, 4, (1, 4096))
-        up(0, (4,), {4: (6, 2048)})
+        new_h(0, 4, 4, (0, 4096))
+        for chunk in (4, 5):
+            both(0, chunk, (6, 2048 * (chunk - 3)))
+            multiply(0, chunk)
         weave_wg(1, 1, 0, nc.scalar.copy)
-        weave_wg(1, 1, 1, nc.scalar.copy)
-        deal_wu(1, (6, 0))
+        weave_wg(1, 1, 1, nc.scalar.copy, slice(0, 80))
+        weave_wg(1, 1, 1, nc.vector.tensor_copy, slice(80, P))
+        deal_wu(1, "wu_w1")
         quantize_wg(1, 1, "wg_s11")
-        up(0, (5, 6, 7), {5: (7, 0), 6: (7, 2048), 7: (7, 4096)})
-        quantize_h(0, 3, 1)
+        turns["ga"].append(None)
+        turns["ub"].append(None)
+        for chunk in (6, 7):
+            both(0, chunk, (7, 2048 * (chunk - 6)))
+            multiply(0, chunk)
         quantize_h(0, 4, 4)
-        gather_gate_half(2, 0, (7, 2048))
+        gather_gate_half(2, 0, (7, 0))
         new_h(1, 0, 4, "h10")
-        up(1, (0, 1))
-        gather_gate_half(2, 1, "act10")
-        up(1, (2, 3))
-        quantize_h(1, 0, 4)
-        gather_gate(3, "act13")
-        z0 = product(0, False, (3, 0))
-        z1 = product(1, True, (3, 2048))
-        new_h(1, 4, 4, (3, 4096))
-        up(1, (4, 5, 6, 7), {}, True)
+        for chunk in range(4):
+            gate(1, chunk)
+            up(1, chunk, None, f"y{chunk}" if chunk < 2 else None)
+            multiply(1, chunk)
+        quantize_h(1, 0, 2)
+        quantize_h(1, 2, 2)
+        gather_gate_half(2, 1, "act13")
+        z0 = product(0, False, (5, 2048))
+        z1 = product(1, True, (2, 2048))
+        z2 = product(2, True, (5, 0))
+        new_h(1, 4, 4, (2, 4096))
+        for chunk in range(4, 8):
+            both(1, chunk, None, f"ub_sb1{chunk}")
+            multiply(1, chunk)
         place_product(0, z0)
         place_product(1, z1)
+        place_product(2, z2)
         quantize_h(1, 4, 4)
-        place_half(0, 2, "ub_sb17")
+        gather_gate(3, "ub_sb17")
         for n in range(3):
             place_half(1, n, f"y1{n}")
             store(n)

@@ -22,6 +22,7 @@ PACK = 4
 PASS = P * PACK
 HALF = J // 2
 CHUNK = 128
+KIB = 1024
 
 
 def tile_list_modp_gsilu_mix_gate_kernel(tc, tab_words, tab_scales, wg, wu_words, wu_scales, wd8_words, wd8_scales, wd4_words, wd4_scales, gT, wgo, offs, out):
@@ -31,55 +32,64 @@ def tile_list_modp_gsilu_mix_gate_kernel(tc, tab_words, tab_scales, wg, wu_words
         share = ctx.enter_context(tc.tile_pool(name="share", bufs=1))
         psum = ctx.enter_context(tc.psum_pool(name="psum", bufs=1))
 
+        region = {"gate0": 0, "gate1": 8, "gate2": 16, "gate3": 24, "wg00": 32, "wg10": 40, "wg01": 48, "wg11": 56,
+                  "wu0": 104, "wu1": 68, "woven0": 72, "woven1": 80, "table": 88, "wgo": 96, "gw0": 102}
+
+        def place(shape, dtype, name, where=None):
+            if where is None:
+                return keep.tile(shape, dtype, name=name, align_bytes=64)
+            return share.tile(shape, dtype, name=name, offset=KIB * (region[where[0]] + where[1]), align_bytes=64)
+
+        def bank(number, shape, name):
+            return psum.tile(shape, F32, name=name, tag=f"bank{number}")
+
         offsets = keep.tile([P, J // 16], U16, name="offsets")
         nc.sync.dma_start(offsets[:], offs)
 
-        w_col = keep.tile([P, J // P], F32, name="w_col")
-        nc.sync.dma_start(w_col[:], wgo[0].rearrange("(p c) -> p c", p=P))
+        def places(half):
+            return offsets[:, HALF // 16 * half : HALF // 16 * (half + 1)]
 
-        tab_s = keep.tile([P, T], U8, name="tab_s", tag="tab_s", align_bytes=64)
-        wu_s_raw = keep.tile([P, 2 * R], U8, name="wu_s_raw", tag="wu_s_raw", align_bytes=64)
-        v_s1 = keep.tile([P, J], U8, name="v_s1", align_bytes=64)
-        wd_s = keep.tile([P, N], U8, name="wd_s", align_bytes=64)
-        ident = keep.tile([P, P], F32, name="ident")
-        pages = [keep.tile([P, T], F32, name=f"page{n}") for n in range(3)]
+        w_col = place([P, J // P], F32, "w_col")
+        tab_s = place([P, T], U8, "tab_s")
+        tab_w = place([P, T], I32, "tab_w", ("table", 0))
+        wu_s_raw = place([P, 2 * R], U8, "wu_s_raw")
+        v_s_raw = place([P, J], U8, "v_s_raw")
+        v_s = place([P, 2, J], U8, "v_s")
+        wd_s = place([P, N], U8, "wd_s")
+        ident = place([P, P], F32, "ident")
+        pages = [place([P, T], F32, f"page{n}") for n in range(3)]
+        gates = [place([P, T], F32, f"gate{n}", (f"gate{n}", 0)) for n in range(4)]
+        wu_raw = [place([P, 2, PASS], I32, f"wu_raw{b}", (f"wu{b}", 0)) for b in range(2)]
+        wg_raw = {(a, b): place([P, PACK, PASS], F32, f"wg_raw{a}{b}", (f"wg{a}{b}", 0)) for a in range(2) for b in range(2)}
+        woven = {(a, b): place([P, PACK, P, PACK], BF16, f"woven{a}{b}", (f"woven{b}", 4 * a)) for a in range(2) for b in range(2)}
+        wd8_w = place([P, N], I32, "wd8_w")
+        wd4_w = place([P, 2 * N], U8, "wd4_w")
 
-        nc.vector.memset(tab_s[:].bitcast(I32), 0)
-        make_identity(nc, ident[:])
         nc.gpsimd.memset(wu_s_raw[:].bitcast(I32), 0)
-        nc.gpsimd.memset(v_s1[:].bitcast(I32), 0)
+        nc.gpsimd.memset(tab_s[0:96, :].bitcast(I32), 0)
+        nc.vector.memset(pages[2][:, 0 : T // 2 - 1], 0.0)
+        nc.vector.memset(pages[2][:, T // 2 - 1 : T], 0.0)
+        make_identity(nc, ident[:])
+        nc.gpsimd.memset(v_s[:].bitcast(I32), 0)
         nc.gpsimd.memset(wd_s[:].bitcast(I32), 0)
         for page in pages[:2]:
             nc.gpsimd.memset(page[:], 0.0)
-        nc.vector.memset(pages[2][:, 0 : T // 2 - 1], 0.0)
-        nc.vector.memset(pages[2][:, T // 2 - 1 : T], 0.0)
 
-        for r in range(4):
-            nc.sync.dma_start(tab_s[r:P:16, :].bitcast(I32), tab_scales.rearrange("a (q r) c -> r q a c", r=4)[r].bitcast(I32))
-        tab_w = keep.tile([P, T], I32, name="tab_w")
-        nc.sync.dma_start(tab_w[:], tab_words[0].rearrange("p t i -> p (t i)").bitcast(I32))
-
-        gates = [share.tile([P, T], F32, name=f"gate{n}", offset=4 * T * n, align_bytes=64) for n in range(4)]
-
-        def held(shape, dtype, name, after):
-            if isinstance(after, str):
-                return keep.tile(shape, dtype, name=name, tag=after, align_bytes=64)
-            return share.tile(shape, dtype, name=name, offset=4 * T * after[0] + after[1], align_bytes=64)
-
-        wu_raw = [held([P, 2, PASS], I32, "wu_raw0", (8, 0)), held([P, 2, PASS], I32, "wu_raw1", "wu_raw1")]
-        wg_raw = {}
-        for b in range(2):
+        def load_table_scales():
             for a in range(2):
-                wg_raw[a, b] = share.tile([P, PACK, PASS], F32, name=f"wg_raw{a}{b}", offset=4 * T * (4 + 2 * b + a), align_bytes=64)
+                nc.sync.dma_start(tab_s[96 + a : P : 2, :].bitcast(I32), tab_scales[a].bitcast(I32))
+
+        def load_table_words():
+            nc.sync.dma_start(tab_w[:], tab_words[0].rearrange("p t i -> p (t i)").bitcast(I32))
+
+        def load_wgo():
+            nc.sync.dma_start(w_col[:], wgo[0].rearrange("(p c) -> p c", p=P))
 
         def load_wg(a, b):
             nc.sync.dma_start(wg_raw[a, b][:], wg[PASS * a : PASS * (a + 1), PASS * b : PASS * (b + 1)].rearrange("(p i) c -> p i c", i=PACK))
 
         def load_wu(b):
             nc.sync.dma_start(wu_raw[b][:], wu_words[:, :, PASS * b : PASS * (b + 1), :].rearrange("a p r i -> p a (r i)").bitcast(I32))
-
-        wd8_w = keep.tile([P, N], I32, name="wd8_w", align_bytes=64)
-        wd4_w = keep.tile([P, 2 * N], U8, name="wd4_w", align_bytes=64)
 
         def load_wd():
             nc.sync.dma_start(wd8_w[:], wd8_words[0].rearrange("p n i -> p (n i)").bitcast(I32))
@@ -96,18 +106,20 @@ def tile_list_modp_gsilu_mix_gate_kernel(tc, tab_words, tab_scales, wg, wu_words
         def load_gate(n):
             nc.sync.dma_start(gates[n][:], gT[P * n : P * (n + 1), :])
 
-        load_wu_scales()
-        load_wg(0, 0)
-        v_s_raw = keep.tile([P, J], U8, name="v_s_raw", align_bytes=64)
-        nc.vector.tensor_copy(v_s_raw[:], tab_s[:].indirect(offsets[:]))
+        def gather_table_scales():
+            nc.vector.tensor_copy(v_s_raw[:], tab_s[:].indirect(offsets[:]))
 
-        def shift_planes():
+        def move_table_scales():
             for q in range(4):
-                nc.sync.dma_start(v_s1[32 * q : 32 * q + 4, :].bitcast(I32), v_s_raw[32 * q + 16 : 32 * q + 20, :].bitcast(I32))
+                nc.sync.dma_start(v_s[32 * q : 32 * q + 4].rearrange("r a c -> r (a c)").bitcast(I32), v_s_raw[96 + 8 * q : 96 + 8 * q + 8, :].bitcast(I32))
 
-        v_s = [v_s_raw, v_s1]
-
-        shift_planes()
+        load_table_scales()
+        load_table_words()
+        load_wu_scales()
+        load_wgo()
+        load_wg(0, 0)
+        gather_table_scales()
+        move_table_scales()
         load_wu(0)
         load_wg(1, 0)
         load_gate(0)
@@ -121,238 +133,243 @@ def tile_list_modp_gsilu_mix_gate_kernel(tc, tab_words, tab_scales, wg, wu_words
         load_wd_scales(0, wd4_scales)
         load_gate(3)
 
+        wgo_sb = place([P, P, J // P], F32, "wgo_sb")
+        wgo_all = wgo_sb[:].rearrange("q p c -> q (p c)")
 
-        wgo_sb = keep.tile([P, P, J // P], F32, name="wgo_sb")
-
-        def spread_wgo():
+        def spread_wgo(banks):
             for g in range(2):
-                spread = psum.tile([P, PACK, P], F32, name=f"spread{g}", tag=f"y{g}")
+                spread = bank(banks[g], [P, PACK, P], f"spread{g}")
                 for c in range(PACK):
                     nc.tensor.transpose(spread[:, c, :], w_col[:, PACK * g + c : PACK * g + c + 1].to_broadcast([P, P]), ident[:])
                 nc.scalar.copy(wgo_sb[:, :, PACK * g : PACK * (g + 1)], spread[:].rearrange("q c p -> q p c"))
 
-        wgo_all = wgo_sb[:].rearrange("q p c -> q (p c)")
+        v_pairs = [place([P, HALF], U32, f"v_pairs{half}") for half in range(2)]
+        v_w = [place([P, 2, HALF], U16, f"v_w{half}") for half in range(2)]
 
-        v_pairs = [keep.tile([P, HALF], U32, name=f"v_pairs{half}") for half in range(2)]
-        for half in range(2):
-            nc.vector.tensor_copy(v_pairs[half][:], tab_w[:].bitcast(U32).indirect(offsets[:, HALF // 16 * half : HALF // 16 * (half + 1)]))
-        v_w = [keep.tile([P, 2, HALF], U16, name=f"v_w{half}", align_bytes=64) for half in range(2)]
-        for half in range(2):
-            nc.vector.tensor_copy(
-                v_w[half][:].rearrange("p d (g e) -> p g d e", e=8),
-                v_pairs[half][:].bitcast(U16).rearrange("p (g e d) -> p g d e", e=8, d=2),
-            )
+        def gather_table_words():
+            for half in range(2):
+                nc.vector.tensor_copy(v_pairs[half][:], tab_w[:].bitcast(U32).indirect(places(half)))
+            for half in range(2):
+                nc.vector.tensor_copy(
+                    v_w[half][:].rearrange("p d (g e) -> p g d e", e=8),
+                    v_pairs[half][:].bitcast(U16).rearrange("p (g e d) -> p g d e", e=8, d=2),
+                )
 
-        wu_s = {}
+        wu_s, wu_w, wg_w, wg_s, gw, h, h_w, h_s, sums, act, staged, ys, zs, banks = [{} for name in range(14)]
 
-        def deal_wu_scales(b, after):
-            wu_s[b] = held([P, 2 * PASS], U8, f"wu_s{b}", after)
+        def deal_wu_scales(b, where=None):
+            wu_s[b] = place([P, 2 * PASS], U8, f"wu_s{b}", where)
             nc.vector.tensor_copy(
                 wu_s[b][:].rearrange("p (a t g e) -> p a g t e", a=2, t=PACK, e=16),
                 wu_s_raw[:].rearrange("p (a b g e t) -> p b a g t e", a=2, b=2, t=PACK, e=16)[:, b],
             )
 
-        gw = {}
-
-        def gather_gate(n, after):
-            whole = held([P, J], F32, f"gw{n}", after)
-            nc.vector.tensor_tensor(whole[:], gates[n][:].indirect(offsets[:]), wgo_all, MULT)
-            gw[n] = whole[:]
-            for half in range(2):
-                gw[n, half] = whole[:, HALF * half : HALF * (half + 1)]
-
-        def gather_gate_half(n, half, after):
-            part = held([P, HALF], F32, f"gw{n}{half}", after)
-            nc.vector.tensor_tensor(part[:], gates[n][:].indirect(offsets[:, HALF // 16 * half : HALF // 16 * (half + 1)]), wgo_all[:, HALF * half : HALF * (half + 1)], MULT)
-            gw[n, half] = part[:]
-
-        wg_w, wg_s = {}, {}
-
-        woven = {}
-
-        def weave_wg(a, b, u, copy, ms=slice(0, P)):
-            if (a, b) not in woven:
-                woven[a, b] = keep.tile([P, PACK, P, PACK], BF16, name=f"woven{a}{b}", tag=f"woven{a}{b}", align_bytes=64)
-            ts = slice(2 * u, 2 * u + 2)
+        def deal_wu(b, copy, where=None):
+            wu_w[b] = place([P, 2 * PASS], U32, f"wu_w{b}", where)
             copy(
-                woven[a, b][:, ts, ms, :].rearrange("p t m i -> p m i t"),
-                wg_raw[a, b][:].rearrange("p i (m t) -> p m i t", t=PACK)[:, ms, :, ts],
+                wu_w[b][:].rearrange("p (a u e m) -> p a u m e", a=2, u=2, e=2),
+                wu_raw[b][:].bitcast(U32).rearrange("p a (m u e) -> p a u m e", u=2, e=2),
             )
 
-        def quantize_wg(a, b, after):
-            wg_w[a, b] = keep.tile([P, PASS], U32, name=f"wg_w{a}{b}", align_bytes=64)
-            wg_s[a, b] = held([P, PASS], U8, f"wg_s{a}{b}", after)
+        def weave_wg(a, b, split):
+            for copy, ms in ((nc.scalar.copy, slice(0, split)), (nc.vector.tensor_copy, slice(split, P))):
+                if ms.start < ms.stop:
+                    copy(
+                        woven[a, b][:, :, ms, :].rearrange("p t m i -> p m i t"),
+                        wg_raw[a, b][:].rearrange("p i (m t) -> p m i t", t=PACK)[:, ms],
+                    )
+
+        def quantize_wg(a, b, where=None):
+            wg_w[a, b] = place([P, PASS], U32, f"wg_w{a}{b}")
+            wg_s[a, b] = place([P, PASS], U8, f"wg_s{a}{b}", where)
             nc.vector.quantize_mx(out=wg_w[a, b][:].bitcast(FP8X4), scales=wg_s[a, b][:], in_=woven[a, b][:].rearrange("p t m i -> p (t m i)"))
 
-        wu_w = {}
+        def gather_gate(n, half=None, where=None):
+            if half is None:
+                whole = place([P, J], F32, f"gw{n}", where)
+                nc.vector.tensor_tensor(whole[:], gates[n][:].indirect(offsets[:]), wgo_all, MULT)
+                gw[n, 0], gw[n, 1], gw[n] = whole[:, :HALF], whole[:, HALF:], whole[:]
+            else:
+                part = place([P, HALF], F32, f"gw{n}{half}", where)
+                nc.vector.tensor_tensor(part[:], gates[n][:].indirect(places(half)), wgo_all[:, HALF * half : HALF * (half + 1)], MULT)
+                gw[n, half] = part[:]
 
-        def deal_wu(b, after):
-            wu_w[b] = held([P, 2 * PASS], I32, f"wu_w{b}", after)
-            nc.vector.tensor_copy(
-                wu_w[b][:].rearrange("p (a u e m) -> p a u m e", a=2, u=2, e=2),
-                wu_raw[b][:].rearrange("p a (m u e) -> p a u m e", u=2, e=2),
-            )
-
-        h_w = [keep.tile([P, J], U32, name=f"h_w{b}", align_bytes=64) for b in range(2)]
-        h_s = {(0, 0): held([P, HALF], U8, "h_s00", "h_s00"), (0, 1): held([P, HALF], U8, "h_s01", "h_s01")}
-        for half in range(2):
-            h_s[1, half] = keep.tile([P, HALF], U8, name=f"h_s1{half}", align_bytes=64)
-        h_tiles = {}
-        ub, act, staged = {}, {}, {}
-        turns = {"ga": [], "ub": []}
-
-        def new_h(b, first, count, after):
-            h = held([P, CHUNK * count, PACK], BF16, f"h{b}{first}", after)
-            for c in range(count):
-                h_tiles[b, first + c] = (h, c)
-
-        def first_product(name, spare, words, scales, chunk):
+        def first_product(name, b, chunk, number, passes=None):
+            words = [wu_w[b][:, PASS * a : PASS * (a + 1)] if name == "ub" else wg_w[a, b][:] for a in range(2) if name == "ub" or (a, b) in wg_w]
+            scales = [wu_s[b][:, PASS * a : PASS * (a + 1)] if name == "ub" else wg_s[a, b][:] for a in range(2) if name == "ub" or (a, b) in wg_w]
             tok = slice(CHUNK * chunk, CHUNK * (chunk + 1))
             table = v_w[tok.start // HALF][:, :, tok.start % HALF : tok.start % HALF + CHUNK]
-            if not spare:
-                turns[name].append(chunk)
-            bank = psum.tile([P, PACK, CHUNK], F32, name=f"{name}{len(ub)}_{len(act)}", tag=spare if spare else f"{name}{len(turns[name]) % 3}")
+            if passes != 1:
+                banks[name, b, chunk] = bank(number, [P, PACK, CHUNK], f"{name}{b}{chunk}")
+            acc = banks[name, b, chunk]
             for t in range(PACK):
                 cols = slice(P * t, P * (t + 1))
-                for a in range(2):
-                    nc.tensor.matmul_mx(out=bank[:, t, :], lhsT=words[a][:, cols].bitcast(FP8X4), lhsT_scale=scales[a][:, cols],
-                                        rhs=table[:, a, :].bitcast(FP4X4), rhs_scale=v_s[a][:, tok], start=(a == 0), stop=(a == 1))
-            return bank[:].rearrange("p t (j e) -> p j t e", e=2)
+                for a in range(2) if passes is None else [passes]:
+                    first, last = (a == 0, a == 1) if passes is None else (a == 0 and t == 0, a == 1 and t == PACK - 1)
+                    nc.tensor.matmul_mx(out=acc[:, t, :], lhsT=words[a][:, cols].bitcast(FP8X4), lhsT_scale=scales[a][:, cols],
+                                        rhs=table[:, a, :].bitcast(FP4X4), rhs_scale=v_s[:, a, tok], start=first, stop=last)
+            sums[name, b, chunk] = acc[:].rearrange("p t (j e) -> p j t e", e=2)
 
-        def up(b, chunk, stage=None, spare=False):
-            words = [wu_w[b][:, PASS * a : PASS * (a + 1)] for a in range(2)]
-            scales = [wu_s[b][:, PASS * a : PASS * (a + 1)] for a in range(2)]
-            ub[b, chunk] = first_product("ub", spare, words, scales, chunk)
-            if stage is not None:
-                staged[b, chunk] = held([P, CHUNK, PACK], F32, f"ub_sb{b}{chunk}", stage)
-                nc.scalar.copy(staged[b, chunk][:].rearrange("p (j e) t -> p j t e", e=2), ub[b, chunk])
-
-        def gate(b, chunk, after=None, woven_order=False, spare=False):
-            ga = first_product("ga", spare, [wg_w[a, b][:] for a in range(2)], [wg_s[a, b][:] for a in range(2)], chunk)
-            name = f"act{b}{chunk}"
-            if woven_order:
-                act[b, chunk] = held([P, CHUNK, PACK], F32, name, after or name)
-                nc.scalar.activation(act[b, chunk][:].rearrange("p (j e) t -> p j t e", e=2), ga, SILU)
+        def silu(b, chunk, where=None, for_gpsimd=False):
+            if for_gpsimd:
+                act[b, chunk] = place([P, CHUNK, PACK], F32, f"act{b}{chunk}", where)
+                nc.scalar.activation(act[b, chunk][:].rearrange("p (j e) t -> p j t e", e=2), sums["ga", b, chunk], SILU)
             else:
-                act[b, chunk] = held([P, CHUNK // 2, PACK, 2], F32, name, after or name)
-                nc.scalar.activation(act[b, chunk][:], ga, SILU)
+                act[b, chunk] = place([P, CHUNK // 2, PACK, 2], F32, f"act{b}{chunk}", where)
+                nc.scalar.activation(act[b, chunk][:], sums["ga", b, chunk], SILU)
+
+        def stage(b, chunk, where=None):
+            staged[b, chunk] = place([P, CHUNK, PACK], F32, f"ub_sb{b}{chunk}", where)
+            nc.scalar.copy(staged[b, chunk][:].rearrange("p (j e) t -> p j t e", e=2), sums["ub", b, chunk])
+
+        def multiply_pair(b, first, numbers, act_where, ub_where):
+            act_pair = place([P, 2, CHUNK, PACK], F32, f"act_pair{first}", act_where)
+            ub_pair = place([P, 2, CHUNK, PACK], F32, f"ub_pair{first}", ub_where)
+            for c in range(2):
+                first_product("ga", b, first + c, numbers[2 * c])
+                first_product("ub", b, first + c, numbers[2 * c + 1])
+                nc.scalar.activation(act_pair[:, c].rearrange("p (j e) t -> p j t e", e=2), sums["ga", b, first + c], SILU)
+                nc.scalar.copy(ub_pair[:, c].rearrange("p (j e) t -> p j t e", e=2), sums["ub", b, first + c])
+            rows, c = h[b, first]
+            nc.gpsimd.tensor_tensor(rows[:, CHUNK * c : CHUNK * (c + 2), :], ub_pair[:].rearrange("p c j t -> p (c j) t"), act_pair[:].rearrange("p c j t -> p (c j) t"), MULT)
+
+        def new_h(b, first, count, where=None):
+            rows = place([P, CHUNK * count, PACK], BF16, f"h{b}{first}", where)
+            for c in range(count):
+                h[b, first + c] = (rows, c)
 
         def multiply(b, chunk):
-            h, c = h_tiles[b, chunk]
-            rows = h[:, CHUNK * c : CHUNK * (c + 1), :]
+            rows, c = h[b, chunk]
+            rows = rows[:, CHUNK * c : CHUNK * (c + 1), :]
             if (b, chunk) in staged:
                 nc.gpsimd.tensor_tensor(rows, staged[b, chunk][:], act[b, chunk][:], MULT)
             else:
-                nc.vector.tensor_tensor(rows.rearrange("p (j e) t -> p j t e", e=2), ub[b, chunk], act[b, chunk][:], MULT)
+                nc.vector.tensor_tensor(rows.rearrange("p (j e) t -> p j t e", e=2), sums["ub", b, chunk], act[b, chunk][:], MULT)
 
-        def both(b, chunk, after=None, stage=None):
-            gate(b, chunk, after, stage is not None)
-            up(b, chunk, stage)
+        def quantize_h(b, first, count, where=None):
+            rows, c = h[b, first]
+            half, start = divmod(CHUNK * first, HALF)
+            if (b, half) not in h_w:
+                h_w[b, half] = place([P, HALF], U32, f"h_w{b}{half}", where)
+                h_s[b, half] = place([P, HALF], U8, f"h_s{b}{half}")
+            tok = slice(start, start + CHUNK * count)
+            nc.vector.quantize_mx(out=h_w[b, half][:, tok].bitcast(FP8X4), scales=h_s[b, half][:, tok], in_=rows[:, CHUNK * c : CHUNK * (c + count), :].rearrange("p j t -> p (j t)"))
 
-        def quantize_h(b, first, count):
-            h, c = h_tiles[b, first]
-            tok = slice(CHUNK * first, CHUNK * (first + count))
-            nc.vector.quantize_mx(out=h_w[b][:, tok].bitcast(FP8X4), scales=h_s[b, tok.start // HALF][:, tok.start % HALF : tok.start % HALF + CHUNK * count], in_=h[:, CHUNK * c : CHUNK * (c + count), :].rearrange("p j t -> p (j t)"))
-
-        def down(half, n):
-            y = psum.tile([P, HALF], F32, name=f"y{half}{n}_psum", tag=f"y{n % 2 if half else int(n % 3 == 0)}")
+        def down(half, n, number, first=0):
+            y = bank(number, [P, HALF], f"y{half}{n}_psum")
             cols = slice(P * n, P * (n + 1))
-            tok = slice(HALF * half, HALF * (half + 1))
-            nc.tensor.matmul_mx(out=y[:], lhsT=wd8_w[:, cols].bitcast(FP8X4), lhsT_scale=wd_s[4:P, cols],
-                                rhs=h_w[0][:, tok].bitcast(FP8X4), rhs_scale=h_s[0, half][:], start=True, stop=False)
-            nc.tensor.matmul_mx(out=y[:], lhsT=wd4_w[:, 2 * P * n : 2 * P * (n + 1)].bitcast(FP4X4), lhsT_scale=wd_s[:, cols],
-                                rhs=h_w[1][:, tok].bitcast(FP8X4), rhs_scale=h_s[1, half][:], start=False, stop=True)
-            return y
+            weights = [(wd8_w[:, cols].bitcast(FP8X4), wd_s[4:P, cols]), (wd4_w[:, 2 * P * n : 2 * P * (n + 1)].bitcast(FP4X4), wd_s[:, cols])]
+            for b in (first, 1 - first):
+                nc.tensor.matmul_mx(out=y[:], lhsT=weights[b][0], lhsT_scale=weights[b][1],
+                                    rhs=h_w[b, half][:].bitcast(FP8X4), rhs_scale=h_s[b, half][:], start=(b == first), stop=(b != first))
+            ys[half, n] = y
 
-        def place_half(half, n, after):
-            y_sb = held([P, HALF], F32, f"y{half}{n}", after)
-            nc.scalar.copy(y_sb[:], down(half, n)[:])
-            places = offsets[:, HALF // 16 * half : HALF // 16 * (half + 1)]
-            nc.vector.tensor_tensor(pages[n % 3][:].indirect(places), y_sb[:], gw[n, half], MULT)
+        def empty_y(half, n, where=None):
+            y_sb = place([P, HALF], F32, f"y{half}{n}", where)
+            nc.scalar.copy(y_sb[:], ys[half, n][:])
+            ys[half, n] = y_sb
 
-        def product(n, on_gpsimd, after):
-            z = held([P, HALF], F32, f"z{n}", after)
-            if on_gpsimd:
-                y_sb = keep.tile([P, HALF], F32, name=f"y0{n}", align_bytes=64)
-                nc.scalar.copy(y_sb[:], down(0, n)[:])
-                nc.gpsimd.tensor_tensor(z[:], y_sb[:], gw[n, 0], MULT)
-            else:
-                nc.vector.tensor_tensor(z[:], gw[n, 0], down(0, n)[:], MULT)
-            return z
+        def gate_y(n, engine, where=None):
+            zs[n] = place([P, HALF], F32, f"z{n}", where)
+            engine.tensor_tensor(zs[n][:], gw[n, 0], ys[0, n][:], MULT)
 
-        def place_product(n, z):
-            nc.vector.tensor_copy(pages[n][:].indirect(offsets[:, 0 : HALF // 16]), z[:])
+        def scatter_z(n):
+            nc.vector.tensor_copy(pages[n % 3][:].indirect(places(0)), zs[n][:])
 
-        def place_all(n):
-            y_sb = keep.tile([P, J], F32, name=f"y{n}", align_bytes=64)
-            for half in range(2):
-                nc.scalar.copy(y_sb[:, HALF * half : HALF * (half + 1)], down(half, n)[:])
-            nc.vector.tensor_tensor(pages[n % 3][:].indirect(offsets[:]), y_sb[:], gw[n], MULT)
+        def scatter_y(half, n):
+            nc.vector.tensor_tensor(pages[n % 3][:].indirect(places(half)), ys[half, n][:], gw[n, half], MULT)
+
+        y_last = place([P, J], F32, "y_last")
+
+        def down_last(half, number):
+            down(half, 3, number, half)
+            nc.scalar.copy(y_last[:, HALF * half : HALF * (half + 1)], ys[half, 3][:])
+
+        def scatter_last():
+            nc.vector.tensor_tensor(pages[0][:].indirect(offsets[:]), y_last[:], gw[3], MULT)
 
         def store(n):
             nc.sync.dma_start(out[P * n : P * (n + 1), :], pages[n % 3][:])
 
-        spread_wgo()
-        deal_wu_scales(0, "wu_s0")
-        weave_wg(0, 0, 0, nc.scalar.copy)
-        weave_wg(0, 0, 1, nc.scalar.copy)
-        deal_wu(0, "wu_w0")
-        deal_wu_scales(1, (8, 0))
-        quantize_wg(0, 0, (8, 1024))
-        weave_wg(1, 0, 0, nc.scalar.copy, slice(0, 80))
-        weave_wg(1, 0, 1, nc.vector.tensor_copy)
-        weave_wg(1, 0, 0, nc.vector.tensor_copy, slice(80, P))
-        quantize_wg(1, 0, "wg_s10")
-        gather_gate(0, "woven00")
-        new_h(0, 0, 4, "h00")
+        spread_wgo((4, 5))
+        gather_table_words()
+        deal_wu_scales(0)
+        weave_wg(0, 0, P)
+        deal_wu(0, nc.vector.tensor_copy)
+        deal_wu_scales(1, ("wu0", 1))
+        quantize_wg(0, 0, ("wu0", 0))
         for chunk in range(4):
-            gate(0, chunk)
-            up(0, chunk, None, "y0" if chunk == 3 else None)
+            first_product("ub", 0, chunk, chunk)
+        weave_wg(1, 0, 40)
+        quantize_wg(1, 0)
+        gather_gate(0)
+        new_h(0, 0, 4)
+        for chunk in range(4):
+            first_product("ga", 0, chunk, 4 + chunk)
+            silu(0, chunk, ("wg00", 2 * chunk))
             multiply(0, chunk)
-        weave_wg(0, 1, 0, nc.scalar.copy)
-        weave_wg(0, 1, 1, nc.scalar.copy)
-        gather_gate(1, "gw1")
         quantize_h(0, 0, 2)
         quantize_h(0, 2, 2)
-        quantize_wg(0, 1, (1, 2048))
-        new_h(0, 4, 4, (0, 4096))
+        weave_wg(0, 1, P)
+        gather_gate(1)
+        quantize_wg(0, 1, ("gate1", 7))
+        new_h(0, 4, 4)
         for chunk in (4, 5):
-            both(0, chunk, (6, 2048 * (chunk - 3)))
+            first_product("ga", 0, chunk, 2 * chunk - 4)
+            first_product("ub", 0, chunk, 2 * chunk - 3)
+            silu(0, chunk, ("wg01", 2 * (chunk - 4)))
             multiply(0, chunk)
-        weave_wg(1, 1, 0, nc.scalar.copy)
-        weave_wg(1, 1, 1, nc.scalar.copy, slice(0, 80))
-        weave_wg(1, 1, 1, nc.vector.tensor_copy, slice(80, P))
-        deal_wu(1, "wu_w1")
-        quantize_wg(1, 1, "wg_s11")
-        turns["ga"].append(None)
-        turns["ub"].append(None)
         for chunk in (6, 7):
-            both(0, chunk, (7, 2048 * (chunk - 6)))
+            first_product("ga", 0, chunk, 2 * chunk - 12)
+            first_product("ub", 0, chunk, 2 * chunk - 11)
+        weave_wg(1, 1, 104)
+        deal_wu(1, nc.vector.tensor_copy)
+        for chunk in range(2):
+            first_product("ga", 1, chunk, (4, 6)[chunk], 0)
+        quantize_wg(1, 1)
+        for chunk in (6, 7):
+            silu(0, chunk, ("wg11", 2 * (chunk - 6)))
             multiply(0, chunk)
+        gather_gate(2, 0)
         quantize_h(0, 4, 4)
-        gather_gate_half(2, 0, (7, 0))
-        new_h(1, 0, 4, "h10")
+        new_h(1, 0, 4)
         for chunk in range(4):
-            gate(1, chunk)
-            up(1, chunk, None, f"y{chunk}" if chunk < 2 else None)
+            first_product("ub", 1, chunk, (5, 7, 1, 3)[chunk])
+            first_product("ga", 1, chunk, (4, 6, 0, 2)[chunk], 1 if chunk < 2 else None)
+            silu(1, chunk, ("wg10", 2 * chunk))
             multiply(1, chunk)
         quantize_h(1, 0, 2)
         quantize_h(1, 2, 2)
-        gather_gate_half(2, 1, "act13")
-        z0 = product(0, False, (5, 2048))
-        z1 = product(1, True, (2, 2048))
-        z2 = product(2, True, (5, 0))
-        new_h(1, 4, 4, (2, 4096))
-        for chunk in range(4, 8):
-            both(1, chunk, None, f"ub_sb1{chunk}")
-            multiply(1, chunk)
-        place_product(0, z0)
-        place_product(1, z1)
-        place_product(2, z2)
-        quantize_h(1, 4, 4)
-        gather_gate(3, "ub_sb17")
+        gather_gate(2, 1, ("wg10", 6))
+
         for n in range(3):
-            place_half(1, n, f"y1{n}")
+            down(0, n, (5, 7, 2)[n] if False else (5, 7, 1)[n])
+        gate_y(0, nc.vector)
+        for n in range(1, 3):
+            empty_y(0, n, ("table", 2 * n))
+        gate_y(1, nc.gpsimd)
+        gate_y(2, nc.gpsimd)
+        new_h(1, 4, 4)
+        for chunk in range(4, 8):
+            x, y, z = (5, 7, 1)
+            first_product("ga", 1, chunk, (x, z, y, x)[chunk - 4])
+            first_product("ub", 1, chunk, (y, x, z, y)[chunk - 4])
+            silu(1, chunk, ("gate0", 2 * (chunk - 4)), True)
+            stage(1, chunk, ("woven0", 2 * (chunk - 4)))
+            multiply(1, chunk)
+
+            if chunk == 5:
+                down_last(0, 3)
+        for n in range(3):
+            scatter_z(n)
+
+        quantize_h(1, 4, 4)
+        gather_gate(3, None, ("woven0", 4))
+        for n in range(3):
+            down(1, n, (4, 6, 0)[n], min(n, 1))
+            empty_y(1, n, ("wg01", 2 * n))
+            scatter_y(1, n)
             store(n)
-        place_all(3)
+        down_last(1, 2)
+        scatter_last()
         store(3)

@@ -54,7 +54,7 @@ def tile_list_modp_gsilu_mix_gate_kernel(tc, tab_words, tab_scales, wg, wu_words
         tab_w = place([P, T], I32, "tab_w", ("table", 0))
         wu_s_raw = place([P, 2 * R], U8, "wu_s_raw")
         v_s_raw = place([P, J], U8, "v_s_raw")
-        v_s = place([P, 2, J], U8, "v_s")
+        v_s = place([P, 2, 2, HALF], U8, "v_s")
         wd_s = place([P, N], U8, "wd_s")
         ident = place([P, P], F32, "ident")
         pages = [place([P, T], F32, f"page{n}") for n in range(3)]
@@ -109,9 +109,9 @@ def tile_list_modp_gsilu_mix_gate_kernel(tc, tab_words, tab_scales, wg, wu_words
         def gather_table_scales():
             nc.vector.tensor_copy(v_s_raw[:], tab_s[:].indirect(offsets[:]))
 
-        def move_table_scales():
+        def move_table_scales(half):
             for q in range(4):
-                nc.sync.dma_start(v_s[32 * q : 32 * q + 4].rearrange("r a c -> r (a c)").bitcast(I32), v_s_raw[96 + 8 * q : 96 + 8 * q + 8, :].bitcast(I32))
+                nc.sync.dma_start(v_s[32 * q : 32 * q + 4, half].rearrange("r a c -> r (a c)").bitcast(I32), v_s_raw[96 + 8 * q : 96 + 8 * q + 8, HALF * half : HALF * (half + 1)].bitcast(I32))
 
         load_table_scales()
         load_table_words()
@@ -119,13 +119,14 @@ def tile_list_modp_gsilu_mix_gate_kernel(tc, tab_words, tab_scales, wg, wu_words
         load_wgo()
         load_wg(0, 0)
         gather_table_scales()
-        move_table_scales()
+        move_table_scales(0)
         load_wu(0)
         load_wg(1, 0)
         load_gate(0)
-        load_wd_scales(4, wd8_scales)
+        move_table_scales(1)
         load_wg(0, 1)
         load_gate(1)
+        load_wd_scales(4, wd8_scales)
         load_wg(1, 1)
         load_wu(1)
         load_gate(2)
@@ -207,7 +208,7 @@ def tile_list_modp_gsilu_mix_gate_kernel(tc, tab_words, tab_scales, wg, wu_words
                 for a in range(2) if passes is None else [passes]:
                     first, last = (a == 0, a == 1) if passes is None else (a == 0 and t == 0, a == 1 and t == PACK - 1)
                     nc.tensor.matmul_mx(out=acc[:, t, :], lhsT=words[a][:, cols].bitcast(FP8X4), lhsT_scale=scales[a][:, cols],
-                                        rhs=table[:, a, :].bitcast(FP4X4), rhs_scale=v_s[:, a, tok], start=first, stop=last)
+                                        rhs=table[:, a, :].bitcast(FP4X4), rhs_scale=v_s[:, tok.start // HALF, a, tok.start % HALF : tok.start % HALF + CHUNK], start=first, stop=last)
             sums[name, b, chunk] = acc[:].rearrange("p t (j e) -> p j t e", e=2)
 
         def silu(b, chunk, where=None, for_gpsimd=False):

@@ -127,8 +127,8 @@ def tile_list_modp_gsilu_mix_gate_kernel(tc, tab_words, tab_scales, wg, wu_words
         load_wg(0, 1)
         load_gate(1)
         load_wd_scales(4, wd8_scales)
-        load_wg(1, 1)
         load_wu(1)
+        load_wg(1, 1)
         load_gate(2)
         load_wd()
         load_wd_scales(0, wd4_scales)
@@ -313,6 +313,7 @@ def tile_list_modp_gsilu_mix_gate_kernel(tc, tab_words, tab_scales, wg, wu_words
         quantize_h(0, 2, 2)
         weave_wg(0, 1, P)
         gather_gate(1)
+        deal_wu(1, nc.vector.tensor_copy)
         quantize_wg(0, 1, ("gate1", 7))
         new_h(0, 4, 4)
         for chunk in (4, 5):
@@ -324,9 +325,9 @@ def tile_list_modp_gsilu_mix_gate_kernel(tc, tab_words, tab_scales, wg, wu_words
             first_product("ga", 0, chunk, 2 * chunk - 12)
             first_product("ub", 0, chunk, 2 * chunk - 11)
         weave_wg(1, 1, 104)
-        deal_wu(1, nc.vector.tensor_copy)
         for chunk in range(2):
             first_product("ga", 1, chunk, (4, 6)[chunk], 0)
+            first_product("ub", 1, chunk, (5, 7)[chunk])
         quantize_wg(1, 1)
         for chunk in (6, 7):
             silu(0, chunk, ("wg11", 2 * (chunk - 6)))
@@ -335,8 +336,9 @@ def tile_list_modp_gsilu_mix_gate_kernel(tc, tab_words, tab_scales, wg, wu_words
         quantize_h(0, 4, 4)
         new_h(1, 0, 4)
         for chunk in range(4):
-            first_product("ub", 1, chunk, (5, 7, 1, 3)[chunk])
             first_product("ga", 1, chunk, (4, 6, 0, 2)[chunk], 1 if chunk < 2 else None)
+            if chunk >= 2:
+                first_product("ub", 1, chunk, (1, 3)[chunk - 2])
             silu(1, chunk, ("wg10", 2 * chunk))
             multiply(1, chunk)
         quantize_h(1, 0, 2)

@@ -16,12 +16,14 @@ FP8X4 = mybir.dt.float8_e4m3fn_x4
 FP4X4 = mybir.dt.float4_e2m1fn_x4
 MULT = mybir.AluOpType.mult
 SILU = mybir.ActivationFunctionType.Silu
+COPY = mybir.ActivationFunctionType.Copy
 
 P = 128
 PACK = 4
 PASS = P * PACK
 HALF = J // 2
-CHUNK = 128
+QUARTER = J // 4
+GROUP = 128
 KIB = 1024
 
 
@@ -32,8 +34,8 @@ def tile_list_modp_gsilu_mix_gate_kernel(tc, tab_words, tab_scales, wg, wu_words
         share = ctx.enter_context(tc.tile_pool(name="share", bufs=1))
         psum = ctx.enter_context(tc.psum_pool(name="psum", bufs=1))
 
-        region = {"gate0": 0, "gate1": 8, "gate2": 16, "gate3": 24, "wg00": 32, "wg10": 40, "wg01": 48, "wg11": 56,
-                  "wu0": 104, "wu1": 68, "woven0": 72, "woven1": 80, "table": 88, "wgo": 96, "gw0": 102}
+        region = {"gates": 0, "wg00": 32, "wg10": 40, "wg01": 48, "wg11": 56, "wu0": 114, "wu1": 64,
+                  "woven0": 72, "woven1": 80, "table": 88, "turned": 96, "yw": 104, "spare": 114}
 
         def place(shape, dtype, name, where=None):
             if where is None:
@@ -46,8 +48,8 @@ def tile_list_modp_gsilu_mix_gate_kernel(tc, tab_words, tab_scales, wg, wu_words
         offsets = keep.tile([P, J // 16], U16, name="offsets")
         nc.sync.dma_start(offsets[:], offs)
 
-        def places(half):
-            return offsets[:, HALF // 16 * half : HALF // 16 * (half + 1)]
+        def places(first, count):
+            return offsets[:, first // 16 : (first + count) // 16]
 
         w_col = place([P, J // P], F32, "w_col")
         tab_s = place([P, T], U8, "tab_s")
@@ -58,7 +60,7 @@ def tile_list_modp_gsilu_mix_gate_kernel(tc, tab_words, tab_scales, wg, wu_words
         wd_s = place([P, N], U8, "wd_s")
         ident = place([P, P], F32, "ident")
         pages = [place([P, T], F32, f"page{n}") for n in range(3)]
-        gates = [place([P, T], F32, f"gate{n}", (f"gate{n}", 0)) for n in range(4)]
+        gates = [place([P, T], F32, f"gate{n}", ("gates", 8 * n)) for n in range(4)]
         wu_raw = [place([P, 2, PASS], I32, f"wu_raw{b}", (f"wu{b}", 0)) for b in range(2)]
         wg_raw = {(a, b): place([P, PACK, PASS], F32, f"wg_raw{a}{b}", (f"wg{a}{b}", 0)) for a in range(2) for b in range(2)}
         woven = {(a, b): place([P, PACK, P, PACK], BF16, f"woven{a}{b}", (f"woven{b}", 4 * a)) for a in range(2) for b in range(2)}
@@ -67,12 +69,12 @@ def tile_list_modp_gsilu_mix_gate_kernel(tc, tab_words, tab_scales, wg, wu_words
 
         nc.gpsimd.memset(wu_s_raw[:].bitcast(I32), 0)
         nc.gpsimd.memset(tab_s[0:96, :].bitcast(I32), 0)
-        nc.vector.memset(pages[2][:, 0 : T // 2 - 1], 0.0)
-        nc.vector.memset(pages[2][:, T // 2 - 1 : T], 0.0)
+        nc.vector.memset(pages[0][:, 0 : T // 2 - 1], 0.0)
+        nc.vector.memset(pages[0][:, T // 2 - 1 : T], 0.0)
         make_identity(nc, ident[:])
         nc.gpsimd.memset(v_s[:].bitcast(I32), 0)
         nc.gpsimd.memset(wd_s[:].bitcast(I32), 0)
-        for page in pages[:2]:
+        for page in pages[1:]:
             nc.gpsimd.memset(page[:], 0.0)
 
         def load_table_scales():
@@ -123,40 +125,45 @@ def tile_list_modp_gsilu_mix_gate_kernel(tc, tab_words, tab_scales, wg, wu_words
         load_wu(0)
         load_wg(1, 0)
         load_gate(0)
-        move_table_scales(1)
-        load_wg(0, 1)
-        load_gate(1)
-        load_wd_scales(4, wd8_scales)
         load_wu(1)
+        load_wg(0, 1)
+        move_table_scales(1)
         load_wg(1, 1)
-        load_gate(2)
+        load_wd_scales(4, wd8_scales)
         load_wd()
+        load_gate(1)
         load_wd_scales(0, wd4_scales)
+        load_gate(2)
         load_gate(3)
 
         wgo_sb = place([P, P, J // P], F32, "wgo_sb")
         wgo_all = wgo_sb[:].rearrange("q p c -> q (p c)")
+        w_tok = place([P, HALF // GROUP], F32, "w_tok")
 
-        def spread_wgo(banks):
+        def spread_wgo():
             for g in range(2):
-                spread = bank(banks[g], [P, PACK, P], f"spread{g}")
+                spread = bank(4 + g, [P, PACK, P], f"spread{g}")
                 for c in range(PACK):
                     nc.tensor.transpose(spread[:, c, :], w_col[:, PACK * g + c : PACK * g + c + 1].to_broadcast([P, P]), ident[:])
                 nc.scalar.copy(wgo_sb[:, :, PACK * g : PACK * (g + 1)], spread[:].rearrange("q c p -> q p c"))
+            upright = bank(6, [P, PACK, P], "upright")
+            for c in range(PACK):
+                nc.tensor.transpose(upright[:, c, :], wgo_all[:, GROUP * c : GROUP * (c + 1)], ident[:])
+            nc.scalar.copy(w_tok[:], upright[:, :, 0])
 
         v_pairs = [place([P, HALF], U32, f"v_pairs{half}") for half in range(2)]
         v_w = [place([P, 2, HALF], U16, f"v_w{half}") for half in range(2)]
 
         def gather_table_words():
             for half in range(2):
-                nc.vector.tensor_copy(v_pairs[half][:], tab_w[:].bitcast(U32).indirect(places(half)))
+                nc.vector.tensor_copy(v_pairs[half][:], tab_w[:].bitcast(U32).indirect(places(HALF * half, HALF)))
             for half in range(2):
                 nc.vector.tensor_copy(
                     v_w[half][:].rearrange("p d (g e) -> p g d e", e=8),
                     v_pairs[half][:].bitcast(U16).rearrange("p (g e d) -> p g d e", e=8, d=2),
                 )
 
-        wu_s, wu_w, wg_w, wg_s, gw, h, h_w, h_s, sums, act, staged, ys, zs, banks = [{} for name in range(14)]
+        wu_s, wu_w, wg_w, wg_s, gw, h, h_w, h_s, sums, act, staged, banks, turned, y_bank, yw, z = [{} for name in range(16)]
 
         def deal_wu_scales(b, where=None):
             wu_s[b] = place([P, 2 * PASS], U8, f"wu_s{b}", where)
@@ -185,194 +192,222 @@ def tile_list_modp_gsilu_mix_gate_kernel(tc, tab_words, tab_scales, wg, wu_words
             wg_s[a, b] = place([P, PASS], U8, f"wg_s{a}{b}", where)
             nc.vector.quantize_mx(out=wg_w[a, b][:].bitcast(FP8X4), scales=wg_s[a, b][:], in_=woven[a, b][:].rearrange("p t m i -> p (t m i)"))
 
-        def gather_gate(n, half=None, where=None):
-            if half is None:
-                whole = place([P, J], F32, f"gw{n}", where)
-                nc.vector.tensor_tensor(whole[:], gates[n][:].indirect(offsets[:]), wgo_all, MULT)
-                gw[n, 0], gw[n, 1], gw[n] = whole[:, :HALF], whole[:, HALF:], whole[:]
-            else:
-                part = place([P, HALF], F32, f"gw{n}{half}", where)
-                nc.vector.tensor_tensor(part[:], gates[n][:].indirect(places(half)), wgo_all[:, HALF * half : HALF * (half + 1)], MULT)
-                gw[n, half] = part[:]
+        def gate_times_wgo(n, first, count, where=None):
+            gw[n] = place([P, count], F32, f"gw{n}", where)[:]
+            nc.vector.tensor_tensor(gw[n], gates[n][:].indirect(places(first, count)), wgo_all[:, first : first + count], MULT)
 
-        def first_product(name, b, chunk, number, passes=None):
-            words = [wu_w[b][:, PASS * a : PASS * (a + 1)] if name == "ub" else wg_w[a, b][:] for a in range(2) if name == "ub" or (a, b) in wg_w]
-            scales = [wu_s[b][:, PASS * a : PASS * (a + 1)] if name == "ub" else wg_s[a, b][:] for a in range(2) if name == "ub" or (a, b) in wg_w]
-            tok = slice(CHUNK * chunk, CHUNK * (chunk + 1))
-            table = v_w[tok.start // HALF][:, :, tok.start % HALF : tok.start % HALF + CHUNK]
+        def first_product(name, b, group, number, passes=None):
+            tok = slice(GROUP * group % HALF, GROUP * group % HALF + GROUP)
+            half = GROUP * group // HALF
             if passes != 1:
-                banks[name, b, chunk] = bank(number, [P, PACK, CHUNK], f"{name}{b}{chunk}")
-            acc = banks[name, b, chunk]
+                banks[name, b, group] = bank(number, [P, PACK, GROUP], f"{name}{b}{group}")
+            acc = banks[name, b, group]
             for t in range(PACK):
-                cols = slice(P * t, P * (t + 1))
                 for a in range(2) if passes is None else [passes]:
                     first, last = (a == 0, a == 1) if passes is None else (a == 0 and t == 0, a == 1 and t == PACK - 1)
-                    nc.tensor.matmul_mx(out=acc[:, t, :], lhsT=words[a][:, cols].bitcast(FP8X4), lhsT_scale=scales[a][:, cols],
-                                        rhs=table[:, a, :].bitcast(FP4X4), rhs_scale=v_s[:, tok.start // HALF, a, tok.start % HALF : tok.start % HALF + CHUNK], start=first, stop=last)
-            sums[name, b, chunk] = acc[:].rearrange("p t (j e) -> p j t e", e=2)
+                    if name == "ub":
+                        cols = slice(PASS * a + P * t, PASS * a + P * (t + 1))
+                        words, scales = wu_w[b][:, cols], wu_s[b][:, cols]
+                    else:
+                        cols = slice(P * t, P * (t + 1))
+                        words, scales = wg_w[a, b][:, cols], wg_s[a, b][:, cols]
+                    nc.tensor.matmul_mx(out=acc[:, t, :], lhsT=words.bitcast(FP8X4), lhsT_scale=scales,
+                                        rhs=v_w[half][:, a, tok].bitcast(FP4X4), rhs_scale=v_s[:, half, a, tok], start=first, stop=last)
+            sums[name, b, group] = acc[:].rearrange("p t (j e) -> p j t e", e=2)
 
-        def silu(b, chunk, where=None, for_gpsimd=False):
-            if for_gpsimd:
-                act[b, chunk] = place([P, CHUNK, PACK], F32, f"act{b}{chunk}", where)
-                nc.scalar.activation(act[b, chunk][:].rearrange("p (j e) t -> p j t e", e=2), sums["ga", b, chunk], SILU)
-            else:
-                act[b, chunk] = place([P, CHUNK // 2, PACK, 2], F32, f"act{b}{chunk}", where)
-                nc.scalar.activation(act[b, chunk][:], sums["ga", b, chunk], SILU)
-
-        def stage(b, chunk, where=None):
-            staged[b, chunk] = place([P, CHUNK, PACK], F32, f"ub_sb{b}{chunk}", where)
-            nc.scalar.copy(staged[b, chunk][:].rearrange("p (j e) t -> p j t e", e=2), sums["ub", b, chunk])
-
-        def multiply_pair(b, first, numbers, act_where, ub_where):
-            act_pair = place([P, 2, CHUNK, PACK], F32, f"act_pair{first}", act_where)
-            ub_pair = place([P, 2, CHUNK, PACK], F32, f"ub_pair{first}", ub_where)
-            for c in range(2):
-                first_product("ga", b, first + c, numbers[2 * c])
-                first_product("ub", b, first + c, numbers[2 * c + 1])
-                nc.scalar.activation(act_pair[:, c].rearrange("p (j e) t -> p j t e", e=2), sums["ga", b, first + c], SILU)
-                nc.scalar.copy(ub_pair[:, c].rearrange("p (j e) t -> p j t e", e=2), sums["ub", b, first + c])
-            rows, c = h[b, first]
-            nc.gpsimd.tensor_tensor(rows[:, CHUNK * c : CHUNK * (c + 2), :], ub_pair[:].rearrange("p c j t -> p (c j) t"), act_pair[:].rearrange("p c j t -> p (c j) t"), MULT)
+        def silu(b, group, where=None):
+            act[b, group] = place([P, GROUP // 2, PACK, 2], F32, f"act{b}{group}", where)
+            nc.scalar.activation(act[b, group][:], sums["ga", b, group], SILU)
 
         def new_h(b, first, count, where=None):
-            rows = place([P, CHUNK * count, PACK], BF16, f"h{b}{first}", where)
+            rows = place([P, GROUP * count, PACK], BF16, f"h{b}{first}", where)
             for c in range(count):
                 h[b, first + c] = (rows, c)
 
-        def multiply(b, chunk):
-            rows, c = h[b, chunk]
-            rows = rows[:, CHUNK * c : CHUNK * (c + 1), :]
-            if (b, chunk) in staged:
-                nc.gpsimd.tensor_tensor(rows, staged[b, chunk][:], act[b, chunk][:], MULT)
-            else:
-                nc.vector.tensor_tensor(rows.rearrange("p (j e) t -> p j t e", e=2), sums["ub", b, chunk], act[b, chunk][:], MULT)
+        def multiply(b, group):
+            rows, c = h[b, group]
+            nc.vector.tensor_tensor(rows[:, GROUP * c : GROUP * (c + 1), :].rearrange("p (j e) t -> p j t e", e=2), sums["ub", b, group], act[b, group][:], MULT)
+
+        def new_stage(b, first, count, where):
+            act_sb = place([P, count, GROUP, PACK], F32, f"act_sb{b}{first}", where)
+            ub_sb = place([P, count, GROUP, PACK], F32, f"ub_sb{b}{first}", (where[0], where[1] + 2 * count))
+            staged[b, first] = (act_sb, ub_sb, count)
+
+        def stage(b, first, group, numbers):
+            act_sb, ub_sb, count = staged[b, first]
+            first_product("ga", b, group, numbers[0])
+            first_product("ub", b, group, numbers[1])
+            nc.scalar.activation(act_sb[:, group - first].rearrange("p (j e) t -> p j t e", e=2), sums["ga", b, group], SILU)
+            nc.scalar.copy(ub_sb[:, group - first].rearrange("p (j e) t -> p j t e", e=2), sums["ub", b, group])
+
+        def multiply_staged(b, first):
+            act_sb, ub_sb, count = staged[b, first]
+            rows, c = h[b, first]
+            nc.gpsimd.tensor_tensor(rows[:, GROUP * c : GROUP * (c + count), :], ub_sb[:].rearrange("p c j t -> p (c j) t"), act_sb[:].rearrange("p c j t -> p (c j) t"), MULT)
 
         def quantize_h(b, first, count, where=None):
             rows, c = h[b, first]
-            half, start = divmod(CHUNK * first, HALF)
+            half, start = divmod(GROUP * first, HALF)
             if (b, half) not in h_w:
                 h_w[b, half] = place([P, HALF], U32, f"h_w{b}{half}", where)
                 h_s[b, half] = place([P, HALF], U8, f"h_s{b}{half}")
-            tok = slice(start, start + CHUNK * count)
-            nc.vector.quantize_mx(out=h_w[b, half][:, tok].bitcast(FP8X4), scales=h_s[b, half][:, tok], in_=rows[:, CHUNK * c : CHUNK * (c + count), :].rearrange("p j t -> p (j t)"))
+            tok = slice(start, start + GROUP * count)
+            nc.vector.quantize_mx(out=h_w[b, half][:, tok].bitcast(FP8X4), scales=h_s[b, half][:, tok], in_=rows[:, GROUP * c : GROUP * (c + count), :].rearrange("p j t -> p (j t)"))
 
-        def down(half, n, number, first=0):
-            y = bank(number, [P, HALF], f"y{half}{n}_psum")
-            cols = slice(P * n, P * (n + 1))
-            weights = [(wd8_w[:, cols].bitcast(FP8X4), wd_s[4:P, cols]), (wd4_w[:, 2 * P * n : 2 * P * (n + 1)].bitcast(FP4X4), wd_s[:, cols])]
-            for b in (first, 1 - first):
-                nc.tensor.matmul_mx(out=y[:], lhsT=weights[b][0], lhsT_scale=weights[b][1],
-                                    rhs=h_w[b, half][:].bitcast(FP8X4), rhs_scale=h_s[b, half][:], start=(b == first), stop=(b != first))
-            ys[half, n] = y
+        def wd(b, cols):
+            if b == 0:
+                return wd8_w[:, cols].bitcast(FP8X4), wd_s[4:P, cols]
+            return wd4_w[:, 2 * cols.start : 2 * cols.stop].bitcast(FP4X4), wd_s[:, cols]
 
-        def empty_y(half, n, where=None):
-            y_sb = place([P, HALF], F32, f"y{half}{n}", where)
-            nc.scalar.copy(y_sb[:], ys[half, n][:])
-            ys[half, n] = y_sb
+        yw_middle = place([P, 2, HALF], F32, "yw_middle", ("yw", 2))
+        yw_last = place([P, HALF], F32, "yw_last", ("yw", 8))
+        yw.update({1: yw_middle[:, 0], 2: yw_middle[:, 1], 3: yw_last[:]})
 
-        def gate_y(n, engine, where=None):
-            zs[n] = place([P, HALF], F32, f"z{n}", where)
-            engine.tensor_tensor(zs[n][:], gw[n, 0], ys[0, n][:], MULT)
+        def down_tokens(b, group, number):
+            if b == 0:
+                y_bank[group] = bank(number, [P, 3 * P], f"y_tok{group}")
+            tok = slice(GROUP * group, GROUP * (group + 1))
+            for cols in (slice(0, 2 * P), slice(2 * P, 3 * P)):
+                words, scales = wd(b, slice(P + cols.start, P + cols.stop))
+                nc.tensor.matmul_mx(out=y_bank[group][:, cols], lhsT=h_w[b, 0][:, tok].bitcast(FP8X4), lhsT_scale=h_s[b, 0][:, tok],
+                                    rhs=words, rhs_scale=scales, start=(b == 0 and cols.start == 0), stop=(b == 1 and cols.stop == 3 * P))
+
+        def weigh(group):
+            turned[group] = place([P, 3 * P], F32, f"turned{group}", ("turned", 2 * group))
+            nc.scalar.activation(turned[group][:], y_bank[group][:], COPY, scale=w_tok[:, group : group + 1])
+
+        def turn_middle(pair, number):
+            back = bank(number, [P, 2, 2 * GROUP], f"back{pair}")
+            for c in range(2):
+                for n in range(2):
+                    nc.tensor.transpose(back[:, n, GROUP * c : GROUP * (c + 1)], turned[2 * pair + c][:, P * n : P * (n + 1)], ident[:])
+            nc.scalar.copy(yw_middle[:, :, 2 * GROUP * pair : 2 * GROUP * (pair + 1)], back[:])
+
+        def turn_last(number):
+            back = bank(number, [P, HALF], "back_last")
+            for group in range(4):
+                nc.tensor.transpose(back[:, GROUP * group : GROUP * (group + 1)], turned[group][:, 2 * P :], ident[:])
+            nc.scalar.copy(yw_last[:], back[:])
+
+        def down_rows(half, n, number, target, tok=slice(0, HALF)):
+            y = bank(number, [P, tok.stop - tok.start], f"y_rows{half}{n}{tok.start}")
+            for b in range(2):
+                words, scales = wd(b, slice(P * n, P * (n + 1)))
+                nc.tensor.matmul_mx(out=y[:], lhsT=words, lhsT_scale=scales, rhs=h_w[b, half][:, tok].bitcast(FP8X4), rhs_scale=h_s[b, half][:, tok], start=(b == 0), stop=(b == 1))
+            nc.scalar.copy(target, y[:])
+
+        def gate_times_yw(n, where=None):
+            z[n] = place([P, HALF], F32, f"z{n}", where)
+            nc.vector.tensor_tensor(z[n][:], gates[n][:].indirect(places(0, HALF)), yw[n], MULT)
 
         def scatter_z(n):
-            nc.vector.tensor_copy(pages[n % 3][:].indirect(places(0)), zs[n][:])
+            nc.vector.tensor_copy(pages[n][:].indirect(places(0, HALF)), z[n][:])
 
-        def scatter_y(half, n):
-            nc.vector.tensor_tensor(pages[n % 3][:].indirect(places(half)), ys[half, n][:], gw[n, half], MULT)
+        def scatter_y(n, first, count, y):
+            nc.vector.tensor_tensor(pages[n][:].indirect(places(first, count)), y, gw[n][:, first : first + count] if n == 0 else gw[n], MULT)
 
-        y_last = place([P, J], F32, "y_last")
-
-        def down_last(half, number):
-            down(half, 3, number, half)
-            nc.scalar.copy(y_last[:, HALF * half : HALF * (half + 1)], ys[half, 3][:])
-
-        def scatter_last():
-            nc.vector.tensor_tensor(pages[0][:].indirect(offsets[:]), y_last[:], gw[3], MULT)
+        def clear_last_page(where):
+            pages.append(place([P, T], F32, "page3", where))
+            nc.gpsimd.memset(pages[3][:], 0.0)
 
         def store(n):
-            nc.sync.dma_start(out[P * n : P * (n + 1), :], pages[n % 3][:])
+            nc.sync.dma_start(out[P * n : P * (n + 1), :], pages[n][:])
 
-        spread_wgo((4, 5))
+        spread_wgo()
         gather_table_words()
         deal_wu_scales(0)
         weave_wg(0, 0, P)
         deal_wu(0, nc.vector.tensor_copy)
-        deal_wu_scales(1, ("wu0", 1))
-        quantize_wg(0, 0, ("wu0", 0))
-        for chunk in range(4):
-            first_product("ub", 0, chunk, chunk)
+        deal_wu_scales(1, ("spare", 1))
+        quantize_wg(0, 0, ("spare", 0))
+        for group in range(4):
+            first_product("ub", 0, group, group)
         weave_wg(1, 0, 40)
         quantize_wg(1, 0)
-        gather_gate(0)
-        new_h(0, 0, 4)
-        for chunk in range(4):
-            first_product("ga", 0, chunk, 4 + chunk)
-            silu(0, chunk, ("wg00", 2 * chunk))
-            multiply(0, chunk)
-        quantize_h(0, 0, 2)
-        quantize_h(0, 2, 2)
-        weave_wg(0, 1, P)
-        gather_gate(1)
+        gate_times_wgo(0, 0, J)
         deal_wu(1, nc.vector.tensor_copy)
-        quantize_wg(0, 1, ("gate1", 7))
-        new_h(0, 4, 4)
-        for chunk in (4, 5):
-            first_product("ga", 0, chunk, 2 * chunk - 4)
-            first_product("ub", 0, chunk, 2 * chunk - 3)
-            silu(0, chunk, ("wg01", 2 * (chunk - 4)))
-            multiply(0, chunk)
-        for chunk in (6, 7):
-            first_product("ga", 0, chunk, 2 * chunk - 12)
-            first_product("ub", 0, chunk, 2 * chunk - 11)
-        weave_wg(1, 1, 104)
-        for chunk in range(2):
-            first_product("ga", 1, chunk, (4, 6)[chunk], 0)
-            first_product("ub", 1, chunk, (5, 7)[chunk])
+        new_h(0, 0, 4)
+        for group in range(4):
+            first_product("ga", 0, group, 4 + group)
+            silu(0, group, ("table", 2 * group))
+            multiply(0, group)
+        for group in range(2):
+            first_product("ub", 1, group, 6 + group)
+        for group in range(4, 6):
+            first_product("ga", 0, group, group)
+            first_product("ub", 0, group, group - 4)
+        weave_wg(0, 1, 96)
+        quantize_h(0, 0, 2)
+        quantize_wg(0, 1)
+        for group in range(2):
+            first_product("ga", 1, group, 2 + group, 0)
+        weave_wg(1, 1, 56)
+        quantize_h(0, 2, 2)
         quantize_wg(1, 1)
-        for chunk in (6, 7):
-            silu(0, chunk, ("wg11", 2 * (chunk - 6)))
-            multiply(0, chunk)
-        gather_gate(2, 0)
-        quantize_h(0, 4, 4)
+        clear_last_page(("woven1", 4))
+        new_h(0, 4, 2)
+        for group in range(4, 6):
+            silu(0, group, ("wg11", 2 * (group - 4)))
+            multiply(0, group)
+        for group in range(2):
+            first_product("ga", 1, group, None, 1)
+        for group in range(2, 4):
+            first_product("ga", 1, group, 2 + group)
+            first_product("ub", 1, group, group - 2)
         new_h(1, 0, 4)
-        for chunk in range(4):
-            first_product("ga", 1, chunk, (4, 6, 0, 2)[chunk], 1 if chunk < 2 else None)
-            if chunk >= 2:
-                first_product("ub", 1, chunk, (1, 3)[chunk - 2])
-            silu(1, chunk, ("wg10", 2 * chunk))
-            multiply(1, chunk)
+        for group in range(4):
+            silu(1, group, ("wg10", 2 * group))
+        for group in range(3):
+            multiply(1, group)
         quantize_h(1, 0, 2)
+        multiply(1, 3)
+        quantize_h(0, 4, 2)
+        y_first = [place([P, QUARTER], F32, f"y_first{pair}") for pair in range(2)]
+        down_rows(0, 0, 2, y_first[0][:], slice(0, QUARTER))
+        for group in range(2):
+            down_tokens(0, group, 6 + group)
+            down_tokens(1, group, None)
+            weigh(group)
         quantize_h(1, 2, 2)
-        gather_gate(2, 1, ("wg10", 6))
-
-        for n in range(3):
-            down(0, n, (5, 7, 2)[n] if False else (5, 7, 1)[n])
-        gate_y(0, nc.vector)
-        for n in range(1, 3):
-            empty_y(0, n, ("table", 2 * n))
-        gate_y(1, nc.gpsimd)
-        gate_y(2, nc.gpsimd)
-        new_h(1, 4, 4)
-        for chunk in range(4, 8):
-            x, y, z = (5, 7, 1)
-            first_product("ga", 1, chunk, (x, z, y, x)[chunk - 4])
-            first_product("ub", 1, chunk, (y, x, z, y)[chunk - 4])
-            silu(1, chunk, ("gate0", 2 * (chunk - 4)), True)
-            stage(1, chunk, ("woven0", 2 * (chunk - 4)))
-            multiply(1, chunk)
-
-            if chunk == 5:
-                down_last(0, 3)
-        for n in range(3):
-            scatter_z(n)
-
-        quantize_h(1, 4, 4)
-        gather_gate(3, None, ("woven0", 4))
-        for n in range(3):
-            down(1, n, (4, 6, 0)[n], min(n, 1))
-            empty_y(1, n, ("wg01", 2 * n))
-            scatter_y(1, n)
+        scatter_y(0, 0, QUARTER, y_first[0][:])
+        gate_times_wgo(1, HALF, HALF, ("wg10", 6))
+        down_rows(0, 0, 5, y_first[1][:], slice(QUARTER, HALF))
+        for group in range(2, 4):
+            down_tokens(0, group, (0, 1)[group - 2])
+            down_tokens(1, group, None)
+            weigh(group)
+        scatter_y(0, QUARTER, QUARTER, y_first[1][:])
+        turn_middle(0, 3)
+        turn_middle(1, 4)
+        new_stage(0, 6, 2, ("wu1", 0))
+        stage(0, 6, 6, (5, 0))
+        stage(0, 6, 7, (1, 3))
+        gate_times_yw(1)
+        gate_times_yw(2)
+        new_stage(1, 4, 2, ("wg01", 0))
+        stage(1, 4, 4, (4, 5))
+        stage(1, 4, 5, (0, 1))
+        turn_last(3)
+        new_stage(1, 6, 2, ("wg11", 0))
+        stage(1, 6, 6, (4, 5))
+        stage(1, 6, 7, (0, 1))
+        new_h(0, 6, 2, ("yw", 1))
+        new_h(1, 4, 2, ("yw", 4))
+        multiply_staged(0, 6)
+        multiply_staged(1, 4)
+        scatter_z(1)
+        scatter_z(2)
+        gate_times_yw(3, ("wg01", 0))
+        new_h(1, 6, 2, ("yw", 8))
+        multiply_staged(1, 6)
+        quantize_h(0, 6, 2)
+        quantize_h(1, 4, 2)
+        scatter_z(3)
+        quantize_h(1, 6, 2)
+        gate_times_wgo(2, HALF, HALF, ("wg11", 0))
+        gate_times_wgo(3, HALF, HALF, ("wg11", 2))
+        for n in range(4):
+            y = place([P, HALF], F32, f"y{n}", ("wg00", 2 * n))
+            down_rows(1, n, (2, 6, 7, 3)[n], y[:])
+            scatter_y(n, HALF, HALF, y[:])
             store(n)
-        down_last(1, 2)
-        scatter_last()
-        store(3)

@@ -326,6 +326,7 @@ def tile_list_modp_gsilu_mix_gate_kernel(tc, tab_words, tab_scales, wg, wu_words
         quantize_wg(1, 0)
         gate_times_wgo(0, 0, J)
         deal_wu(1, nc.vector.tensor_copy)
+        clear_last_page(("wu1", 0))
         new_h(0, 0, 4)
         for group in range(4):
             first_product("ga", 0, group, 4 + group)
@@ -336,15 +337,13 @@ def tile_list_modp_gsilu_mix_gate_kernel(tc, tab_words, tab_scales, wg, wu_words
         for group in range(4, 6):
             first_product("ga", 0, group, group)
             first_product("ub", 0, group, group - 4)
-        weave_wg(0, 1, 96)
-        quantize_h(0, 0, 2)
+        weave_wg(0, 1, P)
+        quantize_h(0, 0, 4)
         quantize_wg(0, 1)
         for group in range(2):
             first_product("ga", 1, group, 2 + group, 0)
         weave_wg(1, 1, 56)
-        quantize_h(0, 2, 2)
         quantize_wg(1, 1)
-        clear_last_page(("woven1", 4))
         new_h(0, 4, 2)
         for group in range(4, 6):
             silu(0, group, ("wg11", 2 * (group - 4)))
@@ -354,6 +353,7 @@ def tile_list_modp_gsilu_mix_gate_kernel(tc, tab_words, tab_scales, wg, wu_words
         for group in range(2, 4):
             first_product("ga", 1, group, 2 + group)
             first_product("ub", 1, group, group - 2)
+        quantize_h(0, 4, 2)
         new_h(1, 0, 4)
         for group in range(4):
             silu(1, group, ("wg10", 2 * group))
@@ -361,25 +361,23 @@ def tile_list_modp_gsilu_mix_gate_kernel(tc, tab_words, tab_scales, wg, wu_words
             multiply(1, group)
         quantize_h(1, 0, 2)
         multiply(1, 3)
-        quantize_h(0, 4, 2)
-        y_first = [place([P, QUARTER], F32, f"y_first{pair}") for pair in range(2)]
-        down_rows(0, 0, 2, y_first[0][:], slice(0, QUARTER))
+        y_first = place([P, HALF], F32, "y_first")
+        down_rows(0, 0, 2, y_first[:, :QUARTER], slice(0, QUARTER))
         for group in range(2):
             down_tokens(0, group, 6 + group)
             down_tokens(1, group, None)
             weigh(group)
         quantize_h(1, 2, 2)
-        scatter_y(0, 0, QUARTER, y_first[0][:])
         gate_times_wgo(1, HALF, HALF, ("wg10", 6))
-        down_rows(0, 0, 5, y_first[1][:], slice(QUARTER, HALF))
+        down_rows(0, 0, 5, y_first[:, QUARTER:], slice(QUARTER, HALF))
+        scatter_y(0, 0, HALF, y_first[:])
         for group in range(2, 4):
             down_tokens(0, group, (0, 1)[group - 2])
             down_tokens(1, group, None)
             weigh(group)
-        scatter_y(0, QUARTER, QUARTER, y_first[1][:])
         turn_middle(0, 3)
         turn_middle(1, 4)
-        new_stage(0, 6, 2, ("wu1", 0))
+        new_stage(0, 6, 2, ("woven0", 0))
         stage(0, 6, 6, (5, 0))
         stage(0, 6, 7, (1, 3))
         gate_times_yw(1)

@@ -332,28 +332,25 @@ def tile_list_modp_gsilu_mix_gate_kernel(tc, tab_words, tab_scales, wg, wu_words
             first_product("ga", 0, group, 4 + group)
             silu(0, group, ("table", 2 * group))
             multiply(0, group)
-        for group in range(2):
-            first_product("ub", 1, group, 6 + group)
-        for group in range(4, 6):
-            first_product("ga", 0, group, group)
-            first_product("ub", 0, group, group - 4)
+        for group in range(3):
+            first_product("ub", 1, group, (6, 7, 5)[group])
+        first_product("ga", 0, 4, 4)
+        first_product("ub", 0, 4, 0)
         weave_wg(0, 1, P)
         quantize_h(0, 0, 4)
         quantize_wg(0, 1)
-        for group in range(2):
-            first_product("ga", 1, group, 2 + group, 0)
-        weave_wg(1, 1, 56)
+        for group in range(3):
+            first_product("ga", 1, group, (2, 3, 1)[group], 0)
+        weave_wg(1, 1, 72)
         quantize_wg(1, 1)
-        new_h(0, 4, 2)
-        for group in range(4, 6):
-            silu(0, group, ("wg11", 2 * (group - 4)))
-            multiply(0, group)
-        for group in range(2):
+        new_h(0, 4, 1)
+        silu(0, 4, ("wg11", 0))
+        multiply(0, 4)
+        for group in range(3):
             first_product("ga", 1, group, None, 1)
-        for group in range(2, 4):
-            first_product("ga", 1, group, 2 + group)
-            first_product("ub", 1, group, group - 2)
-        quantize_h(0, 4, 2)
+        first_product("ga", 1, 3, 4)
+        first_product("ub", 1, 3, 0)
+        quantize_h(0, 4, 1)
         new_h(1, 0, 4)
         for group in range(4):
             silu(1, group, ("wg10", 2 * group))
@@ -369,36 +366,37 @@ def tile_list_modp_gsilu_mix_gate_kernel(tc, tab_words, tab_scales, wg, wu_words
             weigh(group)
         quantize_h(1, 2, 2)
         gate_times_wgo(1, HALF, HALF, ("wg10", 6))
-        down_rows(0, 0, 5, y_first[:, QUARTER:], slice(QUARTER, HALF))
+        down_rows(0, 0, 1, y_first[:, QUARTER:], slice(QUARTER, HALF))
         scatter_y(0, 0, HALF, y_first[:])
         for group in range(2, 4):
-            down_tokens(0, group, (0, 1)[group - 2])
+            down_tokens(0, group, (5, 0)[group - 2])
             down_tokens(1, group, None)
             weigh(group)
         turn_middle(0, 3)
         turn_middle(1, 4)
-        new_stage(0, 6, 2, ("woven0", 0))
-        stage(0, 6, 6, (5, 0))
-        stage(0, 6, 7, (1, 3))
+        new_stage(0, 5, 3, ("woven0", 0))
+        stage(0, 5, 5, (2, 6))
+        stage(0, 5, 6, (7, 1))
+        stage(0, 5, 7, (5, 0))
         gate_times_yw(1)
         gate_times_yw(2)
         new_stage(1, 4, 2, ("wg01", 0))
-        stage(1, 4, 4, (4, 5))
-        stage(1, 4, 5, (0, 1))
-        turn_last(3)
+        stage(1, 4, 4, (3, 4))
+        stage(1, 4, 5, (2, 6))
+        turn_last(7)
         new_stage(1, 6, 2, ("wg11", 0))
-        stage(1, 6, 6, (4, 5))
-        stage(1, 6, 7, (0, 1))
-        new_h(0, 6, 2, ("yw", 1))
+        stage(1, 6, 6, (1, 5))
+        stage(1, 6, 7, (0, 3))
+        new_h(0, 5, 3, ("yw", 0))
         new_h(1, 4, 2, ("yw", 4))
-        multiply_staged(0, 6)
+        multiply_staged(0, 5)
         multiply_staged(1, 4)
         scatter_z(1)
         scatter_z(2)
         gate_times_yw(3, ("wg01", 0))
         new_h(1, 6, 2, ("yw", 8))
         multiply_staged(1, 6)
-        quantize_h(0, 6, 2)
+        quantize_h(0, 5, 3)
         quantize_h(1, 4, 2)
         scatter_z(3)
         quantize_h(1, 6, 2)
@@ -406,6 +404,6 @@ def tile_list_modp_gsilu_mix_gate_kernel(tc, tab_words, tab_scales, wg, wu_words
         gate_times_wgo(3, HALF, HALF, ("wg11", 2))
         for n in range(4):
             y = place([P, HALF], F32, f"y{n}", ("wg00", 2 * n))
-            down_rows(1, n, (2, 6, 7, 3)[n], y[:])
+            down_rows(1, n, (4, 2, 6, 7)[n], y[:])
             scatter_y(n, HALF, HALF, y[:])
             store(n)

@@ -35,7 +35,7 @@ def tile_list_modp_gsilu_mix_gate_kernel(tc, tab_words, tab_scales, wg, wu_words
         psum = ctx.enter_context(tc.psum_pool(name="psum", bufs=1))
 
         region = {"gates": 0, "wg00": 32, "wg10": 40, "wg01": 48, "wg11": 56, "wu0": 114, "wu1": 64,
-                  "woven0": 72, "woven1": 80, "table": 88, "turned": 96, "yw": 104, "spare": 114}
+                  "woven0": 72, "woven1": 80, "table": 88, "turned": 96, "yw": 104, "spare": 114, "scales": 118}
 
         def place(shape, dtype, name, where=None):
             if where is None:
@@ -52,11 +52,10 @@ def tile_list_modp_gsilu_mix_gate_kernel(tc, tab_words, tab_scales, wg, wu_words
             return offsets[:, first // 16 : (first + count) // 16]
 
         w_col = place([P, J // P], F32, "w_col")
-        tab_s = place([P, T], U8, "tab_s")
+        tab_s = place([P, T], U8, "tab_s", ("scales", 0))
         tab_w = place([P, T], I32, "tab_w", ("table", 0))
         wu_s_raw = place([P, 2 * R], U8, "wu_s_raw")
         v_s_raw = place([P, J], U8, "v_s_raw")
-        v_s = place([P, 2, 2, HALF], U8, "v_s")
         wd_s = place([P, N], U8, "wd_s")
         ident = place([P, P], F32, "ident")
         pages = [place([P, T], F32, f"page{n}") for n in range(3)]
@@ -72,10 +71,11 @@ def tile_list_modp_gsilu_mix_gate_kernel(tc, tab_words, tab_scales, wg, wu_words
         nc.vector.memset(pages[0][:, 0 : T // 2 - 1], 0.0)
         nc.vector.memset(pages[0][:, T // 2 - 1 : T], 0.0)
         make_identity(nc, ident[:])
-        nc.gpsimd.memset(v_s[:].bitcast(I32), 0)
         nc.gpsimd.memset(wd_s[:].bitcast(I32), 0)
         for page in pages[1:]:
             nc.gpsimd.memset(page[:], 0.0)
+
+        v_s = place([P, 2, 2, HALF], U8, "v_s", ("scales", 0))
 
         def load_table_scales():
             for a in range(2):

@@ -326,7 +326,6 @@ def tile_list_modp_gsilu_mix_gate_kernel(tc, tab_words, tab_scales, wg, wu_words
         quantize_wg(1, 0)
         gate_times_wgo(0, 0, J)
         deal_wu(1, nc.vector.tensor_copy)
-        clear_last_page(("wu1", 0))
         new_h(0, 0, 4)
         for group in range(4):
             first_product("ga", 0, group, 4 + group)
@@ -336,13 +335,14 @@ def tile_list_modp_gsilu_mix_gate_kernel(tc, tab_words, tab_scales, wg, wu_words
             first_product("ub", 1, group, (6, 7, 5)[group])
         first_product("ga", 0, 4, 4)
         first_product("ub", 0, 4, 0)
-        weave_wg(0, 1, P)
+        weave_wg(0, 1, 96)
         quantize_h(0, 0, 4)
         quantize_wg(0, 1)
         for group in range(3):
             first_product("ga", 1, group, (2, 3, 1)[group], 0)
         weave_wg(1, 1, 72)
         quantize_wg(1, 1)
+        clear_last_page(("woven1", 4))
         new_h(0, 4, 1)
         silu(0, 4, ("wg11", 0))
         multiply(0, 4)
@@ -350,10 +350,9 @@ def tile_list_modp_gsilu_mix_gate_kernel(tc, tab_words, tab_scales, wg, wu_words
             first_product("ga", 1, group, None, 1)
         first_product("ga", 1, 3, 4)
         first_product("ub", 1, 3, 0)
-        quantize_h(0, 4, 1)
         new_h(1, 0, 4)
         for group in range(4):
-            silu(1, group, ("wg10", 2 * group))
+            silu(1, group, ("wg10", (0, 2, 8, 5)[group]))
         for group in range(3):
             multiply(1, group)
         quantize_h(1, 0, 2)
@@ -365,6 +364,7 @@ def tile_list_modp_gsilu_mix_gate_kernel(tc, tab_words, tab_scales, wg, wu_words
             down_tokens(1, group, None)
             weigh(group)
         quantize_h(1, 2, 2)
+        quantize_h(0, 4, 1, ("wg10", 4))
         gate_times_wgo(1, HALF, HALF, ("wg10", 6))
         down_rows(0, 0, 1, y_first[:, QUARTER:], slice(QUARTER, HALF))
         scatter_y(0, 0, HALF, y_first[:])

@@ -25,6 +25,7 @@ HALF = J // 2
 QUARTER = J // 4
 GROUP = 128
 KIB = 1024
+LIFT = 2432
 
 
 def tile_list_modp_gsilu_mix_gate_kernel(tc, tab_words, tab_scales, wg, wu_words, wu_scales, wd8_words, wd8_scales, wd4_words, wd4_scales, gT, wgo, offs, out):
@@ -34,13 +35,13 @@ def tile_list_modp_gsilu_mix_gate_kernel(tc, tab_words, tab_scales, wg, wu_words
         share = ctx.enter_context(tc.tile_pool(name="share", bufs=1))
         psum = ctx.enter_context(tc.psum_pool(name="psum", bufs=1))
 
-        region = {"gates": 0, "wg00": 32, "wg10": 40, "wg01": 48, "wg11": 56, "wu0": 114, "wu1": 64,
-                  "woven0": 72, "woven1": 80, "table": 88, "turned": 96, "yw": 104, "spare": 114, "scales": 118}
+        region = {"words": 0, "woven": 32, "wu1": 44, "h": 48, "pages": 64, "gates": 96, "wg00": 128, "wg10": 136, "wg01": 144, "wg11": 152,
+                  "table": 160, "turned": 168, "yw": 176, "gw0": 186, "wu0": 192, "scales": 196, "pairs": 208}
 
         def place(shape, dtype, name, where=None):
             if where is None:
                 return keep.tile(shape, dtype, name=name, align_bytes=64)
-            return share.tile(shape, dtype, name=name, offset=KIB * (region[where[0]] + where[1]), align_bytes=64)
+            return share.tile(shape, dtype, name=name, offset=LIFT + int(KIB * (region[where[0]] + where[1])), align_bytes=64)
 
         def bank(number, shape, name):
             return psum.tile(shape, F32, name=name, tag=f"bank{number}")
@@ -52,30 +53,30 @@ def tile_list_modp_gsilu_mix_gate_kernel(tc, tab_words, tab_scales, wg, wu_words
             return offsets[:, first // 16 : (first + count) // 16]
 
         w_col = place([P, J // P], F32, "w_col")
-        tab_s = place([P, T], U8, "tab_s", ("scales", 0))
+        tab_s = place([P, T], U8, "tab_s")
         tab_w = place([P, T], I32, "tab_w", ("table", 0))
         wu_s_raw = place([P, 2 * R], U8, "wu_s_raw")
         v_s_raw = place([P, J], U8, "v_s_raw")
-        wd_s = place([P, N], U8, "wd_s")
-        ident = place([P, P], F32, "ident")
-        pages = [place([P, T], F32, f"page{n}") for n in range(3)]
+        v_s = place([P, 2, 2, HALF], U8, "v_s", ("scales", 0))
+        wd_s = place([P, N], U8, "wd_s", ("scales", 2))
+        ident = place([P, P], F32, "ident", ("scales", 8))
+        pages = [place([P, T], F32, f"page{n}", ("pages", 8 * n)) for n in range(3)]
         gates = [place([P, T], F32, f"gate{n}", ("gates", 8 * n)) for n in range(4)]
         wu_raw = [place([P, 2, PASS], I32, f"wu_raw{b}", (f"wu{b}", 0)) for b in range(2)]
         wg_raw = {(a, b): place([P, PACK, PASS], F32, f"wg_raw{a}{b}", (f"wg{a}{b}", 0)) for a in range(2) for b in range(2)}
-        woven = {(a, b): place([P, PACK, P, PACK], BF16, f"woven{a}{b}", (f"woven{b}", 4 * a)) for a in range(2) for b in range(2)}
-        wd8_w = place([P, N], I32, "wd8_w")
-        wd4_w = place([P, 2 * N], U8, "wd4_w")
+        woven = {(a, b): place([P, PACK, P, PACK], BF16, f"woven{a}{b}", ("pages", 24) if a + b == 2 else ("woven", 4 * a + 8 * b)) for a in range(2) for b in range(2)}
+        wd8_w = place([P, N], I32, "wd8_w", ("words", 20))
+        wd4_w = place([P, 2 * N], U8, "wd4_w", ("words", 22))
 
         nc.gpsimd.memset(wu_s_raw[:].bitcast(I32), 0)
         nc.gpsimd.memset(tab_s[0:96, :].bitcast(I32), 0)
         nc.vector.memset(pages[0][:, 0 : T // 2 - 1], 0.0)
         nc.vector.memset(pages[0][:, T // 2 - 1 : T], 0.0)
         make_identity(nc, ident[:])
+        nc.gpsimd.memset(v_s[:].bitcast(I32), 0)
         nc.gpsimd.memset(wd_s[:].bitcast(I32), 0)
         for page in pages[1:]:
             nc.gpsimd.memset(page[:], 0.0)
-
-        v_s = place([P, 2, 2, HALF], U8, "v_s", ("scales", 0))
 
         def load_table_scales():
             for a in range(2):
@@ -151,8 +152,8 @@ def tile_list_modp_gsilu_mix_gate_kernel(tc, tab_words, tab_scales, wg, wu_words
                 nc.tensor.transpose(upright[:, c, :], wgo_all[:, GROUP * c : GROUP * (c + 1)], ident[:])
             nc.scalar.copy(w_tok[:], upright[:, :, 0])
 
-        v_pairs = [place([P, HALF], U32, f"v_pairs{half}") for half in range(2)]
-        v_w = [place([P, 2, HALF], U16, f"v_w{half}") for half in range(2)]
+        v_pairs = [place([P, HALF], U32, f"v_pairs{half}", ("pairs", 2 * half)) for half in range(2)]
+        v_w = [place([P, 2, HALF], U16, f"v_w{half}", ("words", 2 * half)) for half in range(2)]
 
         def gather_table_words():
             for half in range(2):
@@ -165,15 +166,15 @@ def tile_list_modp_gsilu_mix_gate_kernel(tc, tab_words, tab_scales, wg, wu_words
 
         wu_s, wu_w, wg_w, wg_s, gw, h, h_w, h_s, sums, act, staged, banks, turned, y_bank, yw, z = [{} for name in range(16)]
 
-        def deal_wu_scales(b, where=None):
+        def deal_wu_scales(b, where):
             wu_s[b] = place([P, 2 * PASS], U8, f"wu_s{b}", where)
             nc.vector.tensor_copy(
                 wu_s[b][:].rearrange("p (a t g e) -> p a g t e", a=2, t=PACK, e=16),
                 wu_s_raw[:].rearrange("p (a b g e t) -> p b a g t e", a=2, b=2, t=PACK, e=16)[:, b],
             )
 
-        def deal_wu(b, copy, where=None):
-            wu_w[b] = place([P, 2 * PASS], U32, f"wu_w{b}", where)
+        def deal_wu(b, copy):
+            wu_w[b] = place([P, 2 * PASS], U32, f"wu_w{b}", ("words", 4 + 4 * b))
             copy(
                 wu_w[b][:].rearrange("p (a u e m) -> p a u m e", a=2, u=2, e=2),
                 wu_raw[b][:].bitcast(U32).rearrange("p a (m u e) -> p a u m e", u=2, e=2),
@@ -187,8 +188,8 @@ def tile_list_modp_gsilu_mix_gate_kernel(tc, tab_words, tab_scales, wg, wu_words
                         wg_raw[a, b][:].rearrange("p i (m t) -> p m i t", t=PACK)[:, ms],
                     )
 
-        def quantize_wg(a, b, where=None):
-            wg_w[a, b] = place([P, PASS], U32, f"wg_w{a}{b}")
+        def quantize_wg(a, b, where):
+            wg_w[a, b] = place([P, PASS], U32, f"wg_w{a}{b}", ("words", 12 + 2 * a + 4 * b))
             wg_s[a, b] = place([P, PASS], U8, f"wg_s{a}{b}", where)
             nc.vector.quantize_mx(out=wg_w[a, b][:].bitcast(FP8X4), scales=wg_s[a, b][:], in_=woven[a, b][:].rearrange("p t m i -> p (t m i)"))
 
@@ -249,8 +250,8 @@ def tile_list_modp_gsilu_mix_gate_kernel(tc, tab_words, tab_scales, wg, wu_words
             rows, c = h[b, first]
             half, start = divmod(GROUP * first, HALF)
             if (b, half) not in h_w:
-                h_w[b, half] = place([P, HALF], U32, f"h_w{b}{half}", where)
-                h_s[b, half] = place([P, HALF], U8, f"h_s{b}{half}")
+                h_w[b, half] = place([P, HALF], U32, f"h_w{b}{half}", where or ("words", 23 + 2 * b + 4 * half))
+                h_s[b, half] = place([P, HALF], U8, f"h_s{b}{half}", ("scales", 6 + 0.5 * b + half))
             tok = slice(start, start + GROUP * count)
             nc.vector.quantize_mx(out=h_w[b, half][:, tok].bitcast(FP8X4), scales=h_s[b, half][:, tok], in_=rows[:, GROUP * c : GROUP * (c + count), :].rearrange("p j t -> p (j t)"))
 
@@ -315,18 +316,18 @@ def tile_list_modp_gsilu_mix_gate_kernel(tc, tab_words, tab_scales, wg, wu_words
 
         spread_wgo()
         gather_table_words()
-        deal_wu_scales(0)
+        deal_wu_scales(0, ("scales", 3))
         weave_wg(0, 0, P)
         deal_wu(0, nc.vector.tensor_copy)
-        deal_wu_scales(1, ("spare", 1))
-        quantize_wg(0, 0, ("spare", 0))
+        deal_wu_scales(1, ("wu0", 1))
+        quantize_wg(0, 0, ("wu0", 0))
         for group in range(4):
             first_product("ub", 0, group, group)
         weave_wg(1, 0, 40)
-        quantize_wg(1, 0)
-        gate_times_wgo(0, 0, J)
+        quantize_wg(1, 0, ("scales", 4))
+        gate_times_wgo(0, 0, J, ("gw0", 0))
         deal_wu(1, nc.vector.tensor_copy)
-        new_h(0, 0, 4)
+        new_h(0, 0, 4, ("h", 0))
         for group in range(4):
             first_product("ga", 0, group, 4 + group)
             silu(0, group, ("table", 2 * group))
@@ -337,27 +338,27 @@ def tile_list_modp_gsilu_mix_gate_kernel(tc, tab_words, tab_scales, wg, wu_words
         first_product("ub", 0, 4, 0)
         weave_wg(0, 1, 96)
         quantize_h(0, 0, 4)
-        quantize_wg(0, 1)
+        quantize_wg(0, 1, ("scales", 4.5))
         for group in range(3):
             first_product("ga", 1, group, (2, 3, 1)[group], 0)
         weave_wg(1, 1, 72)
-        quantize_wg(1, 1)
-        clear_last_page(("woven1", 4))
-        new_h(0, 4, 1)
+        quantize_wg(1, 1, ("scales", 5))
+        clear_last_page(("pages", 24))
+        new_h(0, 4, 1, ("h", 4))
         silu(0, 4, ("wg11", 0))
         multiply(0, 4)
         for group in range(3):
             first_product("ga", 1, group, None, 1)
         first_product("ga", 1, 3, 4)
         first_product("ub", 1, 3, 0)
-        new_h(1, 0, 4)
+        new_h(1, 0, 4, ("h", 5))
         for group in range(4):
             silu(1, group, ("wg10", (0, 2, 8, 5)[group]))
         for group in range(3):
             multiply(1, group)
         quantize_h(1, 0, 2)
         multiply(1, 3)
-        y_first = place([P, HALF], F32, "y_first")
+        y_first = place([P, HALF], F32, "y_first", ("h", 9))
         down_rows(0, 0, 2, y_first[:, :QUARTER], slice(0, QUARTER))
         for group in range(2):
             down_tokens(0, group, 6 + group)
@@ -374,7 +375,7 @@ def tile_list_modp_gsilu_mix_gate_kernel(tc, tab_words, tab_scales, wg, wu_words
             weigh(group)
         turn_middle(0, 3)
         turn_middle(1, 4)
-        new_stage(0, 5, 3, ("woven0", 0))
+        new_stage(0, 5, 3, ("woven", 0))
         stage(0, 5, 5, (2, 6))
         stage(0, 5, 6, (7, 1))
         stage(0, 5, 7, (5, 0))

from contextlib import ExitStack

import concourse.mybir as mybir
from concourse.masks import make_identity

K, R, N, T, J = 1024, 1024, 512, 2048, 1024
FLOPS = 2 * K * R * J * 2 + 2 * R * N * J

F32 = mybir.dt.float32
BF16 = mybir.dt.bfloat16
I32 = mybir.dt.int32
U32 = mybir.dt.uint32
U16 = mybir.dt.uint16
U8 = mybir.dt.uint8
FP8X4 = mybir.dt.float8_e4m3fn_x4
FP4X4 = mybir.dt.float4_e2m1fn_x4
MULT = mybir.AluOpType.mult
SILU = mybir.ActivationFunctionType.Silu
COPY = mybir.ActivationFunctionType.Copy

P = 128
PACK = 4
PASS = P * PACK
HALF = J // 2
QUARTER = J // 4
GROUP = 128
KIB = 1024
LIFT = 2432


def tile_list_modp_gsilu_mix_gate_kernel(tc, tab_words, tab_scales, wg, wu_words, wu_scales, wd8_words, wd8_scales, wd4_words, wd4_scales, gT, wgo, offs, out):
    nc = tc.nc
    with ExitStack() as ctx:
        keep = ctx.enter_context(tc.tile_pool(name="keep", bufs=1))
        share = ctx.enter_context(tc.tile_pool(name="share", bufs=1))
        psum = ctx.enter_context(tc.psum_pool(name="psum", bufs=1))

        region = {"words": 0, "woven": 32, "wu1": 44, "h": 48, "pages": 64, "gates": 96, "wg00": 128, "wg10": 136, "wg01": 144, "wg11": 152,
                  "table": 160, "turned": 168, "yw": 176, "gw0": 186, "wu0": 192, "scales": 196, "pairs": 208}

        def place(shape, dtype, name, where=None):
            if where is None:
                return keep.tile(shape, dtype, name=name, align_bytes=64)
            return share.tile(shape, dtype, name=name, offset=LIFT + int(KIB * (region[where[0]] + where[1])), align_bytes=64)

        def bank(number, shape, name):
            return psum.tile(shape, F32, name=name, tag=f"bank{number}")

        offsets = keep.tile([P, J // 16], U16, name="offsets")
        nc.sync.dma_start(offsets[:], offs)

        def places(first, count):
            return offsets[:, first // 16 : (first + count) // 16]

        w_col = place([P, J // P], F32, "w_col")
        tab_s = place([P, T], U8, "tab_s")
        tab_w = place([P, T], I32, "tab_w", ("table", 0))
        wu_s_raw = place([P, 2 * R], U8, "wu_s_raw")
        v_s_raw = place([P, J], U8, "v_s_raw")
        v_s = place([P, 2, 2, HALF], U8, "v_s", ("scales", 0))
        wd_s = place([P, N], U8, "wd_s", ("scales", 2))
        ident = place([P, P], F32, "ident", ("scales", 8))
        pages = [place([P, T], F32, f"page{n}", ("pages", 8 * n)) for n in range(3)]
        gates = [place([P, T], F32, f"gate{n}", ("gates", 8 * n)) for n in range(4)]
        wu_raw = [place([P, 2, PASS], I32, f"wu_raw{b}", (f"wu{b}", 0)) for b in range(2)]
        wg_raw = {(a, b): place([P, PACK, PASS], F32, f"wg_raw{a}{b}", (f"wg{a}{b}", 0)) for a in range(2) for b in range(2)}
        woven = {(a, b): place([P, PACK, P, PACK], BF16, f"woven{a}{b}", ("pages", 24) if a + b == 2 else ("woven", 4 * a + 8 * b)) for a in range(2) for b in range(2)}
        wd8_w = place([P, N], I32, "wd8_w", ("words", 20))
        wd4_w = place([P, 2 * N], U8, "wd4_w", ("words", 22))

        nc.gpsimd.memset(wu_s_raw[:].bitcast(I32), 0)
        nc.gpsimd.memset(tab_s[0:96, :].bitcast(I32), 0)
        nc.vector.memset(pages[0][:, 0 : T // 2 - 1], 0.0)
        nc.vector.memset(pages[0][:, T // 2 - 1 : T], 0.0)
        make_identity(nc, ident[:])
        nc.gpsimd.memset(v_s[:].bitcast(I32), 0)
        nc.gpsimd.memset(wd_s[:].bitcast(I32), 0)
        for page in pages[1:]:
            nc.gpsimd.memset(page[:], 0.0)

        def load_table_scales():
            for a in range(2):
                nc.sync.dma_start(tab_s[96 + a : P : 2, :].bitcast(I32), tab_scales[a].bitcast(I32))

        def load_table_words():
            nc.sync.dma_start(tab_w[:], tab_words[0].rearrange("p t i -> p (t i)").bitcast(I32))

        def load_wgo():
            nc.sync.dma_start(w_col[:], wgo[0].rearrange("(p c) -> p c", p=P))

        def load_wg(a, b):
            nc.sync.dma_start(wg_raw[a, b][:], wg[PASS * a : PASS * (a + 1), PASS * b : PASS * (b + 1)].rearrange("(p i) c -> p i c", i=PACK))

        def load_wu(b):
            nc.sync.dma_start(wu_raw[b][:], wu_words[:, :, PASS * b : PASS * (b + 1), :].rearrange("a p r i -> p a (r i)").bitcast(I32))

        def load_wd():
            nc.sync.dma_start(wd8_w[:], wd8_words[0].rearrange("p n i -> p (n i)").bitcast(I32))
            nc.sync.dma_start(wd4_w[:].bitcast(I32), wd4_words[0].bitcast(I32))

        def load_wd_scales(first, scales):
            for q in range(4):
                nc.sync.dma_start(wd_s[32 * q + first : 32 * q + first + 4, :].bitcast(I32), scales[0, 4 * q : 4 * q + 4, :].bitcast(I32))

        def load_wu_scales():
            for q in range(4):
                nc.sync.dma_start(wu_s_raw[32 * q : 32 * q + 4, :].bitcast(I32).rearrange("r (a c) -> r a c", a=2), wu_scales[:, 4 * q : 4 * q + 4, :].bitcast(I32).rearrange("a r c -> r a c"))

        def load_gate(n):
            nc.sync.dma_start(gates[n][:], gT[P * n : P * (n + 1), :])

        def gather_table_scales():
            nc.vector.tensor_copy(v_s_raw[:], tab_s[:].indirect(offsets[:]))

        def move_table_scales(half):
            for q in range(4):
                nc.sync.dma_start(v_s[32 * q : 32 * q + 4, half].rearrange("r a c -> r (a c)").bitcast(I32), v_s_raw[96 + 8 * q : 96 + 8 * q + 8, HALF * half : HALF * (half + 1)].bitcast(I32))

        load_table_scales()
        load_table_words()
        load_wu_scales()
        load_wgo()
        load_wg(0, 0)
        gather_table_scales()
        move_table_scales(0)
        load_wu(0)
        load_wg(1, 0)
        load_gate(0)
        load_wu(1)
        load_wg(0, 1)
        move_table_scales(1)
        load_wg(1, 1)
        load_wd_scales(4, wd8_scales)
        load_wd()
        load_gate(1)
        load_wd_scales(0, wd4_scales)
        load_gate(2)
        load_gate(3)

        wgo_sb = place([P, P, J // P], F32, "wgo_sb")
        wgo_all = wgo_sb[:].rearrange("q p c -> q (p c)")
        w_tok = place([P, HALF // GROUP], F32, "w_tok")

        def spread_wgo():
            for g in range(2):
                spread = bank(4 + g, [P, PACK, P], f"spread{g}")
                for c in range(PACK):
                    nc.tensor.transpose(spread[:, c, :], w_col[:, PACK * g + c : PACK * g + c + 1].to_broadcast([P, P]), ident[:])
                nc.scalar.copy(wgo_sb[:, :, PACK * g : PACK * (g + 1)], spread[:].rearrange("q c p -> q p c"))
            upright = bank(6, [P, PACK, P], "upright")
            for c in range(PACK):
                nc.tensor.transpose(upright[:, c, :], wgo_all[:, GROUP * c : GROUP * (c + 1)], ident[:])
            nc.scalar.copy(w_tok[:], upright[:, :, 0])

        v_pairs = [place([P, HALF], U32, f"v_pairs{half}", ("pairs", 2 * half)) for half in range(2)]
        v_w = [place([P, 2, HALF], U16, f"v_w{half}", ("words", 2 * half)) for half in range(2)]

        def gather_table_words():
            for half in range(2):
                nc.vector.tensor_copy(v_pairs[half][:], tab_w[:].bitcast(U32).indirect(places(HALF * half, HALF)))
            for half in range(2):
                nc.vector.tensor_copy(
                    v_w[half][:].rearrange("p d (g e) -> p g d e", e=8),
                    v_pairs[half][:].bitcast(U16).rearrange("p (g e d) -> p g d e", e=8, d=2),
                )

        wu_s, wu_w, wg_w, wg_s, gw, h, h_w, h_s, sums, act, staged, banks, turned, y_bank, yw, z = [{} for name in range(16)]

        def deal_wu_scales(b, where):
            wu_s[b] = place([P, 2 * PASS], U8, f"wu_s{b}", where)
            nc.vector.tensor_copy(
                wu_s[b][:].rearrange("p (a t g e) -> p a g t e", a=2, t=PACK, e=16),
                wu_s_raw[:].rearrange("p (a b g e t) -> p b a g t e", a=2, b=2, t=PACK, e=16)[:, b],
            )

        def deal_wu(b, copy):
            wu_w[b] = place([P, 2 * PASS], U32, f"wu_w{b}", ("words", 4 + 4 * b))
            copy(
                wu_w[b][:].rearrange("p (a u e m) -> p a u m e", a=2, u=2, e=2),
                wu_raw[b][:].bitcast(U32).rearrange("p a (m u e) -> p a u m e", u=2, e=2),
            )

        def weave_wg(a, b, split):
            for copy, ms in ((nc.scalar.copy, slice(0, split)), (nc.vector.tensor_copy, slice(split, P))):
                if ms.start < ms.stop:
                    copy(
                        woven[a, b][:, :, ms, :].rearrange("p t m i -> p m i t"),
                        wg_raw[a, b][:].rearrange("p i (m t) -> p m i t", t=PACK)[:, ms],
                    )

        def quantize_wg(a, b, where):
            wg_w[a, b] = place([P, PASS], U32, f"wg_w{a}{b}", ("words", 12 + 2 * a + 4 * b))
            wg_s[a, b] = place([P, PASS], U8, f"wg_s{a}{b}", where)
            nc.vector.quantize_mx(out=wg_w[a, b][:].bitcast(FP8X4), scales=wg_s[a, b][:], in_=woven[a, b][:].rearrange("p t m i -> p (t m i)"))

        def gate_times_wgo(n, first, count, where=None):
            gw[n] = place([P, count], F32, f"gw{n}", where)[:]
            nc.vector.tensor_tensor(gw[n], gates[n][:].indirect(places(first, count)), wgo_all[:, first : first + count], MULT)

        def first_product(name, b, group, number, passes=None):
            tok = slice(GROUP * group % HALF, GROUP * group % HALF + GROUP)
            half = GROUP * group // HALF
            if passes != 1:
                banks[name, b, group] = bank(number, [P, PACK, GROUP], f"{name}{b}{group}")
            acc = banks[name, b, group]
            for t in range(PACK):
                for a in range(2) if passes is None else [passes]:
                    first, last = (a == 0, a == 1) if passes is None else (a == 0 and t == 0, a == 1 and t == PACK - 1)
                    if name == "ub":
                        cols = slice(PASS * a + P * t, PASS * a + P * (t + 1))
                        words, scales = wu_w[b][:, cols], wu_s[b][:, cols]
                    else:
                        cols = slice(P * t, P * (t + 1))
                        words, scales = wg_w[a, b][:, cols], wg_s[a, b][:, cols]
                    nc.tensor.matmul_mx(out=acc[:, t, :], lhsT=words.bitcast(FP8X4), lhsT_scale=scales,
                                        rhs=v_w[half][:, a, tok].bitcast(FP4X4), rhs_scale=v_s[:, half, a, tok], start=first, stop=last)
            sums[name, b, group] = acc[:].rearrange("p t (j e) -> p j t e", e=2)

        def silu(b, group, where=None):
            act[b, group] = place([P, GROUP // 2, PACK, 2], F32, f"act{b}{group}", where)
            nc.scalar.activation(act[b, group][:], sums["ga", b, group], SILU)

        def new_h(b, first, count, where=None):
            rows = place([P, GROUP * count, PACK], BF16, f"h{b}{first}", where)
            for c in range(count):
                h[b, first + c] = (rows, c)

        def multiply(b, group):
            rows, c = h[b, group]
            nc.vector.tensor_tensor(rows[:, GROUP * c : GROUP * (c + 1), :].rearrange("p (j e) t -> p j t e", e=2), sums["ub", b, group], act[b, group][:], MULT)

        def new_stage(b, first, count, where):
            act_sb = place([P, count, GROUP, PACK], F32, f"act_sb{b}{first}", where)
            ub_sb = place([P, count, GROUP, PACK], F32, f"ub_sb{b}{first}", (where[0], where[1] + 2 * count))
            staged[b, first] = (act_sb, ub_sb, count)

        def stage(b, first, group, numbers):
            act_sb, ub_sb, count = staged[b, first]
            first_product("ga", b, group, numbers[0])
            first_product("ub", b, group, numbers[1])
            nc.scalar.activation(act_sb[:, group - first].rearrange("p (j e) t -> p j t e", e=2), sums["ga", b, group], SILU)
            nc.scalar.copy(ub_sb[:, group - first].rearrange("p (j e) t -> p j t e", e=2), sums["ub", b, group])

        def multiply_staged(b, first):
            act_sb, ub_sb, count = staged[b, first]
            rows, c = h[b, first]
            nc.gpsimd.tensor_tensor(rows[:, GROUP * c : GROUP * (c + count), :], ub_sb[:].rearrange("p c j t -> p (c j) t"), act_sb[:].rearrange("p c j t -> p (c j) t"), MULT)

        def quantize_h(b, first, count, where=None):
            rows, c = h[b, first]
            half, start = divmod(GROUP * first, HALF)
            if (b, half) not in h_w:
                h_w[b, half] = place([P, HALF], U32, f"h_w{b}{half}", where or ("words", 23 + 2 * b + 4 * half))
                h_s[b, half] = place([P, HALF], U8, f"h_s{b}{half}", ("scales", 6 + 0.5 * b + half))
            tok = slice(start, start + GROUP * count)
            nc.vector.quantize_mx(out=h_w[b, half][:, tok].bitcast(FP8X4), scales=h_s[b, half][:, tok], in_=rows[:, GROUP * c : GROUP * (c + count), :].rearrange("p j t -> p (j t)"))

        def wd(b, cols):
            if b == 0:
                return wd8_w[:, cols].bitcast(FP8X4), wd_s[4:P, cols]
            return wd4_w[:, 2 * cols.start : 2 * cols.stop].bitcast(FP4X4), wd_s[:, cols]

        yw_middle = place([P, 2, HALF], F32, "yw_middle", ("yw", 2))
        yw_last = place([P, HALF], F32, "yw_last", ("yw", 8))
        yw.update({1: yw_middle[:, 0], 2: yw_middle[:, 1], 3: yw_last[:]})

        def down_tokens(b, group, number):
            if b == 0:
                y_bank[group] = bank(number, [P, 3 * P], f"y_tok{group}")
            tok = slice(GROUP * group, GROUP * (group + 1))
            for cols in (slice(0, 2 * P), slice(2 * P, 3 * P)):
                words, scales = wd(b, slice(P + cols.start, P + cols.stop))
                nc.tensor.matmul_mx(out=y_bank[group][:, cols], lhsT=h_w[b, 0][:, tok].bitcast(FP8X4), lhsT_scale=h_s[b, 0][:, tok],
                                    rhs=words, rhs_scale=scales, start=(b == 0 and cols.start == 0), stop=(b == 1 and cols.stop == 3 * P))

        def weigh(group):
            turned[group] = place([P, 3 * P], F32, f"turned{group}", ("turned", 2 * group))
            nc.scalar.activation(turned[group][:], y_bank[group][:], COPY, scale=w_tok[:, group : group + 1])

        def turn_middle(pair, number):
            back = bank(number, [P, 2, 2 * GROUP], f"back{pair}")
            for c in range(2):
                for n in range(2):
                    nc.tensor.transpose(back[:, n, GROUP * c : GROUP * (c + 1)], turned[2 * pair + c][:, P * n : P * (n + 1)], ident[:])
            nc.scalar.copy(yw_middle[:, :, 2 * GROUP * pair : 2 * GROUP * (pair + 1)], back[:])

        def turn_last(number):
            back = bank(number, [P, HALF], "back_last")
            for group in range(4):
                nc.tensor.transpose(back[:, GROUP * group : GROUP * (group + 1)], turned[group][:, 2 * P :], ident[:])
            nc.scalar.copy(yw_last[:], back[:])

        def down_rows(half, n, number, target, tok=slice(0, HALF)):
            y = bank(number, [P, tok.stop - tok.start], f"y_rows{half}{n}{tok.start}")
            for b in range(2):
                words, scales = wd(b, slice(P * n, P * (n + 1)))
                nc.tensor.matmul_mx(out=y[:], lhsT=words, lhsT_scale=scales, rhs=h_w[b, half][:, tok].bitcast(FP8X4), rhs_scale=h_s[b, half][:, tok], start=(b == 0), stop=(b == 1))
            nc.scalar.copy(target, y[:])

        def gate_times_yw(n, where=None):
            z[n] = place([P, HALF], F32, f"z{n}", where)
            nc.vector.tensor_tensor(z[n][:], gates[n][:].indirect(places(0, HALF)), yw[n], MULT)

        def scatter_z(n):
            nc.vector.tensor_copy(pages[n][:].indirect(places(0, HALF)), z[n][:])

        def scatter_y(n, first, count, y):
            nc.vector.tensor_tensor(pages[n][:].indirect(places(first, count)), y, gw[n][:, first : first + count] if n == 0 else gw[n], MULT)

        def clear_last_page(where):
            pages.append(place([P, T], F32, "page3", where))
            nc.gpsimd.memset(pages[3][:], 0.0)

        def store(n):
            nc.sync.dma_start(out[P * n : P * (n + 1), :], pages[n][:])

        spread_wgo()
        gather_table_words()
        deal_wu_scales(0, ("scales", 3))
        weave_wg(0, 0, P)
        deal_wu(0, nc.vector.tensor_copy)
        deal_wu_scales(1, ("wu0", 1))
        quantize_wg(0, 0, ("wu0", 0))
        for group in range(4):
            first_product("ub", 0, group, group)
        weave_wg(1, 0, 40)
        quantize_wg(1, 0, ("scales", 4))
        gate_times_wgo(0, 0, J, ("gw0", 0))
        deal_wu(1, nc.vector.tensor_copy)
        new_h(0, 0, 4, ("h", 0))
        for group in range(4):
            first_product("ga", 0, group, 4 + group)
            silu(0, group, ("table", 2 * group))
            multiply(0, group)
        for group in range(3):
            first_product("ub", 1, group, (6, 7, 5)[group])
        first_product("ga", 0, 4, 4)
        first_product("ub", 0, 4, 0)
        weave_wg(0, 1, 96)
        quantize_h(0, 0, 4)
        quantize_wg(0, 1, ("scales", 4.5))
        for group in range(3):
            first_product("ga", 1, group, (2, 3, 1)[group], 0)
        weave_wg(1, 1, 72)
        quantize_wg(1, 1, ("scales", 5))
        clear_last_page(("pages", 24))
        new_h(0, 4, 1, ("h", 4))
        silu(0, 4, ("wg11", 0))
        multiply(0, 4)
        for group in range(3):
            first_product("ga", 1, group, None, 1)
        first_product("ga", 1, 3, 4)
        first_product("ub", 1, 3, 0)
        new_h(1, 0, 4, ("h", 5))
        for group in range(4):
            silu(1, group, ("wg10", (0, 2, 8, 5)[group]))
        for group in range(3):
            multiply(1, group)
        quantize_h(1, 0, 2)
        multiply(1, 3)
        y_first = place([P, HALF], F32, "y_first", ("h", 9))
        down_rows(0, 0, 2, y_first[:, :QUARTER], slice(0, QUARTER))
        for group in range(2):
            down_tokens(0, group, 6 + group)
            down_tokens(1, group, None)
            weigh(group)
        quantize_h(1, 2, 2)
        quantize_h(0, 4, 1, ("wg10", 4))
        gate_times_wgo(1, HALF, HALF, ("wg10", 6))
        down_rows(0, 0, 1, y_first[:, QUARTER:], slice(QUARTER, HALF))
        scatter_y(0, 0, HALF, y_first[:])
        for group in range(2, 4):
            down_tokens(0, group, (5, 0)[group - 2])
            down_tokens(1, group, None)
            weigh(group)
        turn_middle(0, 3)
        turn_middle(1, 4)
        new_stage(0, 5, 3, ("woven", 0))
        stage(0, 5, 5, (2, 6))
        stage(0, 5, 6, (7, 1))
        stage(0, 5, 7, (5, 0))
        gate_times_yw(1)
        gate_times_yw(2)
        new_stage(1, 4, 2, ("wg01", 0))
        stage(1, 4, 4, (3, 4))
        stage(1, 4, 5, (2, 6))
        turn_last(7)
        new_stage(1, 6, 2, ("wg11", 0))
        stage(1, 6, 6, (1, 5))
        stage(1, 6, 7, (0, 3))
        new_h(0, 5, 3, ("yw", 0))
        new_h(1, 4, 2, ("yw", 4))
        multiply_staged(0, 5)
        multiply_staged(1, 4)
        scatter_z(1)
        scatter_z(2)
        gate_times_yw(3, ("wg01", 0))
        new_h(1, 6, 2, ("yw", 8))
        multiply_staged(1, 6)
        quantize_h(0, 5, 3)
        quantize_h(1, 4, 2)
        scatter_z(3)
        quantize_h(1, 6, 2)
        gate_times_wgo(2, HALF, HALF, ("wg11", 0))
        gate_times_wgo(3, HALF, HALF, ("wg11", 2))
        for n in range(4):
            y = place([P, HALF], F32, f"y{n}", ("wg00", 2 * n))
            down_rows(1, n, (4, 2, 6, 7)[n], y[:])
            scatter_y(n, HALF, HALF, y[:])
            store(n)
